import numpy as np
import ml_dtypes


def mxq(x, axis, fmt="e4m3"):
    dtype, down = {"e4m3": (ml_dtypes.float8_e4m3fn, 7), "e5m2": (ml_dtypes.float8_e5m2, 14)}[fmt]
    v = np.moveaxis(np.asarray(x, np.float32).astype(ml_dtypes.bfloat16).astype(np.float64), axis, -1)
    blocks = v.reshape(v.shape[:-1] + (-1, 32))
    amax = np.abs(blocks).max(-1, keepdims=True)
    byte = np.maximum(np.where(amax > 0, np.frexp(amax)[1] - 1 + 127, 0) - down, 1)
    scale = np.exp2(byte - 127.0)
    codes = (blocks / scale).astype(np.float32).astype(dtype).astype(np.float64)
    return np.moveaxis((codes * scale).reshape(v.shape), -1, axis)


WIDE = False


def mx_kscale(k):
    if not WIDE:
        return np.ones(k)
    levels = np.array([10, -10, 5, -5, 0])
    if k % 512:
        return np.exp2(np.random.permutation(np.resize(levels, k // 32))).repeat(32)
    a = np.empty((k // 512, 16))
    for p in range(k // 512):
        a[p, :8] = np.random.permutation(np.resize(levels, 8))
        for g in range(8):
            far = levels[np.abs(levels - a[p, g]) >= 10]
            a[p, g + 8] = far[np.random.randint(len(far))]
    return np.exp2(a.ravel()).repeat(32)


def f64(x):
    return np.asarray(x).astype(np.float64)


def striped(idx):
    return np.tile(idx.reshape(-1, 16).T, (8, 1)).astype(np.uint16)


def unstriped(offs):
    return offs[:16].T.reshape(-1).astype(np.int64)


E2M1 = np.array([0.0, 0.5, 1.0, 1.5, 2.0, 3.0, 4.0, 6.0, -0.0, -0.5, -1.0, -1.5, -2.0, -3.0, -4.0, -6.0])


def pack_weight(w, fmt):
    k, n = w.shape
    w = f64(np.asarray(w, np.float32).astype(ml_dtypes.bfloat16)).reshape(k // 32, 32, n)
    amax = np.abs(w).max(1)
    if fmt == "e4m3":
        byte = np.frexp(amax)[1] - 1 + 127 - 7
    else:
        mant, ex = np.frexp(amax / 6.0)
        byte = np.where(mant > 0.5, ex, ex - 1) + 127
    byte = np.clip(np.where(amax > 0, byte, 1), 1, 254)
    scaled = (w * np.exp2(127.0 - byte)[:, None, :]).reshape(k, n).astype(np.float32)
    by_word = np.ascontiguousarray(scaled.reshape(k // 512, 128, 4, n).transpose(0, 1, 3, 2))
    if fmt == "e4m3":
        words = by_word.astype(ml_dtypes.float8_e4m3fn).view(np.uint8)
    else:
        c = by_word.astype(ml_dtypes.float4_e2m1fn).view(np.uint8) & 0xF
        words = (c[..., 0::2] | (c[..., 1::2] << 4)).reshape(k // 512, 128, 2 * n)
    return np.ascontiguousarray(words), np.ascontiguousarray(byte.astype(np.uint8).reshape(k // 512, 16, n))


def unpack_weight(words, scales, fmt):
    g, _, n = scales.shape
    words = np.ascontiguousarray(words).reshape(g, 128, n, -1)
    if fmt == "e4m3":
        vals = words.view(ml_dtypes.float8_e4m3fn).astype(np.float64)
    else:
        nib = np.empty((g, 128, n, 4), np.uint8)
        nib[..., 0::2] = words & 0xF
        nib[..., 1::2] = words >> 4
        vals = E2M1[nib]
    vals = vals * np.repeat(np.exp2(scales.astype(np.float64) - 127.0), 8, axis=1)[..., None]
    return vals.transpose(0, 1, 3, 2).reshape(g * 512, n)


def gelu(v):
    return 0.5 * v * (1.0 + np.tanh(np.sqrt(2.0 / np.pi) * (v + 0.044715 * v**3)))


K, H, N, T, S, T2 = 1536, 512, 768, 4096, 1024, 2048

def setup_inputs():
    n = np.random.standard_normal
    s = mx_kscale(K)[:, None]
    u = mx_kscale(H)[:, None]
    tab_words, tab_scales = pack_weight(n((K, T)) * s, "e4m3")
    wl_words, wl_scales = pack_weight(n((K, H)) / np.sqrt(K) / s * u.T, "e2m1")
    wd_words, wd_scales = pack_weight(n((H, N)) / np.sqrt(H) / u, "e4m3")
    return {
        "tab_words": tab_words, "tab_scales": tab_scales,
        "wl_words": wl_words, "wl_scales": wl_scales,
        "wr": (n((K, H)) / np.sqrt(K) / s * u.T).astype(np.float32),
        "wd_words": wd_words, "wd_scales": wd_scales,
        "offs": striped(np.random.permutation(T)[:S]),
        "offs2": striped(np.random.permutation(T2)[:S]),
        "offs3": striped(np.random.permutation(T2)[:S]),
        "wg1": np.exp(0.3 * n((128, S))).astype(np.float32),
        "wg2": np.exp(0.3 * n((128, S))).astype(np.float32),
        "band": (np.random.uniform(0.2, 1.2, (H, T2)) * u).astype(np.float32),
        "style": (0.5 * n((N, T2))).astype(np.float32),
    }

def reference(tab_words, tab_scales, wl_words, wl_scales, wr, wd_words, wd_scales,
              offs, offs2, offs3, wg1, wg2, band, style):
    v = unpack_weight(tab_words, tab_scales, "e4m3")[:, unstriped(offs)]
    h1 = unpack_weight(wl_words, wl_scales, "e2m1").T @ v
    h2 = mxq(f64(wr), 0, "e4m3").T @ v
    pageA = np.zeros((H, T2))
    pageA[:, unstriped(offs2)] = np.tile(f64(wg1), (H // 128, 1)) * h1
    pageB = np.zeros((H, T2))
    pageB[:, unstriped(offs3)] = np.tile(f64(wg2), (H // 128, 1)) * h2
    z = np.maximum(np.abs(pageA - pageB), f64(band))
    y = unpack_weight(wd_words, wd_scales, "e4m3").T @ mxq(z, 0, "e4m3")
    return y + f64(style)

@@ -1,0 +1,278 @@
+from contextlib import ExitStack
+
+import concourse.mybir as mybir
+from concourse.masks import make_identity
+
+K, H, N, T, S, T2 = 1536, 512, 768, 4096, 1024, 2048
+FLOPS = 2 * (2 * K * H * S + H * N * T2)
+
+F32 = mybir.dt.float32
+BF16 = mybir.dt.bfloat16
+I32 = mybir.dt.int32
+U32 = mybir.dt.uint32
+U16 = mybir.dt.uint16
+U8 = mybir.dt.uint8
+E4M3 = mybir.dt.float8_e4m3fn_x4
+E2M1 = mybir.dt.float4_e2m1fn_x4
+ALU = mybir.AluOpType
+ACT = mybir.ActivationFunctionType
+
+P = 128
+PACK = 4
+PASSES = K // (P * PACK)
+BANK = 512
+HALVES = S // BANK
+ROW_TILES = H // P
+CHUNKS = T2 // BANK
+BLOCKS = BANK // P
+QUADS = 4
+ALIGN = 64
+
+
+def tile_list_stereo_patch_pages_kernel(
+    tc, tab_words, tab_scales, wl_words, wl_scales, wr, wd_words, wd_scales,
+    offs, offs2, offs3, wg1, wg2, band, style, out,
+):
+    nc = tc.nc
+    with ExitStack() as ctx:
+        lists = ctx.enter_context(tc.tile_pool(name="lists", bufs=1))
+        sb = ctx.enter_context(tc.tile_pool(name="sb", bufs=1))
+        ps = ctx.enter_context(tc.psum_pool(name="ps", bufs=1))
+
+        def sbuf(shape, dtype, name, tag=None, bufs=1):
+            return sb.tile(shape, dtype, name=name, tag=tag or name, bufs=bufs, align_bytes=ALIGN)
+
+        def bank(shape, name):
+            return ps.tile(shape, F32, name=name, tag="bank", bufs=8)
+
+        def clear(engine, tile):
+            engine.memset(tile.bitcast(I32), 0)
+
+        idx = lists.tile([P, S // 16], U16, name="idx")
+        idx2 = lists.tile([P, S // 16], U16, name="idx2")
+        idx3 = lists.tile([P, S // 16], U16, name="idx3")
+
+        nc.sync.dma_start(idx[:], offs)
+        nc.sync.dma_start(idx2[:], offs2)
+        nc.sync.dma_start(idx3[:], offs3)
+        wl_w = sbuf([P, PASSES, 2 * H], U8, "wl_w")
+        nc.sync.dma_start(wl_w[:].bitcast(I32), wl_words.rearrange("a p c -> p a c").bitcast(I32))
+        tab_sc = sbuf([P, T], U8, "tab_sc", "pageB1")
+        clear(nc.vector, tab_sc[:])
+        nc.gpsimd.dma_start(
+            tab_sc[0 : PASSES * 16, :].bitcast(I32),
+            tab_scales.rearrange("a q t -> (a q) t").bitcast(I32),
+        )
+        wl_sc = sbuf([P, PASSES, H], U8, "wl_sc", "w_sc")
+        clear(nc.vector, wl_sc[:].rearrange("p a c -> p (a c)"))
+        for q in range(QUADS):
+            nc.gpsimd.dma_start(
+                wl_sc[32 * q : 32 * q + 4, :, :].bitcast(I32),
+                wl_scales[:, 4 * q : 4 * q + 4, :].rearrange("a r c -> r a c").bitcast(I32),
+            )
+        tab = []
+        for a in range(PASSES):
+            tab.append(sbuf([P, T], I32, f"tab{a}", f"slot{a}"))
+            nc.sync.dma_start(tab[a][:], tab_words[a].rearrange("p t i -> p (t i)").bitcast(I32))
+        gain1 = sbuf([P, S], F32, "gain1")
+        nc.sync.dma_start(gain1[:], wg1)
+
+        picked_sc = sbuf([P, S], U8, "picked_sc", "pageB0")
+        nc.vector.tensor_copy(picked_sc[:], tab_sc[:].indirect(idx[:]))
+        v_sc = []
+        for a in range(PASSES):
+            v_sc.append(sbuf([P, S], U8, f"v_sc{a}"))
+            clear(nc.vector, v_sc[a][:])
+            queue = nc.scalar if a == 0 else nc.gpsimd
+            for q in range(QUADS):
+                row = 16 * a + 4 * q
+                queue.dma_start(
+                    v_sc[a][32 * q : 32 * q + 4, :].bitcast(I32),
+                    picked_sc[row : row + 4, :].bitcast(I32),
+                )
+        v_w = []
+        for a in range(PASSES):
+            v_w.append(sbuf([P, S], U32, f"v_w{a}"))
+            pieces = HALVES if a == PASSES - 1 else 1
+            n = S // pieces
+            for i in range(pieces):
+                nc.vector.tensor_copy(
+                    v_w[a][:, i * n : (i + 1) * n],
+                    tab[a][:].bitcast(U32).indirect(idx[:, i * n // 16 : (i + 1) * n // 16]),
+                )
+
+        pageA = [sbuf([P, T2], F32, f"pageA{i}") for i in range(2)]
+        for page in pageA:
+            nc.gpsimd.memset(page[:], 0.0)
+        pageB = [sbuf([P, T2], F32, f"pageB{i}") for i in range(2)]
+        for page in pageB:
+            nc.gpsimd.memset(page[:], 0.0)
+        ident = sbuf([P, P], F32, "ident")
+        make_identity(nc, ident[:])
+
+        def features(a_row, weights, scales, name, negate):
+            h = sbuf([P, S], F32, name)
+            for i in range(HALVES):
+                cols = slice(i * BANK, (i + 1) * BANK)
+                acc = bank([P, BANK], "acc")
+                for a in range(PASSES):
+                    nc.tensor.matmul_mx(
+                        acc[:],
+                        lhsT=weights(a, a_row),
+                        lhsT_scale=scales[:, a, a_row * P : (a_row + 1) * P],
+                        rhs=v_w[a][:, cols].bitcast(E4M3),
+                        rhs_scale=v_sc[a][:, cols],
+                        start=(a == 0),
+                        stop=(a == PASSES - 1),
+                    )
+                if negate:
+                    nc.scalar.activation(h[:, cols], acc[:], ACT.Copy, scale=-1.0)
+                else:
+                    nc.scalar.copy(h[:, cols], acc[:])
+            return h
+
+        def place(page, h, gain, places, pieces=1):
+            n = S // pieces
+            for i in range(pieces):
+                cols = slice(i * n, (i + 1) * n)
+                nc.vector.tensor_tensor(
+                    page[:].indirect(places[:, i * n // 16 : (i + 1) * n // 16]),
+                    h[:, cols], gain[:, cols], ALU.mult,
+                )
+
+        def left(a, r):
+            return wl_w[:, a, 2 * P * r : 2 * P * (r + 1)].bitcast(E2M1)
+
+        h1 = [features(r, left, wl_sc, f"h1_{r}", False) for r in range(ROW_TILES)]
+        place(pageA[0], h1[0], gain1, idx2, HALVES)
+        place(pageA[1], h1[1], gain1, idx2)
+
+        wr_bf = sbuf([P, PASSES, H * PACK], BF16, "wr_bf", "style0")
+        wr_w = sbuf([P, PASSES, H], U32, "wr_w")
+        wr_sc = sbuf([P, PASSES, H], U8, "wr_sc")
+        for a in range(PASSES):
+            raw = sbuf([P, PACK, H], F32, f"wr_raw{a}", f"slot{a}")
+            nc.sync.dma_start(
+                raw[:], wr[a * P * PACK : (a + 1) * P * PACK, :].rearrange("(p t) c -> p t c", t=PACK)
+            )
+            nc.scalar.copy(
+                wr_bf[:, a, :].rearrange("p (c i t) -> p c t i", i=4, t=PACK),
+                raw[:].rearrange("p t (c i) -> p c t i", i=4),
+            )
+        for a in range(PASSES):
+            nc.vector.quantize_mx(wr_w[:, a, :].bitcast(E4M3), wr_sc[:, a, :], wr_bf[:, a, :])
+        gain2 = sbuf([P, S], F32, "gain2", "wl_w")
+        nc.sync.dma_start(gain2[:], wg2)
+
+        pageA.append(sbuf([P, T2], F32, "pageA2", f"slot{PASSES - 1}"))
+        nc.gpsimd.memset(pageA[2][:], 0.0)
+        place(pageA[2], h1[2], gain1, idx2)
+
+        def right(a, r):
+            return wr_w[:, a, P * r : P * (r + 1)].bitcast(E4M3)
+
+        h2 = [features(r, right, wr_sc, f"h2_{r}", True) for r in range(ROW_TILES)]
+
+        band_bf = [sbuf([P, BANK * PACK], BF16, f"band_bf{c}") for c in range(CHUNKS)]
+        for s in range(2):
+            raw = sbuf([P, PACK, 2 * BANK], F32, f"band_raw{s}", f"slot{s}")
+            nc.sync.dma_start(
+                raw[:],
+                band[:, 2 * BANK * s : 2 * BANK * (s + 1)].rearrange("(p t) m -> p t m", t=PACK),
+            )
+            for k in range(2):
+                nc.scalar.copy(
+                    band_bf[2 * s + k][:].rearrange("p (m i t) -> p m t i", i=4, t=PACK),
+                    raw[:, :, k * BANK : (k + 1) * BANK].rearrange("p t (m i) -> p m t i", i=4),
+                )
+        wd_w = sbuf([P, N], I32, "wd_w", "v_w0")
+        nc.sync.dma_start(wd_w[:], wd_words[0].rearrange("p c i -> p (c i)").bitcast(I32))
+        wd_sc = sbuf([P, N], U8, "wd_sc", "w_sc")
+        clear(nc.gpsimd, wd_sc[:])
+        for q in range(QUADS):
+            nc.sync.dma_start(
+                wd_sc[32 * q : 32 * q + 4, :].bitcast(I32),
+                wd_scales[0, 4 * q : 4 * q + 4, :].bitcast(I32),
+            )
+        res = []
+        for s, tag in enumerate(("style0", "slot0", "slot1")):
+            res.append(sbuf([P, 2, T2], F32, f"res{s}", tag))
+            nc.sync.dma_start(
+                res[s][:], style[2 * P * s : 2 * P * (s + 1), :].rearrange("(i p) m -> p i m", p=P)
+            )
+
+        gap = [sbuf([P, 2, BLOCKS, P, 2], BF16, f"gap{c}") for c in range(CHUNKS)]
+
+        def turn(turned, page, c, first):
+            for b in range(BLOCKS):
+                nc.tensor.matmul(
+                    turned[:, b, :], page[:, c * BANK + b * P : c * BANK + (b + 1) * P], ident[:],
+                    start=(first and b == 0), stop=(not first and b == BLOCKS - 1), is_transpose=True,
+                )
+
+        def magnitude(turned, r, c):
+            nc.scalar.activation(
+                gap[c][:, :, :, 32 * r : 32 * (r + 1), :],
+                turned[:].rearrange("m b (p u e) -> m u b p e", u=2, e=2),
+                ACT.Abs,
+            )
+
+        last = ROW_TILES - 1
+        for r in range(last):
+            if r == 2:
+                place(pageA[0], h1[3], gain1, idx2)
+            place(pageB[r % 2], h2[r], gain2, idx3)
+            for c in range(CHUNKS):
+                turned = bank([P, BLOCKS, P], "turned")
+                turn(turned, pageA[r], c, True)
+                turn(turned, pageB[r % 2], c, False)
+                magnitude(turned, r, c)
+        place(pageB[last % 2], h2[last], gain2, idx3)
+        held = [bank([P, BLOCKS, P], "held") for c in range(CHUNKS)]
+        for c in range(CHUNKS):
+            turn(held[c], pageA[0], c, True)
+
+        for c in range(CHUNKS):
+            turn(held[c], pageB[last % 2], c, False)
+            magnitude(held[c], last, c)
+            words = gap[c][:].rearrange("m u b p e -> m (u b p e)").bitcast(F32)
+            z = sbuf([P, BANK * PACK], BF16, "z", bufs=2)
+            half = BANK * PACK // 2
+            for k in range(2):
+                back = bank([P, 2, 2 * P], "back")
+                for u in range(2):
+                    for b in range(2):
+                        w0 = (u * BLOCKS + 2 * k + b) * P
+                        nc.tensor.transpose(
+                            back[:, u, b * P : (b + 1) * P], words[:, w0 : w0 + P], ident[:]
+                        )
+                nc.vector.tensor_tensor(
+                    z[:, k * half : (k + 1) * half].rearrange("p (m u e) -> p m u e", u=2, e=2),
+                    back[:].bitcast(BF16).rearrange("p u (m e) -> p m u e", e=2),
+                    band_bf[c][:, k * half : (k + 1) * half].rearrange("p (m u e) -> p m u e", u=2, e=2),
+                    ALU.max,
+                )
+            z_w = sbuf([P, BANK], U32, "z_w", bufs=2)
+            z_sc = sbuf([P, BANK], U8, "z_sc", bufs=2)
+            nc.vector.quantize_mx(z_w[:].bitcast(E4M3), z_sc[:], z[:])
+            cols = slice(c * BANK, (c + 1) * BANK)
+            for s in range(3):
+                for i in range(2):
+                    n0 = (2 * s + i) * P
+                    acc = bank([P, BANK], "acc")
+                    nc.tensor.matmul_mx(
+                        acc[:],
+                        lhsT=wd_w[:, n0 : n0 + P].bitcast(E4M3),
+                        lhsT_scale=wd_sc[:, n0 : n0 + P],
+                        rhs=z_w[:].bitcast(E4M3),
+                        rhs_scale=z_sc[:],
+                        start=True,
+                        stop=True,
+                    )
+                    if i == 0 and (c < CHUNKS - 1 or s < 2):
+                        y = sbuf([P, BANK], F32, "y", bufs=3)
+                        nc.scalar.copy(y[:], acc[:])
+                        nc.gpsimd.tensor_tensor(res[s][:, i, cols], y[:], res[s][:, i, cols], ALU.add)
+                    else:
+                        nc.vector.tensor_tensor(res[s][:, i, cols], acc[:], res[s][:, i, cols], ALU.add)
+                    nc.sync.dma_start(out[n0 : n0 + P, cols], res[s][:, i, cols])

@@ -27,6 +27,7 @@ CHUNKS = T2 // BANK
 BLOCKS = BANK // P
 QUADS = 4
 ALIGN = 64
+MOVES_AHEAD = 6
 
 
 def tile_list_stereo_patch_pages_kernel(
@@ -37,10 +38,19 @@ def tile_list_stereo_patch_pages_kernel(
     with ExitStack() as ctx:
         lists = ctx.enter_context(tc.tile_pool(name="lists", bufs=1))
         sb = ctx.enter_context(tc.tile_pool(name="sb", bufs=1))
+        placed = ctx.enter_context(tc.tile_pool(name="placed", bufs=1))
         ps = ctx.enter_context(tc.psum_pool(name="ps", bufs=1))
 
         def sbuf(shape, dtype, name, tag=None, bufs=1):
             return sb.tile(shape, dtype, name=name, tag=tag or name, bufs=bufs, align_bytes=ALIGN)
+
+        def sbuf_at(offset, shape, dtype, name):
+            return placed.tile(shape, dtype, name=name, offset=offset, align_bytes=ALIGN)
+
+        def slot(a, shape, dtype, name):
+            if a == PASSES - 1:
+                return sbuf_at(0, shape, dtype, name)
+            return sbuf(shape, dtype, name, f"slot{a}")
 
         def bank(shape, name):
             return ps.tile(shape, F32, name=name, tag="bank", bufs=8)
@@ -57,9 +67,9 @@ def tile_list_stereo_patch_pages_kernel(
         nc.sync.dma_start(idx3[:], offs3)
         wl_w = sbuf([P, PASSES, 2 * H], U8, "wl_w")
         nc.sync.dma_start(wl_w[:].bitcast(I32), wl_words.rearrange("a p c -> p a c").bitcast(I32))
-        tab_sc = sbuf([P, T], U8, "tab_sc", "pageB1")
+        tab_sc = sbuf_at(4 * T - T // 2, [P, T], U8, "tab_sc")
         clear(nc.vector, tab_sc[:])
-        nc.gpsimd.dma_start(
+        nc.sync.dma_start(
             tab_sc[0 : PASSES * 16, :].bitcast(I32),
             tab_scales.rearrange("a q t -> (a q) t").bitcast(I32),
         )
@@ -71,25 +81,30 @@ def tile_list_stereo_patch_pages_kernel(
                 wl_scales[:, 4 * q : 4 * q + 4, :].rearrange("a r c -> r a c").bitcast(I32),
             )
         tab = []
-        for a in range(PASSES):
-            tab.append(sbuf([P, T], I32, f"tab{a}", f"slot{a}"))
-            nc.sync.dma_start(tab[a][:], tab_words[a].rearrange("p t i -> p (t i)").bitcast(I32))
-        gain1 = sbuf([P, S], F32, "gain1")
-        nc.sync.dma_start(gain1[:], wg1)
 
-        picked_sc = sbuf([P, S], U8, "picked_sc", "pageB0")
+        def load_table(a):
+            tab.append(slot(a, [P, T], I32, f"tab{a}"))
+            nc.sync.dma_start(tab[a][:], tab_words[a].rearrange("p t i -> p (t i)").bitcast(I32))
+
+        for a in range(PASSES - 1):
+            load_table(a)
+
+        picked_sc = sbuf([P, S], U8, "picked_sc")
         nc.vector.tensor_copy(picked_sc[:], tab_sc[:].indirect(idx[:]))
         v_sc = []
         for a in range(PASSES):
             v_sc.append(sbuf([P, S], U8, f"v_sc{a}"))
             clear(nc.vector, v_sc[a][:])
-            queue = nc.scalar if a == 0 else nc.gpsimd
-            for q in range(QUADS):
-                row = 16 * a + 4 * q
-                queue.dma_start(
-                    v_sc[a][32 * q : 32 * q + 4, :].bitcast(I32),
-                    picked_sc[row : row + 4, :].bitcast(I32),
-                )
+        for k in range(PASSES * QUADS):
+            if k == MOVES_AHEAD:
+                load_table(PASSES - 1)
+            a, q = divmod(k, QUADS)
+            nc.sync.dma_start(
+                v_sc[a][32 * q : 32 * q + 4, :].bitcast(I32),
+                picked_sc[4 * k : 4 * k + 4, :].bitcast(I32),
+            )
+        gain1 = sbuf_at(4 * T, [P, S], F32, "gain1")
+        nc.sync.dma_start(gain1[:], wg1)
         v_w = []
         for a in range(PASSES):
             v_w.append(sbuf([P, S], U32, f"v_w{a}"))
@@ -103,7 +118,7 @@ def tile_list_stereo_patch_pages_kernel(
 
         pageA = [sbuf([P, T2], F32, f"pageA{i}") for i in range(2)]
         for page in pageA:
-            nc.gpsimd.memset(page[:], 0.0)
+            nc.vector.memset(page[:], 0.0)
         pageB = [sbuf([P, T2], F32, f"pageB{i}") for i in range(2)]
         for page in pageB:
             nc.gpsimd.memset(page[:], 0.0)
@@ -151,7 +166,7 @@ def tile_list_stereo_patch_pages_kernel(
         wr_w = sbuf([P, PASSES, H], U32, "wr_w")
         wr_sc = sbuf([P, PASSES, H], U8, "wr_sc")
         for a in range(PASSES):
-            raw = sbuf([P, PACK, H], F32, f"wr_raw{a}", f"slot{a}")
+            raw = slot(a, [P, PACK, H], F32, f"wr_raw{a}")
             nc.sync.dma_start(
                 raw[:], wr[a * P * PACK : (a + 1) * P * PACK, :].rearrange("(p t) c -> p t c", t=PACK)
             )
@@ -164,7 +179,7 @@ def tile_list_stereo_patch_pages_kernel(
         gain2 = sbuf([P, S], F32, "gain2", "wl_w")
         nc.sync.dma_start(gain2[:], wg2)
 
-        pageA.append(sbuf([P, T2], F32, "pageA2", f"slot{PASSES - 1}"))
+        pageA.append(slot(PASSES - 1, [P, T2], F32, "pageA2"))
         nc.gpsimd.memset(pageA[2][:], 0.0)
         place(pageA[2], h1[2], gain1, idx2)
 

@@ -65,7 +65,7 @@ def tile_list_stereo_patch_pages_kernel(
         nc.sync.dma_start(idx[:], offs)
         nc.sync.dma_start(idx2[:], offs2)
         nc.sync.dma_start(idx3[:], offs3)
-        wl_w = sbuf([P, PASSES, 2 * H], U8, "wl_w")
+        wl_w = sbuf([P, PASSES, 2 * H], U8, "wl_w", "res1")
         nc.sync.dma_start(wl_w[:].bitcast(I32), wl_words.rearrange("a p c -> p a c").bitcast(I32))
         tab_sc = sbuf_at(4 * T - T // 2, [P, T], U8, "tab_sc")
         clear(nc.vector, tab_sc[:])
@@ -119,14 +119,15 @@ def tile_list_stereo_patch_pages_kernel(
         pageA = [sbuf([P, T2], F32, f"pageA{i}") for i in range(2)]
         for page in pageA:
             nc.vector.memset(page[:], 0.0)
-        pageB = [sbuf([P, T2], F32, f"pageB{i}") for i in range(2)]
-        for page in pageB:
+        pageA_last = sbuf([P, T2], F32, "pageA_last")
+        pageB = [sbuf([P, T2], F32, f"pageB{i}") for i in range(3)]
+        for page in [pageA_last] + pageB:
             nc.gpsimd.memset(page[:], 0.0)
         ident = sbuf([P, P], F32, "ident")
         make_identity(nc, ident[:])
 
-        def features(a_row, weights, scales, name, negate):
-            h = sbuf([P, S], F32, name)
+        def features(a_row, weights, scales, name, tag, negate):
+            h = sbuf([P, S], F32, name, tag)
             for i in range(HALVES):
                 cols = slice(i * BANK, (i + 1) * BANK)
                 acc = bank([P, BANK], "acc")
@@ -158,11 +159,12 @@ def tile_list_stereo_patch_pages_kernel(
         def left(a, r):
             return wl_w[:, a, 2 * P * r : 2 * P * (r + 1)].bitcast(E2M1)
 
-        h1 = [features(r, left, wl_sc, f"h1_{r}", False) for r in range(ROW_TILES)]
+        h1 = [features(r, left, wl_sc, f"h1_{r}", ("res2", "h_a", "h_b", "h_c")[r], False) for r in range(ROW_TILES)]
         place(pageA[0], h1[0], gain1, idx2, HALVES)
         place(pageA[1], h1[1], gain1, idx2)
+        place(pageA_last, h1[3], gain1, idx2)
 
-        wr_bf = sbuf([P, PASSES, H * PACK], BF16, "wr_bf", "style0")
+        wr_bf = sbuf([P, PASSES, H * PACK], BF16, "wr_bf", "res0")
         wr_w = sbuf([P, PASSES, H], U32, "wr_w")
         wr_sc = sbuf([P, PASSES, H], U8, "wr_sc")
         for a in range(PASSES):
@@ -171,12 +173,12 @@ def tile_list_stereo_patch_pages_kernel(
                 raw[:], wr[a * P * PACK : (a + 1) * P * PACK, :].rearrange("(p t) c -> p t c", t=PACK)
             )
             nc.scalar.copy(
-                wr_bf[:, a, :].rearrange("p (c i t) -> p c t i", i=4, t=PACK),
-                raw[:].rearrange("p t (c i) -> p c t i", i=4),
+                wr_bf[:, a, :].rearrange("p (c t) -> p c t", t=PACK),
+                raw[:].rearrange("p t c -> p c t"),
             )
         for a in range(PASSES):
             nc.vector.quantize_mx(wr_w[:, a, :].bitcast(E4M3), wr_sc[:, a, :], wr_bf[:, a, :])
-        gain2 = sbuf([P, S], F32, "gain2", "wl_w")
+        gain2 = sbuf([P, S], F32, "gain2", "w_sc")
         nc.sync.dma_start(gain2[:], wg2)
 
         pageA.append(slot(PASSES - 1, [P, T2], F32, "pageA2"))
@@ -186,7 +188,7 @@ def tile_list_stereo_patch_pages_kernel(
         def right(a, r):
             return wr_w[:, a, P * r : P * (r + 1)].bitcast(E4M3)
 
-        h2 = [features(r, right, wr_sc, f"h2_{r}", True) for r in range(ROW_TILES)]
+        h2 = [features(r, right, wr_sc, f"h2_{r}", ("h_d", "h_e", "h_a", "h_c")[r], True) for r in range(ROW_TILES)]
 
         band_bf = [sbuf([P, BANK * PACK], BF16, f"band_bf{c}") for c in range(CHUNKS)]
         for s in range(2):
@@ -197,12 +199,12 @@ def tile_list_stereo_patch_pages_kernel(
             )
             for k in range(2):
                 nc.scalar.copy(
-                    band_bf[2 * s + k][:].rearrange("p (m i t) -> p m t i", i=4, t=PACK),
-                    raw[:, :, k * BANK : (k + 1) * BANK].rearrange("p t (m i) -> p m t i", i=4),
+                    band_bf[2 * s + k][:].rearrange("p (m t) -> p m t", t=PACK),
+                    raw[:, :, k * BANK : (k + 1) * BANK].rearrange("p t m -> p m t"),
                 )
         wd_w = sbuf([P, N], I32, "wd_w", "v_w0")
         nc.sync.dma_start(wd_w[:], wd_words[0].rearrange("p c i -> p (c i)").bitcast(I32))
-        wd_sc = sbuf([P, N], U8, "wd_sc", "w_sc")
+        wd_sc = sbuf([P, N], U8, "wd_sc", "v_w2")
         clear(nc.gpsimd, wd_sc[:])
         for q in range(QUADS):
             nc.sync.dma_start(
@@ -210,8 +212,8 @@ def tile_list_stereo_patch_pages_kernel(
                 wd_scales[0, 4 * q : 4 * q + 4, :].bitcast(I32),
             )
         res = []
-        for s, tag in enumerate(("style0", "slot0", "slot1")):
-            res.append(sbuf([P, 2, T2], F32, f"res{s}", tag))
+        for s in range(3):
+            res.append(sbuf([P, 2, T2], F32, f"res{s}"))
             nc.sync.dma_start(
                 res[s][:], style[2 * P * s : 2 * P * (s + 1), :].rearrange("(i p) m -> p i m", p=P)
             )
@@ -234,24 +236,22 @@ def tile_list_stereo_patch_pages_kernel(
 
         last = ROW_TILES - 1
         for r in range(last):
-            if r == 2:
-                place(pageA[0], h1[3], gain1, idx2)
-            place(pageB[r % 2], h2[r], gain2, idx3)
+            place(pageB[r], h2[r], gain2, idx3)
             for c in range(CHUNKS):
                 turned = bank([P, BLOCKS, P], "turned")
                 turn(turned, pageA[r], c, True)
-                turn(turned, pageB[r % 2], c, False)
+                turn(turned, pageB[r], c, False)
                 magnitude(turned, r, c)
-        place(pageB[last % 2], h2[last], gain2, idx3)
+        place(pageB[0], h2[last], gain2, idx3)
         held = [bank([P, BLOCKS, P], "held") for c in range(CHUNKS)]
         for c in range(CHUNKS):
-            turn(held[c], pageA[0], c, True)
+            turn(held[c], pageA_last, c, True)
 
         for c in range(CHUNKS):
-            turn(held[c], pageB[last % 2], c, False)
+            turn(held[c], pageB[0], c, False)
             magnitude(held[c], last, c)
             words = gap[c][:].rearrange("m u b p e -> m (u b p e)").bitcast(F32)
-            z = sbuf([P, BANK * PACK], BF16, "z", bufs=2)
+            z = sbuf([P, BANK * PACK], BF16, "z", ("h_d", "h_e")[c % 2])
             half = BANK * PACK // 2
             for k in range(2):
                 back = bank([P, 2, 2 * P], "back")
@@ -263,8 +263,8 @@ def tile_list_stereo_patch_pages_kernel(
                         )
                 nc.vector.tensor_tensor(
                     z[:, k * half : (k + 1) * half].rearrange("p (m u e) -> p m u e", u=2, e=2),
-                    back[:].bitcast(BF16).rearrange("p u (m e) -> p m u e", e=2),
                     band_bf[c][:, k * half : (k + 1) * half].rearrange("p (m u e) -> p m u e", u=2, e=2),
+                    back[:].bitcast(BF16).rearrange("p u (m e) -> p m u e", e=2),
                     ALU.max,
                 )
             z_w = sbuf([P, BANK], U32, "z_w", bufs=2)
@@ -284,10 +284,5 @@ def tile_list_stereo_patch_pages_kernel(
                         start=True,
                         stop=True,
                     )
-                    if i == 0 and (c < CHUNKS - 1 or s < 2):
-                        y = sbuf([P, BANK], F32, "y", bufs=3)
-                        nc.scalar.copy(y[:], acc[:])
-                        nc.gpsimd.tensor_tensor(res[s][:, i, cols], y[:], res[s][:, i, cols], ALU.add)
-                    else:
-                        nc.vector.tensor_tensor(res[s][:, i, cols], acc[:], res[s][:, i, cols], ALU.add)
+                    nc.vector.tensor_tensor(res[s][:, i, cols], res[s][:, i, cols], acc[:], ALU.add)
                     nc.sync.dma_start(out[n0 : n0 + P, cols], res[s][:, i, cols])

@@ -28,6 +28,7 @@ BLOCKS = BANK // P
 QUADS = 4
 ALIGN = 64
 MOVES_AHEAD = 6
+SLOT = 4 * T
 
 
 def tile_list_stereo_patch_pages_kernel(
@@ -47,10 +48,8 @@ def tile_list_stereo_patch_pages_kernel(
         def sbuf_at(offset, shape, dtype, name):
             return placed.tile(shape, dtype, name=name, offset=offset, align_bytes=ALIGN)
 
-        def slot(a, shape, dtype, name):
-            if a == PASSES - 1:
-                return sbuf_at(0, shape, dtype, name)
-            return sbuf(shape, dtype, name, f"slot{a}")
+        def slot(a, half, shape, dtype, name):
+            return sbuf_at(SLOT * a + half * SLOT // 2, shape, dtype, name)
 
         def bank(shape, name):
             return ps.tile(shape, F32, name=name, tag="bank", bufs=8)
@@ -65,25 +64,26 @@ def tile_list_stereo_patch_pages_kernel(
         nc.sync.dma_start(idx[:], offs)
         nc.sync.dma_start(idx2[:], offs2)
         nc.sync.dma_start(idx3[:], offs3)
-        wl_w = sbuf([P, PASSES, 2 * H], U8, "wl_w", "res1")
+        wl_w = sbuf([P, PASSES, 2 * H], U8, "wl_w")
         nc.sync.dma_start(wl_w[:].bitcast(I32), wl_words.rearrange("a p c -> p a c").bitcast(I32))
-        tab_sc = sbuf_at(4 * T - T // 2, [P, T], U8, "tab_sc")
-        clear(nc.vector, tab_sc[:])
+        tab_sc = sbuf_at(PASSES * SLOT - T // 2, [P, T], U8, "tab_sc")
+        clear(nc.gpsimd, tab_sc[:, 0 : T // 2])
+        clear(nc.vector, tab_sc[:, T // 2 : T])
         nc.sync.dma_start(
             tab_sc[0 : PASSES * 16, :].bitcast(I32),
             tab_scales.rearrange("a q t -> (a q) t").bitcast(I32),
         )
         wl_sc = sbuf([P, PASSES, H], U8, "wl_sc", "w_sc")
-        clear(nc.vector, wl_sc[:].rearrange("p a c -> p (a c)"))
+        clear(nc.gpsimd, wl_sc[:].rearrange("p a c -> p (a c)"))
         for q in range(QUADS):
-            nc.gpsimd.dma_start(
+            nc.sync.dma_start(
                 wl_sc[32 * q : 32 * q + 4, :, :].bitcast(I32),
                 wl_scales[:, 4 * q : 4 * q + 4, :].rearrange("a r c -> r a c").bitcast(I32),
             )
         tab = []
 
         def load_table(a):
-            tab.append(slot(a, [P, T], I32, f"tab{a}"))
+            tab.append(slot(a, 0, [P, T], I32, f"tab{a}"))
             nc.sync.dma_start(tab[a][:], tab_words[a].rearrange("p t i -> p (t i)").bitcast(I32))
 
         for a in range(PASSES - 1):
@@ -103,7 +103,7 @@ def tile_list_stereo_patch_pages_kernel(
                 v_sc[a][32 * q : 32 * q + 4, :].bitcast(I32),
                 picked_sc[4 * k : 4 * k + 4, :].bitcast(I32),
             )
-        gain1 = sbuf_at(4 * T, [P, S], F32, "gain1")
+        gain1 = sbuf_at(PASSES * SLOT, [P, S], F32, "gain1")
         nc.sync.dma_start(gain1[:], wg1)
         v_w = []
         for a in range(PASSES):
@@ -116,18 +116,14 @@ def tile_list_stereo_patch_pages_kernel(
                     tab[a][:].bitcast(U32).indirect(idx[:, i * n // 16 : (i + 1) * n // 16]),
                 )
 
-        pageA = [sbuf([P, T2], F32, f"pageA{i}") for i in range(2)]
-        for page in pageA:
+        pageA = [sbuf([P, T2], F32, f"pageA{i}") for i in range(ROW_TILES)]
+        pageB = [slot(i, 1, [P, T2], F32, f"pageB{i}") for i in range(2)]
+        for page in pageA + pageB:
             nc.vector.memset(page[:], 0.0)
-        pageA_last = sbuf([P, T2], F32, "pageA_last")
-        pageB = [sbuf([P, T2], F32, f"pageB{i}") for i in range(3)]
-        for page in [pageA_last] + pageB:
-            nc.gpsimd.memset(page[:], 0.0)
         ident = sbuf([P, P], F32, "ident")
         make_identity(nc, ident[:])
 
-        def features(a_row, weights, scales, name, tag, negate):
-            h = sbuf([P, S], F32, name, tag)
+        def features(a_row, weights, scales, h, negate):
             for i in range(HALVES):
                 cols = slice(i * BANK, (i + 1) * BANK)
                 acc = bank([P, BANK], "acc")
@@ -159,16 +155,16 @@ def tile_list_stereo_patch_pages_kernel(
         def left(a, r):
             return wl_w[:, a, 2 * P * r : 2 * P * (r + 1)].bitcast(E2M1)
 
-        h1 = [features(r, left, wl_sc, f"h1_{r}", ("res2", "h_a", "h_b", "h_c")[r], False) for r in range(ROW_TILES)]
-        place(pageA[0], h1[0], gain1, idx2, HALVES)
-        place(pageA[1], h1[1], gain1, idx2)
-        place(pageA_last, h1[3], gain1, idx2)
+        last = ROW_TILES - 1
+        for r, tag in ((0, "res2"), (1, "res1")):
+            h = features(r, left, wl_sc, sbuf([P, S], F32, f"h1_{r}", tag), False)
+            place(pageA[r], h, gain1, idx2, HALVES if r == 0 else 1)
 
         wr_bf = sbuf([P, PASSES, H * PACK], BF16, "wr_bf", "res0")
         wr_w = sbuf([P, PASSES, H], U32, "wr_w")
         wr_sc = sbuf([P, PASSES, H], U8, "wr_sc")
         for a in range(PASSES):
-            raw = slot(a, [P, PACK, H], F32, f"wr_raw{a}")
+            raw = slot(a, 0, [P, PACK, H], F32, f"wr_raw{a}")
             nc.sync.dma_start(
                 raw[:], wr[a * P * PACK : (a + 1) * P * PACK, :].rearrange("(p t) c -> p t c", t=PACK)
             )
@@ -178,38 +174,35 @@ def tile_list_stereo_patch_pages_kernel(
             )
         for a in range(PASSES):
             nc.vector.quantize_mx(wr_w[:, a, :].bitcast(E4M3), wr_sc[:, a, :], wr_bf[:, a, :])
-        gain2 = sbuf([P, S], F32, "gain2", "w_sc")
+        h = features(2, left, wl_sc, slot(PASSES - 1, 0, [P, S], F32, "h1_2"), False)
+        place(pageA[2], h, gain1, idx2)
+        gain2 = sbuf([P, S], F32, "gain2", "picked_sc")
         nc.sync.dma_start(gain2[:], wg2)
-
-        pageA.append(slot(PASSES - 1, [P, T2], F32, "pageA2"))
-        nc.gpsimd.memset(pageA[2][:], 0.0)
-        place(pageA[2], h1[2], gain1, idx2)
 
         def right(a, r):
             return wr_w[:, a, P * r : P * (r + 1)].bitcast(E4M3)
 
-        h2 = [features(r, right, wr_sc, f"h2_{r}", ("h_d", "h_e", "h_a", "h_c")[r], True) for r in range(ROW_TILES)]
+        h2 = [
+            features(r, right, wr_sc, sbuf([P, S], F32, f"h2_{r}", tag), True)
+            for r, tag in enumerate(("h_d", "h_e", "h_b", "h_c"))
+        ]
+
+        place(pageB[0], h2[0], gain2, idx3)
+        h = features(last, left, wl_sc, sbuf([P, S], F32, "h1_last", "h_d"), False)
 
         band_bf = [sbuf([P, BANK * PACK], BF16, f"band_bf{c}") for c in range(CHUNKS)]
-        for s in range(2):
-            raw = sbuf([P, PACK, 2 * BANK], F32, f"band_raw{s}", f"slot{s}")
+        for c in range(CHUNKS):
+            if c < 2:
+                raw = slot(c, 0, [P, PACK, BANK], F32, f"band_raw{c}")
+            elif c == 2:
+                raw = slot(c, 1, [P, PACK, BANK], F32, f"band_raw{c}")
+            else:
+                raw = sbuf([P, PACK, BANK], F32, f"band_raw{c}", "wl_w")
             nc.sync.dma_start(
-                raw[:],
-                band[:, 2 * BANK * s : 2 * BANK * (s + 1)].rearrange("(p t) m -> p t m", t=PACK),
+                raw[:], band[:, c * BANK : (c + 1) * BANK].rearrange("(p t) m -> p t m", t=PACK)
             )
-            for k in range(2):
-                nc.scalar.copy(
-                    band_bf[2 * s + k][:].rearrange("p (m t) -> p m t", t=PACK),
-                    raw[:, :, k * BANK : (k + 1) * BANK].rearrange("p t m -> p m t"),
-                )
-        wd_w = sbuf([P, N], I32, "wd_w", "v_w0")
-        nc.sync.dma_start(wd_w[:], wd_words[0].rearrange("p c i -> p (c i)").bitcast(I32))
-        wd_sc = sbuf([P, N], U8, "wd_sc", "v_w2")
-        clear(nc.gpsimd, wd_sc[:])
-        for q in range(QUADS):
-            nc.sync.dma_start(
-                wd_sc[32 * q : 32 * q + 4, :].bitcast(I32),
-                wd_scales[0, 4 * q : 4 * q + 4, :].bitcast(I32),
+            nc.scalar.copy(
+                band_bf[c][:].rearrange("p (m t) -> p m t", t=PACK), raw[:].rearrange("p t m -> p m t")
             )
         res = []
         for s in range(3):
@@ -234,25 +227,36 @@ def tile_list_stereo_patch_pages_kernel(
                 ACT.Abs,
             )
 
-        last = ROW_TILES - 1
         for r in range(last):
-            place(pageB[r], h2[r], gain2, idx3)
+            if r == 2:
+                place(pageA[last], h, gain1, idx2)
+            if r > 0:
+                place(pageB[r % 2], h2[r], gain2, idx3)
             for c in range(CHUNKS):
                 turned = bank([P, BLOCKS, P], "turned")
                 turn(turned, pageA[r], c, True)
-                turn(turned, pageB[r], c, False)
+                turn(turned, pageB[r % 2], c, False)
                 magnitude(turned, r, c)
-        place(pageB[0], h2[last], gain2, idx3)
+        place(pageB[last % 2], h2[last], gain2, idx3)
         held = [bank([P, BLOCKS, P], "held") for c in range(CHUNKS)]
         for c in range(CHUNKS):
-            turn(held[c], pageA_last, c, True)
+            turn(held[c], pageA[last], c, True)
 
-        for c in range(CHUNKS):
-            turn(held[c], pageB[0], c, False)
+        wd_w = sbuf([P, N], I32, "wd_w", "v_w0")
+        nc.sync.dma_start(wd_w[:], wd_words[0].rearrange("p c i -> p (c i)").bitcast(I32))
+        wd_sc = sbuf([P, N], U8, "wd_sc", "w_sc")
+        clear(nc.gpsimd, wd_sc[:])
+        for q in range(QUADS):
+            nc.sync.dma_start(
+                wd_sc[32 * q : 32 * q + 4, :].bitcast(I32),
+                wd_scales[0, 4 * q : 4 * q + 4, :].bitcast(I32),
+            )
+
+        def weave(c):
+            turn(held[c], pageB[last % 2], c, False)
             magnitude(held[c], last, c)
             words = gap[c][:].rearrange("m u b p e -> m (u b p e)").bitcast(F32)
-            z = sbuf([P, BANK * PACK], BF16, "z", ("h_d", "h_e")[c % 2])
-            half = BANK * PACK // 2
+            woven = sbuf([P, BANK, 2], F32, "woven", ("h_b", "h_c")[c % 2])
             for k in range(2):
                 back = bank([P, 2, 2 * P], "back")
                 for u in range(2):
@@ -261,28 +265,51 @@ def tile_list_stereo_patch_pages_kernel(
                         nc.tensor.transpose(
                             back[:, u, b * P : (b + 1) * P], words[:, w0 : w0 + P], ident[:]
                         )
-                nc.vector.tensor_tensor(
-                    z[:, k * half : (k + 1) * half].rearrange("p (m u e) -> p m u e", u=2, e=2),
-                    band_bf[c][:, k * half : (k + 1) * half].rearrange("p (m u e) -> p m u e", u=2, e=2),
-                    back[:].bitcast(BF16).rearrange("p u (m e) -> p m u e", e=2),
-                    ALU.max,
+                nc.scalar.copy(
+                    woven[:, 2 * P * k : 2 * P * (k + 1), :], back[:].rearrange("p u m -> p m u")
                 )
+            return woven
+
+        def floor_at_band(c, woven):
+            z = sbuf([P, BANK * PACK], BF16, "z", ("h_d", "h_e")[c % 2])
+            nc.vector.tensor_tensor(
+                z[:], woven[:].rearrange("p m u -> p (m u)").bitcast(BF16), band_bf[c][:], ALU.max
+            )
+            return z
+
+        def quantise(z):
             z_w = sbuf([P, BANK], U32, "z_w", bufs=2)
             z_sc = sbuf([P, BANK], U8, "z_sc", bufs=2)
             nc.vector.quantize_mx(z_w[:].bitcast(E4M3), z_sc[:], z[:])
+            return z_w, z_sc
+
+        def project(c, z_mx, tiles):
             cols = slice(c * BANK, (c + 1) * BANK)
-            for s in range(3):
-                for i in range(2):
-                    n0 = (2 * s + i) * P
-                    acc = bank([P, BANK], "acc")
-                    nc.tensor.matmul_mx(
-                        acc[:],
-                        lhsT=wd_w[:, n0 : n0 + P].bitcast(E4M3),
-                        lhsT_scale=wd_sc[:, n0 : n0 + P],
-                        rhs=z_w[:].bitcast(E4M3),
-                        rhs_scale=z_sc[:],
-                        start=True,
-                        stop=True,
-                    )
-                    nc.vector.tensor_tensor(res[s][:, i, cols], res[s][:, i, cols], acc[:], ALU.add)
-                    nc.sync.dma_start(out[n0 : n0 + P, cols], res[s][:, i, cols])
+            for n in tiles:
+                rows = slice(n * P, (n + 1) * P)
+                acc = bank([P, BANK], "acc")
+                nc.tensor.matmul_mx(
+                    acc[:],
+                    lhsT=wd_w[:, rows].bitcast(E4M3),
+                    lhsT_scale=wd_sc[:, rows],
+                    rhs=z_mx[0][:].bitcast(E4M3),
+                    rhs_scale=z_mx[1][:],
+                    start=True,
+                    stop=True,
+                )
+                total = res[n // 2][:, n % 2, cols]
+                nc.vector.tensor_tensor(total, total, acc[:], ALU.add)
+                nc.sync.dma_start(out[rows, cols], total)
+
+        z_mx = quantise(floor_at_band(0, weave(0)))
+        woven = weave(1)
+        for c in range(CHUNKS):
+            if c + 1 < CHUNKS:
+                z = floor_at_band(c + 1, woven)
+            project(c, z_mx, range(0, 3))
+            if c + 1 < CHUNKS:
+                z_next = quantise(z)
+            if c + 2 < CHUNKS:
+                woven = weave(c + 2)
+            project(c, z_mx, range(3, 6))
+            z_mx = z_next

@@ -23,12 +23,15 @@ PASSES = K // (P * PACK)
 BANK = 512
 HALVES = S // BANK
 ROW_TILES = H // P
+OUT_TILES = N // P
 CHUNKS = T2 // BANK
 BLOCKS = BANK // P
 QUADS = 4
+SPAN = P // ROW_TILES
 ALIGN = 64
-MOVES_AHEAD = 6
-SLOT = 4 * T
+KB = 1024
+SLOT = 16 * KB
+TURNED = PASSES * SLOT
 
 
 def tile_list_stereo_patch_pages_kernel(
@@ -51,8 +54,8 @@ def tile_list_stereo_patch_pages_kernel(
         def slot(a, half, shape, dtype, name):
             return sbuf_at(SLOT * a + half * SLOT // 2, shape, dtype, name)
 
-        def bank(shape, name):
-            return ps.tile(shape, F32, name=name, tag="bank", bufs=8)
+        def bank(i, shape, name):
+            return ps.tile(shape, F32, name=name, tag=f"bank{i}", bufs=1)
 
         def clear(engine, tile):
             engine.memset(tile.bitcast(I32), 0)
@@ -66,44 +69,33 @@ def tile_list_stereo_patch_pages_kernel(
         nc.sync.dma_start(idx3[:], offs3)
         wl_w = sbuf([P, PASSES, 2 * H], U8, "wl_w")
         nc.sync.dma_start(wl_w[:].bitcast(I32), wl_words.rearrange("a p c -> p a c").bitcast(I32))
-        tab_sc = sbuf_at(PASSES * SLOT - T // 2, [P, T], U8, "tab_sc")
-        clear(nc.gpsimd, tab_sc[:, 0 : T // 2])
-        clear(nc.vector, tab_sc[:, T // 2 : T])
-        nc.sync.dma_start(
+        tab = [slot(a, 0, [P, T], I32, f"tab{a}") for a in range(PASSES)]
+        for a in range(PASSES):
+            nc.sync.dma_start(tab[a][:], tab_words[a].rearrange("p t i -> p (t i)").bitcast(I32))
+        tab_sc = sbuf([P, T], U8, "tab_sc", "gain1")
+        clear(nc.vector, tab_sc[:])
+        nc.scalar.dma_start(
             tab_sc[0 : PASSES * 16, :].bitcast(I32),
-            tab_scales.rearrange("a q t -> (a q) t").bitcast(I32),
+            tab_scales.rearrange("a q t -> q a t").bitcast(I32),
         )
         wl_sc = sbuf([P, PASSES, H], U8, "wl_sc", "w_sc")
         clear(nc.gpsimd, wl_sc[:].rearrange("p a c -> p (a c)"))
         for q in range(QUADS):
-            nc.sync.dma_start(
+            nc.gpsimd.dma_start(
                 wl_sc[32 * q : 32 * q + 4, :, :].bitcast(I32),
                 wl_scales[:, 4 * q : 4 * q + 4, :].rearrange("a r c -> r a c").bitcast(I32),
             )
-        tab = []
 
-        def load_table(a):
-            tab.append(slot(a, 0, [P, T], I32, f"tab{a}"))
-            nc.sync.dma_start(tab[a][:], tab_words[a].rearrange("p t i -> p (t i)").bitcast(I32))
-
-        for a in range(PASSES - 1):
-            load_table(a)
-
-        picked_sc = sbuf([P, S], U8, "picked_sc")
+        picked_sc = sbuf_at(TURNED + 2 * KB, [P, S], U8, "picked_sc")
         nc.vector.tensor_copy(picked_sc[:], tab_sc[:].indirect(idx[:]))
-        v_sc = []
-        for a in range(PASSES):
-            v_sc.append(sbuf([P, S], U8, f"v_sc{a}"))
-            clear(nc.vector, v_sc[a][:])
-        for k in range(PASSES * QUADS):
-            if k == MOVES_AHEAD:
-                load_table(PASSES - 1)
-            a, q = divmod(k, QUADS)
-            nc.sync.dma_start(
-                v_sc[a][32 * q : 32 * q + 4, :].bitcast(I32),
-                picked_sc[4 * k : 4 * k + 4, :].bitcast(I32),
+        v_sc = sbuf([P, PASSES, S], U8, "v_sc")
+        clear(nc.vector, v_sc[:].rearrange("p a s -> p (a s)"))
+        for q in range(QUADS):
+            nc.scalar.dma_start(
+                v_sc[32 * q : 32 * q + 4, :, :].bitcast(I32),
+                picked_sc[4 * PASSES * q : 4 * PASSES * (q + 1), :].bitcast(I32),
             )
-        gain1 = sbuf_at(PASSES * SLOT, [P, S], F32, "gain1")
+        gain1 = sbuf([P, S], F32, "gain1")
         nc.sync.dma_start(gain1[:], wg1)
         v_w = []
         for a in range(PASSES):
@@ -116,24 +108,24 @@ def tile_list_stereo_patch_pages_kernel(
                     tab[a][:].bitcast(U32).indirect(idx[:, i * n // 16 : (i + 1) * n // 16]),
                 )
 
-        pageA = [sbuf([P, T2], F32, f"pageA{i}") for i in range(ROW_TILES)]
-        pageB = [slot(i, 1, [P, T2], F32, f"pageB{i}") for i in range(2)]
+        pageA = [sbuf([P, T2], F32, f"pageA{i}") for i in range(3)]
+        pageB = [sbuf([P, T2], F32, f"pageB{i}") for i in range(2)]
         for page in pageA + pageB:
             nc.vector.memset(page[:], 0.0)
         ident = sbuf([P, P], F32, "ident")
         make_identity(nc, ident[:])
 
-        def features(a_row, weights, scales, h, negate):
+        def features(row, weights, scales, h, negate):
             for i in range(HALVES):
                 cols = slice(i * BANK, (i + 1) * BANK)
-                acc = bank([P, BANK], "acc")
+                acc = bank(2 * (row % 2) + i, [P, BANK], "acc")
                 for a in range(PASSES):
                     nc.tensor.matmul_mx(
                         acc[:],
-                        lhsT=weights(a, a_row),
-                        lhsT_scale=scales[:, a, a_row * P : (a_row + 1) * P],
+                        lhsT=weights(a, row),
+                        lhsT_scale=scales[:, a, row * P : (row + 1) * P],
                         rhs=v_w[a][:, cols].bitcast(E4M3),
-                        rhs_scale=v_sc[a][:, cols],
+                        rhs_scale=v_sc[:, a, cols],
                         start=(a == 0),
                         stop=(a == PASSES - 1),
                     )
@@ -156,15 +148,15 @@ def tile_list_stereo_patch_pages_kernel(
             return wl_w[:, a, 2 * P * r : 2 * P * (r + 1)].bitcast(E2M1)
 
         last = ROW_TILES - 1
-        for r, tag in ((0, "res2"), (1, "res1")):
-            h = features(r, left, wl_sc, sbuf([P, S], F32, f"h1_{r}", tag), False)
+        for r in range(2):
+            h = features(r, left, wl_sc, sbuf([P, S], F32, f"h1_{r}"), False)
             place(pageA[r], h, gain1, idx2, HALVES if r == 0 else 1)
 
-        wr_bf = sbuf([P, PASSES, H * PACK], BF16, "wr_bf", "res0")
+        wr_bf = sbuf([P, PASSES, H * PACK], BF16, "wr_bf")
         wr_w = sbuf([P, PASSES, H], U32, "wr_w")
         wr_sc = sbuf([P, PASSES, H], U8, "wr_sc")
         for a in range(PASSES):
-            raw = slot(a, 0, [P, PACK, H], F32, f"wr_raw{a}")
+            raw = slot(a // 2, a % 2, [P, PACK, H], F32, f"wr_raw{a}")
             nc.sync.dma_start(
                 raw[:], wr[a * P * PACK : (a + 1) * P * PACK, :].rearrange("(p t) c -> p t c", t=PACK)
             )
@@ -174,73 +166,17 @@ def tile_list_stereo_patch_pages_kernel(
             )
         for a in range(PASSES):
             nc.vector.quantize_mx(wr_w[:, a, :].bitcast(E4M3), wr_sc[:, a, :], wr_bf[:, a, :])
-        h = features(2, left, wl_sc, slot(PASSES - 1, 0, [P, S], F32, "h1_2"), False)
+        h = features(2, left, wl_sc, slot(1, 0, [P, S], F32, "h1_2"), False)
         place(pageA[2], h, gain1, idx2)
-        gain2 = sbuf([P, S], F32, "gain2", "picked_sc")
+        gain2 = sbuf_at(TURNED + 2 * KB, [P, S], F32, "gain2")
         nc.sync.dma_start(gain2[:], wg2)
 
         def right(a, r):
             return wr_w[:, a, P * r : P * (r + 1)].bitcast(E4M3)
 
-        h2 = [
-            features(r, right, wr_sc, sbuf([P, S], F32, f"h2_{r}", tag), True)
-            for r, tag in enumerate(("h_d", "h_e", "h_b", "h_c"))
-        ]
-
-        place(pageB[0], h2[0], gain2, idx3)
-        h = features(last, left, wl_sc, sbuf([P, S], F32, "h1_last", "h_d"), False)
-
-        band_bf = [sbuf([P, BANK * PACK], BF16, f"band_bf{c}") for c in range(CHUNKS)]
-        for c in range(CHUNKS):
-            if c < 2:
-                raw = slot(c, 0, [P, PACK, BANK], F32, f"band_raw{c}")
-            elif c == 2:
-                raw = slot(c, 1, [P, PACK, BANK], F32, f"band_raw{c}")
-            else:
-                raw = sbuf([P, PACK, BANK], F32, f"band_raw{c}", "wl_w")
-            nc.sync.dma_start(
-                raw[:], band[:, c * BANK : (c + 1) * BANK].rearrange("(p t) m -> p t m", t=PACK)
-            )
-            nc.scalar.copy(
-                band_bf[c][:].rearrange("p (m t) -> p m t", t=PACK), raw[:].rearrange("p t m -> p m t")
-            )
-        res = []
-        for s in range(3):
-            res.append(sbuf([P, 2, T2], F32, f"res{s}"))
-            nc.sync.dma_start(
-                res[s][:], style[2 * P * s : 2 * P * (s + 1), :].rearrange("(i p) m -> p i m", p=P)
-            )
-
-        gap = [sbuf([P, 2, BLOCKS, P, 2], BF16, f"gap{c}") for c in range(CHUNKS)]
-
-        def turn(turned, page, c, first):
-            for b in range(BLOCKS):
-                nc.tensor.matmul(
-                    turned[:, b, :], page[:, c * BANK + b * P : c * BANK + (b + 1) * P], ident[:],
-                    start=(first and b == 0), stop=(not first and b == BLOCKS - 1), is_transpose=True,
-                )
-
-        def magnitude(turned, r, c):
-            nc.scalar.activation(
-                gap[c][:, :, :, 32 * r : 32 * (r + 1), :],
-                turned[:].rearrange("m b (p u e) -> m u b p e", u=2, e=2),
-                ACT.Abs,
-            )
-
-        for r in range(last):
-            if r == 2:
-                place(pageA[last], h, gain1, idx2)
-            if r > 0:
-                place(pageB[r % 2], h2[r], gain2, idx3)
-            for c in range(CHUNKS):
-                turned = bank([P, BLOCKS, P], "turned")
-                turn(turned, pageA[r], c, True)
-                turn(turned, pageB[r % 2], c, False)
-                magnitude(turned, r, c)
-        place(pageB[last % 2], h2[last], gain2, idx3)
-        held = [bank([P, BLOCKS, P], "held") for c in range(CHUNKS)]
-        for c in range(CHUNKS):
-            turn(held[c], pageA[last], c, True)
+        h2 = [features(r, right, wr_sc, sbuf([P, S], F32, f"h2_{r}"), True) for r in range(last)]
+        h2.append(features(last, right, wr_sc, sbuf_at(TURNED + 10 * KB, [P, S], F32, "h2_last"), True))
+        h1_last = features(last, left, wl_sc, sbuf([P, S], F32, "h1_last"), False)
 
         wd_w = sbuf([P, N], I32, "wd_w", "v_w0")
         nc.sync.dma_start(wd_w[:], wd_words[0].rearrange("p c i -> p (c i)").bitcast(I32))
@@ -252,13 +188,68 @@ def tile_list_stereo_patch_pages_kernel(
                 wd_scales[0, 4 * q : 4 * q + 4, :].bitcast(I32),
             )
 
-        def weave(c):
-            turn(held[c], pageB[last % 2], c, False)
-            magnitude(held[c], last, c)
-            words = gap[c][:].rearrange("m u b p e -> m (u b p e)").bitcast(F32)
-            woven = sbuf([P, BANK, 2], F32, "woven", ("h_b", "h_c")[c % 2])
+        def turn(turned, page, c, start, stop):
+            for b in range(BLOCKS):
+                nc.tensor.matmul(
+                    turned[:, b, :], page[:, c * BANK + b * P : c * BANK + (b + 1) * P], ident[:],
+                    start=(start and b == 0), stop=(stop and b == BLOCKS - 1), is_transpose=True,
+                )
+
+        def rows_of(tile, first, count):
+            return tile[:, :, :, SPAN * first : SPAN * (first + count), :]
+
+        def leave_bank(dst, turned, r, func):
+            nc.scalar.activation(
+                rows_of(dst, r, 1), turned[:].rearrange("m b (p u e) -> m u b p e", u=2, e=2), func
+            )
+
+        floor = [sbuf([P, 2, BLOCKS, P, 2], BF16, f"floor{c}") for c in range(CHUNKS)]
+        for r in range(ROW_TILES):
+            raw = slot(2 if r < 2 else 0, r % 2, [P, T2], F32, f"band_raw{r}")
+            nc.sync.dma_start(raw[:], band[r * P : (r + 1) * P, :])
+            for c in range(CHUNKS):
+                turned = bank(4 + c, [P, BLOCKS, P], "band_turned")
+                turn(turned, raw, c, True, True)
+                leave_bank(floor[c], turned, r, ACT.Copy)
+        res = []
+        for s in range(PASSES):
+            res.append(slot(s, 0, [P, 2, T2], F32, f"res{s}"))
+            nc.sync.dma_start(
+                res[s][:], style[2 * P * s : 2 * P * (s + 1), :].rearrange("(i p) m -> p i m", p=P)
+            )
+
+        gap = [sbuf([P, 2, BLOCKS, P, 2], BF16, f"gap{c}") for c in range(CHUNKS)]
+        for r in range(last):
+            if r == 2:
+                place(pageA[0], h1_last, gain1, idx2)
+            place(pageB[r % 2], h2[r], gain2, idx3)
+            for c in range(CHUNKS):
+                turned = bank(4 + c, [P, BLOCKS, P], "turned")
+                turn(turned, pageA[r], c, True, False)
+                turn(turned, pageB[r % 2], c, False, True)
+                leave_bank(gap[c], turned, r, ACT.Abs)
+        held = [bank(c, [P, BLOCKS, P], "held") for c in range(CHUNKS)]
+        for c in range(CHUNKS):
+            turn(held[c], pageA[0], c, True, False)
+        place(pageB[last % 2], h2[last], gain2, idx3)
+        for c in range(CHUNKS):
+            turn(held[c], pageB[last % 2], c, False, True)
+            leave_bank(gap[c], held[c], last, ACT.Abs)
+
+        def floor_at_band(c):
+            z_t = sbuf_at(TURNED + 4 * KB * c, [P, 2, BLOCKS, P, 2], BF16, f"z_t{c}")
+            for first, count in ((0, last), (last, 1)):
+                nc.vector.tensor_tensor(
+                    rows_of(z_t, first, count), rows_of(gap[c], first, count),
+                    rows_of(floor[c], first, count), ALU.max,
+                )
+            return z_t
+
+        def weave(c, z_t):
+            words = z_t[:].rearrange("m u b p e -> m (u b p e)").bitcast(F32)
+            woven = sbuf([P, BANK, 2], F32, "woven", bufs=2)
             for k in range(2):
-                back = bank([P, 2, 2 * P], "back")
+                back = bank(4 + 2 * (c % 2) + k, [P, 2, 2 * P], "back")
                 for u in range(2):
                     for b in range(2):
                         w0 = (u * BLOCKS + 2 * k + b) * P
@@ -270,24 +261,19 @@ def tile_list_stereo_patch_pages_kernel(
                 )
             return woven
 
-        def floor_at_band(c, woven):
-            z = sbuf([P, BANK * PACK], BF16, "z", ("h_d", "h_e")[c % 2])
-            nc.vector.tensor_tensor(
-                z[:], woven[:].rearrange("p m u -> p (m u)").bitcast(BF16), band_bf[c][:], ALU.max
+        def quantise(c, woven):
+            z_w = sbuf([P, BANK], U32, f"z_w{c}")
+            z_sc = sbuf([P, BANK], U8, f"z_sc{c}")
+            nc.vector.quantize_mx(
+                z_w[:].bitcast(E4M3), z_sc[:], woven[:].rearrange("p m u -> p (m u)").bitcast(BF16)
             )
-            return z
-
-        def quantise(z):
-            z_w = sbuf([P, BANK], U32, "z_w", bufs=2)
-            z_sc = sbuf([P, BANK], U8, "z_sc", bufs=2)
-            nc.vector.quantize_mx(z_w[:].bitcast(E4M3), z_sc[:], z[:])
             return z_w, z_sc
 
-        def project(c, z_mx, tiles):
+        def project(c, z_mx):
             cols = slice(c * BANK, (c + 1) * BANK)
-            for n in tiles:
+            for n in range(OUT_TILES):
                 rows = slice(n * P, (n + 1) * P)
-                acc = bank([P, BANK], "acc")
+                acc = bank((c * OUT_TILES + n) % 4, [P, BANK], "acc")
                 nc.tensor.matmul_mx(
                     acc[:],
                     lhsT=wd_w[:, rows].bitcast(E4M3),
@@ -301,15 +287,6 @@ def tile_list_stereo_patch_pages_kernel(
                 nc.vector.tensor_tensor(total, total, acc[:], ALU.add)
                 nc.sync.dma_start(out[rows, cols], total)
 
-        z_mx = quantise(floor_at_band(0, weave(0)))
-        woven = weave(1)
+        z_mx = [quantise(c, weave(c, floor_at_band(c))) for c in range(CHUNKS)]
         for c in range(CHUNKS):
-            if c + 1 < CHUNKS:
-                z = floor_at_band(c + 1, woven)
-            project(c, z_mx, range(0, 3))
-            if c + 1 < CHUNKS:
-                z_next = quantise(z)
-            if c + 2 < CHUNKS:
-                woven = weave(c + 2)
-            project(c, z_mx, range(3, 6))
-            z_mx = z_next
+            project(c, z_mx[c])

@@ -1,7 +1,6 @@
 from contextlib import ExitStack
 
 import concourse.mybir as mybir
-from concourse.masks import make_identity
 
 K, H, N, T, S, T2 = 1536, 512, 768, 4096, 1024, 2048
 FLOPS = 2 * (2 * K * H * S + H * N * T2)
@@ -31,7 +30,8 @@ SPAN = P // ROW_TILES
 ALIGN = 64
 KB = 1024
 SLOT = 16 * KB
-TURNED = PASSES * SLOT
+SPARE = PASSES * SLOT + 4 * KB
+TURNED = SPARE + SLOT
 
 
 def tile_list_stereo_patch_pages_kernel(
@@ -65,19 +65,32 @@ def tile_list_stereo_patch_pages_kernel(
         idx3 = lists.tile([P, S // 16], U16, name="idx3")
 
         nc.sync.dma_start(idx[:], offs)
-        nc.sync.dma_start(idx2[:], offs2)
-        nc.sync.dma_start(idx3[:], offs3)
         wl_w = sbuf([P, PASSES, 2 * H], U8, "wl_w")
         nc.sync.dma_start(wl_w[:].bitcast(I32), wl_words.rearrange("a p c -> p a c").bitcast(I32))
-        tab = [slot(a, 0, [P, T], I32, f"tab{a}") for a in range(PASSES)]
+        nc.sync.dma_start(idx2[:], offs2)
+        nc.sync.dma_start(idx3[:], offs3)
+        tab_sc = sbuf_at(PASSES * SLOT - T // 2, [P, T], U8, "tab_sc")
+        clear(nc.gpsimd, tab_sc[:, 0 : T // 2])
+        clear(nc.vector, tab_sc[:, T // 2 : T])
         for a in range(PASSES):
-            nc.sync.dma_start(tab[a][:], tab_words[a].rearrange("p t i -> p (t i)").bitcast(I32))
-        tab_sc = sbuf([P, T], U8, "tab_sc", "gain1")
-        clear(nc.vector, tab_sc[:])
-        nc.scalar.dma_start(
-            tab_sc[0 : PASSES * 16, :].bitcast(I32),
-            tab_scales.rearrange("a q t -> q a t").bitcast(I32),
+            nc.sync.dma_start(
+                tab_sc[a : PASSES * 16 : PASSES, :].bitcast(I32), tab_scales[a].bitcast(I32)
+            )
+        zeros = sbuf_at(SLOT - 2 * P, [P, P], F32, "zeros")
+        nc.vector.memset(zeros[:], 0.0)
+        ident = sbuf([P, P], F32, "ident")
+        nc.gpsimd.affine_select(
+            out=ident[:], in_=zeros[:], compare_op=ALU.not_equal, fill=1.0, base=0,
+            pattern=[[-1, P]], channel_multiplier=1,
         )
+        tab = []
+
+        def load_table(a):
+            tab.append(slot(a, 0, [P, T], I32, f"tab{a}"))
+            nc.sync.dma_start(tab[a][:], tab_words[a].rearrange("p t i -> p (t i)").bitcast(I32))
+
+        for a in range(PASSES - 1):
+            load_table(a)
         wl_sc = sbuf([P, PASSES, H], U8, "wl_sc", "w_sc")
         clear(nc.gpsimd, wl_sc[:].rearrange("p a c -> p (a c)"))
         for q in range(QUADS):
@@ -86,7 +99,7 @@ def tile_list_stereo_patch_pages_kernel(
                 wl_scales[:, 4 * q : 4 * q + 4, :].rearrange("a r c -> r a c").bitcast(I32),
             )
 
-        picked_sc = sbuf_at(TURNED + 2 * KB, [P, S], U8, "picked_sc")
+        picked_sc = sbuf([P, S], U8, "picked_sc")
         nc.vector.tensor_copy(picked_sc[:], tab_sc[:].indirect(idx[:]))
         v_sc = sbuf([P, PASSES, S], U8, "v_sc")
         clear(nc.vector, v_sc[:].rearrange("p a s -> p (a s)"))
@@ -95,7 +108,8 @@ def tile_list_stereo_patch_pages_kernel(
                 v_sc[32 * q : 32 * q + 4, :, :].bitcast(I32),
                 picked_sc[4 * PASSES * q : 4 * PASSES * (q + 1), :].bitcast(I32),
             )
-        gain1 = sbuf([P, S], F32, "gain1")
+        load_table(PASSES - 1)
+        gain1 = sbuf_at(PASSES * SLOT, [P, S], F32, "gain1")
         nc.sync.dma_start(gain1[:], wg1)
         v_w = []
         for a in range(PASSES):
@@ -109,11 +123,9 @@ def tile_list_stereo_patch_pages_kernel(
                 )
 
         pageA = [sbuf([P, T2], F32, f"pageA{i}") for i in range(3)]
-        pageB = [sbuf([P, T2], F32, f"pageB{i}") for i in range(2)]
+        pageB = [slot(0, i, [P, T2], F32, f"pageB{i}") for i in range(2)]
         for page in pageA + pageB:
             nc.vector.memset(page[:], 0.0)
-        ident = sbuf([P, P], F32, "ident")
-        make_identity(nc, ident[:])
 
         def features(row, weights, scales, h, negate):
             for i in range(HALVES):
@@ -148,15 +160,15 @@ def tile_list_stereo_patch_pages_kernel(
             return wl_w[:, a, 2 * P * r : 2 * P * (r + 1)].bitcast(E2M1)
 
         last = ROW_TILES - 1
-        for r in range(2):
-            h = features(r, left, wl_sc, sbuf([P, S], F32, f"h1_{r}"), False)
+        for r, at in enumerate((TURNED + 2 * KB, SPARE)):
+            h = features(r, left, wl_sc, sbuf_at(at, [P, S], F32, f"h1_{r}"), False)
             place(pageA[r], h, gain1, idx2, HALVES if r == 0 else 1)
 
         wr_bf = sbuf([P, PASSES, H * PACK], BF16, "wr_bf")
         wr_w = sbuf([P, PASSES, H], U32, "wr_w")
         wr_sc = sbuf([P, PASSES, H], U8, "wr_sc")
         for a in range(PASSES):
-            raw = slot(a // 2, a % 2, [P, PACK, H], F32, f"wr_raw{a}")
+            raw = slot(1 + a // 2, a % 2, [P, PACK, H], F32, f"wr_raw{a}")
             nc.sync.dma_start(
                 raw[:], wr[a * P * PACK : (a + 1) * P * PACK, :].rearrange("(p t) c -> p t c", t=PACK)
             )
@@ -166,7 +178,7 @@ def tile_list_stereo_patch_pages_kernel(
             )
         for a in range(PASSES):
             nc.vector.quantize_mx(wr_w[:, a, :].bitcast(E4M3), wr_sc[:, a, :], wr_bf[:, a, :])
-        h = features(2, left, wl_sc, slot(1, 0, [P, S], F32, "h1_2"), False)
+        h = features(2, left, wl_sc, slot(2, 0, [P, S], F32, "h1_2"), False)
         place(pageA[2], h, gain1, idx2)
         gain2 = sbuf_at(TURNED + 2 * KB, [P, S], F32, "gain2")
         nc.sync.dma_start(gain2[:], wg2)
@@ -205,15 +217,20 @@ def tile_list_stereo_patch_pages_kernel(
 
         floor = [sbuf([P, 2, BLOCKS, P, 2], BF16, f"floor{c}") for c in range(CHUNKS)]
         for r in range(ROW_TILES):
-            raw = slot(2 if r < 2 else 0, r % 2, [P, T2], F32, f"band_raw{r}")
+            if r == 0:
+                raw = slot(2, 1, [P, T2], F32, "band_raw0")
+            elif r < last:
+                raw = slot(1, r - 1, [P, T2], F32, f"band_raw{r}")
+            else:
+                raw = sbuf([P, T2], F32, "band_raw_last", "wr_bf")
             nc.sync.dma_start(raw[:], band[r * P : (r + 1) * P, :])
             for c in range(CHUNKS):
                 turned = bank(4 + c, [P, BLOCKS, P], "band_turned")
                 turn(turned, raw, c, True, True)
                 leave_bank(floor[c], turned, r, ACT.Copy)
         res = []
-        for s in range(PASSES):
-            res.append(slot(s, 0, [P, 2, T2], F32, f"res{s}"))
+        for s, at in enumerate((SPARE, SLOT, 2 * SLOT)):
+            res.append(sbuf_at(at, [P, 2, T2], F32, f"res{s}"))
             nc.sync.dma_start(
                 res[s][:], style[2 * P * s : 2 * P * (s + 1), :].rearrange("(i p) m -> p i m", p=P)
             )

@@ -1,6 +1,7 @@
 from contextlib import ExitStack
 
 import concourse.mybir as mybir
+from concourse.masks import make_identity
 
 K, H, N, T, S, T2 = 1536, 512, 768, 4096, 1024, 2048
 FLOPS = 2 * (2 * K * H * S + H * N * T2)
@@ -28,6 +29,7 @@ BLOCKS = BANK // P
 QUADS = 4
 SPAN = P // ROW_TILES
 ALIGN = 64
+SC0 = 16
 KB = 1024
 SLOT = 16 * KB
 SPARE = PASSES * SLOT + 4 * KB
@@ -67,22 +69,13 @@ def tile_list_stereo_patch_pages_kernel(
         nc.sync.dma_start(idx[:], offs)
         wl_w = sbuf([P, PASSES, 2 * H], U8, "wl_w")
         nc.sync.dma_start(wl_w[:].bitcast(I32), wl_words.rearrange("a p c -> p a c").bitcast(I32))
-        nc.sync.dma_start(idx2[:], offs2)
-        nc.sync.dma_start(idx3[:], offs3)
         tab_sc = sbuf_at(PASSES * SLOT - T // 2, [P, T], U8, "tab_sc")
-        clear(nc.gpsimd, tab_sc[:, 0 : T // 2])
-        clear(nc.vector, tab_sc[:, T // 2 : T])
-        for a in range(PASSES):
-            nc.sync.dma_start(
-                tab_sc[a : PASSES * 16 : PASSES, :].bitcast(I32), tab_scales[a].bitcast(I32)
-            )
-        zeros = sbuf_at(SLOT - 2 * P, [P, P], F32, "zeros")
-        nc.vector.memset(zeros[:], 0.0)
-        ident = sbuf([P, P], F32, "ident")
-        nc.gpsimd.affine_select(
-            out=ident[:], in_=zeros[:], compare_op=ALU.not_equal, fill=1.0, base=0,
-            pattern=[[-1, P]], channel_multiplier=1,
+        nc.sync.dma_start(
+            tab_sc[SC0 : SC0 + PASSES * 16, :].bitcast(I32),
+            tab_scales.rearrange("a q t -> q a t").bitcast(I32),
         )
+        clear(nc.vector, tab_sc[0:SC0, :])
+        clear(nc.vector, tab_sc[SC0 + PASSES * 16 : P, :])
         tab = []
 
         def load_table(a):
@@ -91,22 +84,24 @@ def tile_list_stereo_patch_pages_kernel(
 
         for a in range(PASSES - 1):
             load_table(a)
-        wl_sc = sbuf([P, PASSES, H], U8, "wl_sc", "w_sc")
-        clear(nc.gpsimd, wl_sc[:].rearrange("p a c -> p (a c)"))
+        nc.sync.dma_start(idx2[:], offs2)
+        nc.sync.dma_start(idx3[:], offs3)
+        wl_sc = sbuf([P, PASSES * H], U8, "wl_sc", "w_sc")
+        clear(nc.gpsimd, wl_sc[:])
         for q in range(QUADS):
             nc.gpsimd.dma_start(
-                wl_sc[32 * q : 32 * q + 4, :, :].bitcast(I32),
+                wl_sc[32 * q : 32 * q + 4, :].bitcast(I32).rearrange("r (a c) -> r a c", a=PASSES),
                 wl_scales[:, 4 * q : 4 * q + 4, :].rearrange("a r c -> r a c").bitcast(I32),
             )
 
         picked_sc = sbuf([P, S], U8, "picked_sc")
         nc.vector.tensor_copy(picked_sc[:], tab_sc[:].indirect(idx[:]))
-        v_sc = sbuf([P, PASSES, S], U8, "v_sc")
-        clear(nc.vector, v_sc[:].rearrange("p a s -> p (a s)"))
+        v_sc = sbuf([P, PASSES * S], U8, "v_sc")
+        clear(nc.vector, v_sc[:])
         for q in range(QUADS):
-            nc.scalar.dma_start(
-                v_sc[32 * q : 32 * q + 4, :, :].bitcast(I32),
-                picked_sc[4 * PASSES * q : 4 * PASSES * (q + 1), :].bitcast(I32),
+            nc.sync.dma_start(
+                v_sc[32 * q : 32 * q + 4, :].bitcast(I32).rearrange("r (a s) -> r a s", a=PASSES),
+                picked_sc[SC0 + 4 * PASSES * q : SC0 + 4 * PASSES * (q + 1), :].bitcast(I32),
             )
         load_table(PASSES - 1)
         gain1 = sbuf_at(PASSES * SLOT, [P, S], F32, "gain1")
@@ -126,6 +121,8 @@ def tile_list_stereo_patch_pages_kernel(
         pageB = [slot(0, i, [P, T2], F32, f"pageB{i}") for i in range(2)]
         for page in pageA + pageB:
             nc.vector.memset(page[:], 0.0)
+        ident = sbuf([P, P], F32, "ident")
+        make_identity(nc, ident[:])
 
         def features(row, weights, scales, h, negate):
             for i in range(HALVES):
@@ -135,9 +132,9 @@ def tile_list_stereo_patch_pages_kernel(
                     nc.tensor.matmul_mx(
                         acc[:],
                         lhsT=weights(a, row),
-                        lhsT_scale=scales[:, a, row * P : (row + 1) * P],
+                        lhsT_scale=scales[:, a * H + row * P : a * H + (row + 1) * P],
                         rhs=v_w[a][:, cols].bitcast(E4M3),
-                        rhs_scale=v_sc[:, a, cols],
+                        rhs_scale=v_sc[:, a * S + i * BANK : a * S + (i + 1) * BANK],
                         start=(a == 0),
                         stop=(a == PASSES - 1),
                     )
@@ -166,7 +163,7 @@ def tile_list_stereo_patch_pages_kernel(
 
         wr_bf = sbuf([P, PASSES, H * PACK], BF16, "wr_bf")
         wr_w = sbuf([P, PASSES, H], U32, "wr_w")
-        wr_sc = sbuf([P, PASSES, H], U8, "wr_sc")
+        wr_sc = sbuf([P, PASSES * H], U8, "wr_sc")
         for a in range(PASSES):
             raw = slot(1 + a // 2, a % 2, [P, PACK, H], F32, f"wr_raw{a}")
             nc.sync.dma_start(
@@ -177,7 +174,7 @@ def tile_list_stereo_patch_pages_kernel(
                 raw[:].rearrange("p t c -> p c t"),
             )
         for a in range(PASSES):
-            nc.vector.quantize_mx(wr_w[:, a, :].bitcast(E4M3), wr_sc[:, a, :], wr_bf[:, a, :])
+            nc.vector.quantize_mx(wr_w[:, a, :].bitcast(E4M3), wr_sc[:, a * H : (a + 1) * H], wr_bf[:, a, :])
         h = features(2, left, wl_sc, slot(2, 0, [P, S], F32, "h1_2"), False)
         place(pageA[2], h, gain1, idx2)
         gain2 = sbuf_at(TURNED + 2 * KB, [P, S], F32, "gain2")

@@ -29,7 +29,7 @@ BLOCKS = BANK // P
 QUADS = 4
 SPAN = P // ROW_TILES
 ALIGN = 64
-SC0 = 16
+SC0 = P - PASSES * 16
 KB = 1024
 SLOT = 16 * KB
 SPARE = PASSES * SLOT + 4 * KB
@@ -75,7 +75,6 @@ def tile_list_stereo_patch_pages_kernel(
             tab_scales.rearrange("a q t -> q a t").bitcast(I32),
         )
         clear(nc.vector, tab_sc[0:SC0, :])
-        clear(nc.vector, tab_sc[SC0 + PASSES * 16 : P, :])
         tab = []
 
         def load_table(a):
@@ -157,9 +156,10 @@ def tile_list_stereo_patch_pages_kernel(
             return wl_w[:, a, 2 * P * r : 2 * P * (r + 1)].bitcast(E2M1)
 
         last = ROW_TILES - 1
-        for r, at in enumerate((TURNED + 2 * KB, SPARE)):
+        for r, at in enumerate((TURNED + 2 * KB, TURNED + 10 * KB)):
             h = features(r, left, wl_sc, sbuf_at(at, [P, S], F32, f"h1_{r}"), False)
             place(pageA[r], h, gain1, idx2, HALVES if r == 0 else 1)
+        h1_last = features(last, left, wl_sc, sbuf([P, S], F32, "h1_last"), False)
 
         wr_bf = sbuf([P, PASSES, H * PACK], BF16, "wr_bf")
         wr_w = sbuf([P, PASSES, H], U32, "wr_w")
@@ -183,9 +183,10 @@ def tile_list_stereo_patch_pages_kernel(
         def right(a, r):
             return wr_w[:, a, P * r : P * (r + 1)].bitcast(E4M3)
 
-        h2 = [features(r, right, wr_sc, sbuf([P, S], F32, f"h2_{r}"), True) for r in range(last)]
-        h2.append(features(last, right, wr_sc, sbuf_at(TURNED + 10 * KB, [P, S], F32, "h2_last"), True))
-        h1_last = features(last, left, wl_sc, sbuf([P, S], F32, "h1_last"), False)
+        h2 = [
+            features(r, right, wr_sc, sbuf_at(at, [P, S], F32, f"h2_{r}"), True)
+            for r, at in enumerate((SPARE, SPARE + 4 * KB, SPARE + 8 * KB, TURNED + 10 * KB))
+        ]
 
         wd_w = sbuf([P, N], I32, "wd_w", "v_w0")
         nc.sync.dma_start(wd_w[:], wd_words[0].rearrange("p c i -> p (c i)").bitcast(I32))
@@ -246,7 +247,8 @@ def tile_list_stereo_patch_pages_kernel(
         for c in range(CHUNKS):
             turn(held[c], pageA[0], c, True, False)
         place(pageB[last % 2], h2[last], gain2, idx3)
-        for c in range(CHUNKS):
+
+        def close_gap(c):
             turn(held[c], pageB[last % 2], c, False, True)
             leave_bank(gap[c], held[c], last, ACT.Abs)
 
@@ -283,9 +285,9 @@ def tile_list_stereo_patch_pages_kernel(
             )
             return z_w, z_sc
 
-        def project(c, z_mx):
+        def project(c, z_mx, tiles):
             cols = slice(c * BANK, (c + 1) * BANK)
-            for n in range(OUT_TILES):
+            for n in tiles:
                 rows = slice(n * P, (n + 1) * P)
                 acc = bank((c * OUT_TILES + n) % 4, [P, BANK], "acc")
                 nc.tensor.matmul_mx(
@@ -301,6 +303,17 @@ def tile_list_stereo_patch_pages_kernel(
                 nc.vector.tensor_tensor(total, total, acc[:], ALU.add)
                 nc.sync.dma_start(out[rows, cols], total)
 
-        z_mx = [quantise(c, weave(c, floor_at_band(c))) for c in range(CHUNKS)]
+        close_gap(0)
+        z_mx = quantise(0, weave(0, floor_at_band(0)))
+        close_gap(1)
+        woven = weave(1, floor_at_band(1))
+        for c in range(2, CHUNKS):
+            close_gap(c)
         for c in range(CHUNKS):
-            project(c, z_mx[c])
+            project(c, z_mx, range(0, 2))
+            if c + 1 < CHUNKS:
+                z_next = quantise(c + 1, woven)
+            if c + 2 < CHUNKS:
+                woven = weave(c + 2, floor_at_band(c + 2))
+            project(c, z_mx, range(2, OUT_TILES))
+            z_mx = z_next

@@ -32,7 +32,9 @@ ALIGN = 64
 SC0 = P - PASSES * 16
 KB = 1024
 SLOT = 16 * KB
-SPARE = PASSES * SLOT + 4 * KB
+HALF = SLOT // 2
+THIRD = 2 * SLOT + HALF
+SPARE = THIRD + SLOT + 4 * KB
 TURNED = SPARE + SLOT
 
 
@@ -69,7 +71,7 @@ def tile_list_stereo_patch_pages_kernel(
         nc.sync.dma_start(idx[:], offs)
         wl_w = sbuf([P, PASSES, 2 * H], U8, "wl_w")
         nc.sync.dma_start(wl_w[:].bitcast(I32), wl_words.rearrange("a p c -> p a c").bitcast(I32))
-        tab_sc = sbuf_at(PASSES * SLOT - T // 2, [P, T], U8, "tab_sc")
+        tab_sc = sbuf_at(THIRD + SLOT - T // 2, [P, T], U8, "tab_sc")
         nc.sync.dma_start(
             tab_sc[SC0 : SC0 + PASSES * 16, :].bitcast(I32),
             tab_scales.rearrange("a q t -> q a t").bitcast(I32),
@@ -78,7 +80,7 @@ def tile_list_stereo_patch_pages_kernel(
         tab = []
 
         def load_table(a):
-            tab.append(slot(a, 0, [P, T], I32, f"tab{a}"))
+            tab.append(sbuf_at((0, SLOT, THIRD - ALIGN)[a], [P, T], I32, f"tab{a}"))
             nc.sync.dma_start(tab[a][:], tab_words[a].rearrange("p t i -> p (t i)").bitcast(I32))
 
         for a in range(PASSES - 1):
@@ -103,9 +105,12 @@ def tile_list_stereo_patch_pages_kernel(
                 picked_sc[SC0 + 4 * PASSES * q : SC0 + 4 * PASSES * (q + 1), :].bitcast(I32),
             )
         load_table(PASSES - 1)
-        gain1 = sbuf_at(PASSES * SLOT, [P, S], F32, "gain1")
+        gain1 = sbuf_at(THIRD + SLOT, [P, S], F32, "gain1")
         nc.sync.dma_start(gain1[:], wg1)
-        v_w = []
+        pageA = [sbuf([P, T2], F32, f"pageA{i}") for i in range(2)]
+        for page in pageA:
+            nc.vector.memset(page[:], 0.0)
+        v_w, pageB = [], []
         for a in range(PASSES):
             v_w.append(sbuf([P, S], U32, f"v_w{a}"))
             pieces = HALVES if a == PASSES - 1 else 1
@@ -115,68 +120,71 @@ def tile_list_stereo_patch_pages_kernel(
                     v_w[a][:, i * n : (i + 1) * n],
                     tab[a][:].bitcast(U32).indirect(idx[:, i * n // 16 : (i + 1) * n // 16]),
                 )
+            if a < 2:
+                pageB.append(slot(a, 0, [P, T2], F32, f"pageB{a}"))
+                nc.vector.memset(pageB[a][:], 0.0)
 
-        pageA = [sbuf([P, T2], F32, f"pageA{i}") for i in range(3)]
-        pageB = [slot(0, i, [P, T2], F32, f"pageB{i}") for i in range(2)]
-        for page in pageA + pageB:
-            nc.vector.memset(page[:], 0.0)
         ident = sbuf([P, P], F32, "ident")
         make_identity(nc, ident[:])
 
+        def half_features(row, i, weights, scales, dst, negate):
+            cols = slice(i * BANK, (i + 1) * BANK)
+            acc = bank(2 * (row % 2) + i, [P, BANK], "acc")
+            for a in range(PASSES):
+                nc.tensor.matmul_mx(
+                    acc[:],
+                    lhsT=weights(a, row),
+                    lhsT_scale=scales[:, a * H + row * P : a * H + (row + 1) * P],
+                    rhs=v_w[a][:, cols].bitcast(E4M3),
+                    rhs_scale=v_sc[:, a * S + i * BANK : a * S + (i + 1) * BANK],
+                    start=(a == 0),
+                    stop=(a == PASSES - 1),
+                )
+            if negate:
+                nc.scalar.activation(dst, acc[:], ACT.Copy, scale=-1.0)
+            else:
+                nc.scalar.copy(dst, acc[:])
+
         def features(row, weights, scales, h, negate):
             for i in range(HALVES):
-                cols = slice(i * BANK, (i + 1) * BANK)
-                acc = bank(2 * (row % 2) + i, [P, BANK], "acc")
-                for a in range(PASSES):
-                    nc.tensor.matmul_mx(
-                        acc[:],
-                        lhsT=weights(a, row),
-                        lhsT_scale=scales[:, a * H + row * P : a * H + (row + 1) * P],
-                        rhs=v_w[a][:, cols].bitcast(E4M3),
-                        rhs_scale=v_sc[:, a * S + i * BANK : a * S + (i + 1) * BANK],
-                        start=(a == 0),
-                        stop=(a == PASSES - 1),
-                    )
-                if negate:
-                    nc.scalar.activation(h[:, cols], acc[:], ACT.Copy, scale=-1.0)
-                else:
-                    nc.scalar.copy(h[:, cols], acc[:])
+                half_features(row, i, weights, scales, h[:, i * BANK : (i + 1) * BANK], negate)
             return h
 
-        def place(page, h, gain, places, pieces=1):
-            n = S // pieces
-            for i in range(pieces):
-                cols = slice(i * n, (i + 1) * n)
-                nc.vector.tensor_tensor(
-                    page[:].indirect(places[:, i * n // 16 : (i + 1) * n // 16]),
-                    h[:, cols], gain[:, cols], ALU.mult,
-                )
+        def place(page, h, gain, places, first=0, count=S):
+            nc.vector.tensor_tensor(
+                page[:].indirect(places[:, first // 16 : (first + count) // 16]),
+                h, gain[:, first : first + count], ALU.mult,
+            )
 
         def left(a, r):
             return wl_w[:, a, 2 * P * r : 2 * P * (r + 1)].bitcast(E2M1)
 
         last = ROW_TILES - 1
-        for r, at in enumerate((TURNED + 2 * KB, TURNED + 10 * KB)):
-            h = features(r, left, wl_sc, sbuf_at(at, [P, S], F32, f"h1_{r}"), False)
-            place(pageA[r], h, gain1, idx2, HALVES if r == 0 else 1)
-        h1_last = features(last, left, wl_sc, sbuf([P, S], F32, "h1_last"), False)
+        h = features(0, left, wl_sc, sbuf_at(TURNED + 2 * KB, [P, S], F32, "h1_0"), False)
+        for i in range(HALVES):
+            place(pageA[0], h[:, i * BANK : (i + 1) * BANK], gain1, idx2, i * BANK, BANK)
+        h = sbuf([P, BANK], F32, "h1_1a")
+        half_features(1, 0, left, wl_sc, h[:], False)
+        place(pageA[1], h[:], gain1, idx2, 0, BANK)
 
         wr_bf = sbuf([P, PASSES, H * PACK], BF16, "wr_bf")
         wr_w = sbuf([P, PASSES, H], U32, "wr_w")
         wr_sc = sbuf([P, PASSES * H], U8, "wr_sc")
         for a in range(PASSES):
-            raw = slot(1 + a // 2, a % 2, [P, PACK, H], F32, f"wr_raw{a}")
+            raw = sbuf_at((HALF, SLOT + HALF, THIRD)[a], [P, PACK, H], F32, f"wr_raw{a}")
             nc.sync.dma_start(
                 raw[:], wr[a * P * PACK : (a + 1) * P * PACK, :].rearrange("(p t) c -> p t c", t=PACK)
             )
             nc.scalar.copy(
-                wr_bf[:, a, :].rearrange("p (c t) -> p c t", t=PACK),
-                raw[:].rearrange("p t c -> p c t"),
+                wr_bf[:, a, :].rearrange("p (c i t) -> p c t i", i=PACK, t=PACK),
+                raw[:].rearrange("p t (c i) -> p c t i", i=PACK),
             )
+        h = sbuf_at(THIRD, [P, BANK], F32, "h1_1b")
+        half_features(1, 1, left, wl_sc, h[:], False)
+        h1 = {r: features(r, left, wl_sc, sbuf([P, S], F32, f"h1_{r}"), False) for r in (2, last)}
         for a in range(PASSES):
             nc.vector.quantize_mx(wr_w[:, a, :].bitcast(E4M3), wr_sc[:, a * H : (a + 1) * H], wr_bf[:, a, :])
-        h = features(2, left, wl_sc, slot(2, 0, [P, S], F32, "h1_2"), False)
-        place(pageA[2], h, gain1, idx2)
+        place(pageA[1], h[:], gain1, idx2, BANK, BANK)
         gain2 = sbuf_at(TURNED + 2 * KB, [P, S], F32, "gain2")
         nc.sync.dma_start(gain2[:], wg2)
 
@@ -185,7 +193,7 @@ def tile_list_stereo_patch_pages_kernel(
 
         h2 = [
             features(r, right, wr_sc, sbuf_at(at, [P, S], F32, f"h2_{r}"), True)
-            for r, at in enumerate((SPARE, SPARE + 4 * KB, SPARE + 8 * KB, TURNED + 10 * KB))
+            for r, at in enumerate((SPARE, SPARE + HALF, THIRD + 4 * KB, TURNED + 10 * KB))
         ]
 
         wd_w = sbuf([P, N], I32, "wd_w", "v_w0")
@@ -214,39 +222,40 @@ def tile_list_stereo_patch_pages_kernel(
             )
 
         floor = [sbuf([P, 2, BLOCKS, P, 2], BF16, f"floor{c}") for c in range(CHUNKS)]
-        for r in range(ROW_TILES):
-            if r == 0:
-                raw = slot(2, 1, [P, T2], F32, "band_raw0")
-            elif r < last:
-                raw = slot(1, r - 1, [P, T2], F32, f"band_raw{r}")
-            else:
-                raw = sbuf([P, T2], F32, "band_raw_last", "wr_bf")
-            nc.sync.dma_start(raw[:], band[r * P : (r + 1) * P, :])
+        band_raw = []
+        for r, at in enumerate((THIRD + HALF, 2 * SLOT, HALF, SLOT + HALF)):
+            band_raw.append(sbuf_at(at, [P, T2], F32, f"band_raw{r}"))
+            nc.sync.dma_start(band_raw[r][:], band[r * P : (r + 1) * P, :])
+
+        def turn_band(r):
             for c in range(CHUNKS):
                 turned = bank(4 + c, [P, BLOCKS, P], "band_turned")
-                turn(turned, raw, c, True, True)
+                turn(turned, band_raw[r], c, True, True)
                 leave_bank(floor[c], turned, r, ACT.Copy)
-        res = []
-        for s, at in enumerate((SPARE, SLOT, 2 * SLOT)):
-            res.append(sbuf_at(at, [P, 2, T2], F32, f"res{s}"))
-            nc.sync.dma_start(
-                res[s][:], style[2 * P * s : 2 * P * (s + 1), :].rearrange("(i p) m -> p i m", p=P)
-            )
+
+        turn_band(0)
 
         gap = [sbuf([P, 2, BLOCKS, P, 2], BF16, f"gap{c}") for c in range(CHUNKS)]
         for r in range(last):
             if r == 2:
-                place(pageA[0], h1_last, gain1, idx2)
-            place(pageB[r % 2], h2[r], gain2, idx3)
+                place(pageA[0], h1[r][:], gain1, idx2)
+            place(pageB[r % 2], h2[r][:], gain2, idx3)
             for c in range(CHUNKS):
                 turned = bank(4 + c, [P, BLOCKS, P], "turned")
-                turn(turned, pageA[r], c, True, False)
+                turn(turned, pageA[r % 2], c, True, False)
                 turn(turned, pageB[r % 2], c, False, True)
                 leave_bank(gap[c], turned, r, ACT.Abs)
+            for later in ((1,), (2, 3), ())[r]:
+                turn_band(later)
+        res = []
+        for n, at in enumerate((SPARE, SPARE + HALF, HALF, SLOT + HALF, THIRD - ALIGN, THIRD + HALF - ALIGN)):
+            res.append(sbuf_at(at, [P, T2], F32, f"res{n}"))
+            nc.sync.dma_start(res[n][:], style[n * P : (n + 1) * P, :])
+        place(pageA[last % 2], h1[last][:], gain1, idx2)
         held = [bank(c, [P, BLOCKS, P], "held") for c in range(CHUNKS)]
         for c in range(CHUNKS):
-            turn(held[c], pageA[0], c, True, False)
-        place(pageB[last % 2], h2[last], gain2, idx3)
+            turn(held[c], pageA[last % 2], c, True, False)
+        place(pageB[last % 2], h2[last][:], gain2, idx3)
 
         def close_gap(c):
             turn(held[c], pageB[last % 2], c, False, True)
@@ -299,7 +308,7 @@ def tile_list_stereo_patch_pages_kernel(
                     start=True,
                     stop=True,
                 )
-                total = res[n // 2][:, n % 2, cols]
+                total = res[n][:, cols]
                 nc.vector.tensor_tensor(total, total, acc[:], ALU.add)
                 nc.sync.dma_start(out[rows, cols], total)
 

@@ -107,7 +107,7 @@ def tile_list_stereo_patch_pages_kernel(
         load_table(PASSES - 1)
         gain1 = sbuf_at(THIRD + SLOT, [P, S], F32, "gain1")
         nc.sync.dma_start(gain1[:], wg1)
-        pageA = [sbuf([P, T2], F32, f"pageA{i}") for i in range(2)]
+        pageA = [sbuf([P, T2], F32, f"pageA{i}") for i in range(3)]
         for page in pageA:
             nc.vector.memset(page[:], 0.0)
         v_w, pageB = [], []
@@ -163,9 +163,9 @@ def tile_list_stereo_patch_pages_kernel(
         h = features(0, left, wl_sc, sbuf_at(TURNED + 2 * KB, [P, S], F32, "h1_0"), False)
         for i in range(HALVES):
             place(pageA[0], h[:, i * BANK : (i + 1) * BANK], gain1, idx2, i * BANK, BANK)
-        h = sbuf([P, BANK], F32, "h1_1a")
-        half_features(1, 0, left, wl_sc, h[:], False)
-        place(pageA[1], h[:], gain1, idx2, 0, BANK)
+        h = features(1, left, wl_sc, sbuf([P, S], F32, "h1_1"), False)
+        place(pageA[1], h[:], gain1, idx2)
+        h1_last = features(last, left, wl_sc, sbuf([P, S], F32, "h1_last"), False)
 
         wr_bf = sbuf([P, PASSES, H * PACK], BF16, "wr_bf")
         wr_w = sbuf([P, PASSES, H], U32, "wr_w")
@@ -179,12 +179,10 @@ def tile_list_stereo_patch_pages_kernel(
                 wr_bf[:, a, :].rearrange("p (c i t) -> p c t i", i=PACK, t=PACK),
                 raw[:].rearrange("p t (c i) -> p c t i", i=PACK),
             )
-        h = sbuf_at(THIRD, [P, BANK], F32, "h1_1b")
-        half_features(1, 1, left, wl_sc, h[:], False)
-        h1 = {r: features(r, left, wl_sc, sbuf([P, S], F32, f"h1_{r}"), False) for r in (2, last)}
+        h = features(2, left, wl_sc, sbuf_at(THIRD, [P, S], F32, "h1_2"), False)
         for a in range(PASSES):
             nc.vector.quantize_mx(wr_w[:, a, :].bitcast(E4M3), wr_sc[:, a * H : (a + 1) * H], wr_bf[:, a, :])
-        place(pageA[1], h[:], gain1, idx2, BANK, BANK)
+        place(pageA[2], h[:], gain1, idx2)
         gain2 = sbuf_at(TURNED + 2 * KB, [P, S], F32, "gain2")
         nc.sync.dma_start(gain2[:], wg2)
 
@@ -238,11 +236,11 @@ def tile_list_stereo_patch_pages_kernel(
         gap = [sbuf([P, 2, BLOCKS, P, 2], BF16, f"gap{c}") for c in range(CHUNKS)]
         for r in range(last):
             if r == 2:
-                place(pageA[0], h1[r][:], gain1, idx2)
+                place(pageA[0], h1_last[:], gain1, idx2)
             place(pageB[r % 2], h2[r][:], gain2, idx3)
             for c in range(CHUNKS):
                 turned = bank(4 + c, [P, BLOCKS, P], "turned")
-                turn(turned, pageA[r % 2], c, True, False)
+                turn(turned, pageA[r], c, True, False)
                 turn(turned, pageB[r % 2], c, False, True)
                 leave_bank(gap[c], turned, r, ACT.Abs)
             for later in ((1,), (2, 3), ())[r]:
@@ -251,10 +249,9 @@ def tile_list_stereo_patch_pages_kernel(
         for n, at in enumerate((SPARE, SPARE + HALF, HALF, SLOT + HALF, THIRD - ALIGN, THIRD + HALF - ALIGN)):
             res.append(sbuf_at(at, [P, T2], F32, f"res{n}"))
             nc.sync.dma_start(res[n][:], style[n * P : (n + 1) * P, :])
-        place(pageA[last % 2], h1[last][:], gain1, idx2)
         held = [bank(c, [P, BLOCKS, P], "held") for c in range(CHUNKS)]
         for c in range(CHUNKS):
-            turn(held[c], pageA[last % 2], c, True, False)
+            turn(held[c], pageA[0], c, True, False)
         place(pageB[last % 2], h2[last][:], gain2, idx3)
 
         def close_gap(c):

@@ -29,6 +29,10 @@ BLOCKS = BANK // P
 QUADS = 4
 SPAN = P // ROW_TILES
 ALIGN = 64
+PIECES = ((0, 0, 2), (0, 2, 2), (1, 0, 4), (2, 0, 4), (3, 0, 4))
+HELD_BANKS = (0, 4, 1, 2, 3)
+DIRECT_BANKS = (0, 4, 1, 2)
+SPARE_BANKS = (5, 6, 7)
 SC0 = P - PASSES * 16
 KB = 1024
 SLOT = 16 * KB
@@ -60,6 +64,13 @@ def tile_list_stereo_patch_pages_kernel(
 
         def bank(i, shape, name):
             return ps.tile(shape, F32, name=name, tag=f"bank{i}", bufs=1)
+
+        def cycle(banks):
+            return {"banks": banks, "turn": 0}
+
+        def take(ring):
+            ring["turn"] += 1
+            return ring["banks"][(ring["turn"] - 1) % len(ring["banks"])]
 
         def clear(engine, tile):
             engine.memset(tile.bitcast(I32), 0)
@@ -121,15 +132,15 @@ def tile_list_stereo_patch_pages_kernel(
                     tab[a][:].bitcast(U32).indirect(idx[:, i * n // 16 : (i + 1) * n // 16]),
                 )
             if a < 2:
-                pageB.append(slot(a, 0, [P, T2], F32, f"pageB{a}"))
+                pageB.append(slot(a, a, [P, T2], F32, f"pageB{a}"))
                 nc.vector.memset(pageB[a][:], 0.0)
 
         ident = sbuf([P, P], F32, "ident")
         make_identity(nc, ident[:])
 
-        def half_features(row, i, weights, scales, dst, negate):
+        def half_features(row, i, weights, scales, dst, negate, at=None):
             cols = slice(i * BANK, (i + 1) * BANK)
-            acc = bank(2 * (row % 2) + i, [P, BANK], "acc")
+            acc = bank(2 * (row % 2) + i if at is None else at, [P, BANK], "acc")
             for a in range(PASSES):
                 nc.tensor.matmul_mx(
                     acc[:],
@@ -171,7 +182,7 @@ def tile_list_stereo_patch_pages_kernel(
         wr_w = sbuf([P, PASSES, H], U32, "wr_w")
         wr_sc = sbuf([P, PASSES * H], U8, "wr_sc")
         for a in range(PASSES):
-            raw = sbuf_at((HALF, SLOT + HALF, THIRD)[a], [P, PACK, H], F32, f"wr_raw{a}")
+            raw = sbuf_at((HALF, SLOT, THIRD)[a], [P, PACK, H], F32, f"wr_raw{a}")
             nc.sync.dma_start(
                 raw[:], wr[a * P * PACK : (a + 1) * P * PACK, :].rearrange("(p t) c -> p t c", t=PACK)
             )
@@ -191,10 +202,12 @@ def tile_list_stereo_patch_pages_kernel(
 
         h2 = [
             features(r, right, wr_sc, sbuf_at(at, [P, S], F32, f"h2_{r}"), True)
-            for r, at in enumerate((SPARE, SPARE + HALF, THIRD + 4 * KB, TURNED + 10 * KB))
+            for r, at in enumerate((SPARE, SPARE + HALF, THIRD + 4 * KB))
         ]
+        h2_last = sbuf_at(TURNED + 10 * KB, [P, S], F32, "h2_last")
+        half_features(last, 0, right, wr_sc, h2_last[:, 0:BANK], True)
 
-        wd_w = sbuf([P, N], I32, "wd_w", "v_w0")
+        wd_w = sbuf([P, N], I32, "wd_w", "wr_bf")
         nc.sync.dma_start(wd_w[:], wd_words[0].rearrange("p c i -> p (c i)").bitcast(I32))
         wd_sc = sbuf([P, N], U8, "wd_sc", "w_sc")
         clear(nc.gpsimd, wd_sc[:])
@@ -204,24 +217,26 @@ def tile_list_stereo_patch_pages_kernel(
                 wd_scales[0, 4 * q : 4 * q + 4, :].bitcast(I32),
             )
 
-        def turn(turned, page, c, start, stop):
-            for b in range(BLOCKS):
+        def turn(turned, page, c, start, stop, first=0, count=BLOCKS):
+            for b in range(count):
+                m0 = c * BANK + (first + b) * P
                 nc.tensor.matmul(
-                    turned[:, b, :], page[:, c * BANK + b * P : c * BANK + (b + 1) * P], ident[:],
-                    start=(start and b == 0), stop=(stop and b == BLOCKS - 1), is_transpose=True,
+                    turned[:, b, :], page[:, m0 : m0 + P], ident[:],
+                    start=(start and b == 0), stop=(stop and b == count - 1), is_transpose=True,
                 )
 
-        def rows_of(tile, first, count):
-            return tile[:, :, :, SPAN * first : SPAN * (first + count), :]
+        def rows_of(tile, r, tiles, first=0, count=BLOCKS):
+            return tile[:, :, first : first + count, SPAN * r : SPAN * (r + tiles), :]
 
-        def leave_bank(dst, turned, r, func):
+        def leave_bank(dst, turned, r, func, first=0, count=BLOCKS):
             nc.scalar.activation(
-                rows_of(dst, r, 1), turned[:].rearrange("m b (p u e) -> m u b p e", u=2, e=2), func
+                rows_of(dst, r, 1, first, count),
+                turned[:].rearrange("m b (p u e) -> m u b p e", u=2, e=2), func,
             )
 
         floor = [sbuf([P, 2, BLOCKS, P, 2], BF16, f"floor{c}") for c in range(CHUNKS)]
         band_raw = []
-        for r, at in enumerate((THIRD + HALF, 2 * SLOT, HALF, SLOT + HALF)):
+        for r, at in enumerate((THIRD + HALF, 2 * SLOT, HALF, SLOT)):
             band_raw.append(sbuf_at(at, [P, T2], F32, f"band_raw{r}"))
             nc.sync.dma_start(band_raw[r][:], band[r * P : (r + 1) * P, :])
 
@@ -235,8 +250,6 @@ def tile_list_stereo_patch_pages_kernel(
 
         gap = [sbuf([P, 2, BLOCKS, P, 2], BF16, f"gap{c}") for c in range(CHUNKS)]
         for r in range(last):
-            if r == 2:
-                place(pageA[0], h1_last[:], gain1, idx2)
             place(pageB[r % 2], h2[r][:], gain2, idx3)
             for c in range(CHUNKS):
                 turned = bank(4 + c, [P, BLOCKS, P], "turned")
@@ -245,36 +258,48 @@ def tile_list_stereo_patch_pages_kernel(
                 leave_bank(gap[c], turned, r, ACT.Abs)
             for later in ((1,), (2, 3), ())[r]:
                 turn_band(later)
+        place(pageA[1], h1_last[:], gain1, idx2)
+        half_features(last, 1, right, wr_sc, h2_last[:, BANK:S], True, 7)
         res = []
-        for n, at in enumerate((SPARE, SPARE + HALF, HALF, SLOT + HALF, THIRD - ALIGN, THIRD + HALF - ALIGN)):
-            res.append(sbuf_at(at, [P, T2], F32, f"res{n}"))
-            nc.sync.dma_start(res[n][:], style[n * P : (n + 1) * P, :])
-        held = [bank(c, [P, BLOCKS, P], "held") for c in range(CHUNKS)]
-        for c in range(CHUNKS):
-            turn(held[c], pageA[0], c, True, False)
-        place(pageB[last % 2], h2[last][:], gain2, idx3)
+        for s, at in enumerate((SPARE, HALF, THIRD)):
+            res.append(sbuf_at(at, [P, 2, T2], F32, f"res{s}"))
+            nc.sync.dma_start(
+                res[s][:], style[2 * P * s : 2 * P * (s + 1), :].rearrange("(i p) m -> p i m", p=P)
+            )
+        held = []
+        for (c, first, count), at in zip(PIECES, HELD_BANKS):
+            held.append(bank(at, [P, count, P], "held"))
+            turn(held[-1], pageA[1], c, True, False, first, count)
+        for i in range(HALVES):
+            place(pageB[last % 2], h2_last[:, i * BANK : (i + 1) * BANK], gain2, idx3, i * BANK, BANK)
 
-        def close_gap(c):
-            turn(held[c], pageB[last % 2], c, False, True)
-            leave_bank(gap[c], held[c], last, ACT.Abs)
+        z_t = [sbuf_at(TURNED + 4 * KB * c, [P, 2, BLOCKS, P, 2], BF16, f"z_t{c}") for c in range(CHUNKS)]
+        spare_banks = cycle(SPARE_BANKS)
+        direct_banks = cycle(DIRECT_BANKS)
 
-        def floor_at_band(c):
-            z_t = sbuf_at(TURNED + 4 * KB * c, [P, 2, BLOCKS, P, 2], BF16, f"z_t{c}")
-            for first, count in ((0, last), (last, 1)):
-                nc.vector.tensor_tensor(
-                    rows_of(z_t, first, count), rows_of(gap[c], first, count),
-                    rows_of(floor[c], first, count), ALU.max,
-                )
-            return z_t
+        def floor_at_band(c, r, tiles, first=0, count=BLOCKS):
+            nc.vector.tensor_tensor(
+                rows_of(z_t[c], r, tiles, first, count), rows_of(gap[c], r, tiles, first, count),
+                rows_of(floor[c], r, tiles, first, count), ALU.max,
+            )
 
-        def weave(c, z_t):
-            words = z_t[:].rearrange("m u b p e -> m (u b p e)").bitcast(F32)
-            woven = sbuf([P, BANK, 2], F32, "woven", bufs=2)
-            for k in range(2):
-                back = bank(4 + 2 * (c % 2) + k, [P, 2, 2 * P], "back")
+        def close(i):
+            c, first, count = PIECES[i]
+            turn(held[i], pageB[last % 2], c, False, True, first, count)
+            leave_bank(gap[c], held[i], last, ACT.Abs, first, count)
+            if first == 0:
+                floor_at_band(c, 0, last)
+            floor_at_band(c, last, 1, first, count)
+
+        def weave(i):
+            c, first, count = PIECES[i]
+            words = z_t[c][:].rearrange("m u b p e -> m (u b p e)").bitcast(F32)
+            woven = sbuf([P, count * P, 2], F32, f"woven{i}")
+            for k in range(count // 2):
+                back = bank(take(spare_banks), [P, 2, 2 * P], "back")
                 for u in range(2):
                     for b in range(2):
-                        w0 = (u * BLOCKS + 2 * k + b) * P
+                        w0 = (u * BLOCKS + first + 2 * k + b) * P
                         nc.tensor.transpose(
                             back[:, u, b * P : (b + 1) * P], words[:, w0 : w0 + P], ident[:]
                         )
@@ -283,43 +308,60 @@ def tile_list_stereo_patch_pages_kernel(
                 )
             return woven
 
-        def quantise(c, woven):
-            z_w = sbuf([P, BANK], U32, f"z_w{c}")
-            z_sc = sbuf([P, BANK], U8, f"z_sc{c}")
+        def quantise(i, woven):
+            width = PIECES[i][2] * P
+            z_w = sbuf([P, width], U32, f"z_w{i}")
+            z_sc = sbuf([P, width], U8, f"z_sc{i}")
             nc.vector.quantize_mx(
                 z_w[:].bitcast(E4M3), z_sc[:], woven[:].rearrange("p m u -> p (m u)").bitcast(BF16)
             )
             return z_w, z_sc
 
-        def project(c, z_mx, tiles):
-            cols = slice(c * BANK, (c + 1) * BANK)
-            for n in tiles:
-                rows = slice(n * P, (n + 1) * P)
-                acc = bank((c * OUT_TILES + n) % 4, [P, BANK], "acc")
-                nc.tensor.matmul_mx(
-                    acc[:],
-                    lhsT=wd_w[:, rows].bitcast(E4M3),
-                    lhsT_scale=wd_sc[:, rows],
-                    rhs=z_mx[0][:].bitcast(E4M3),
-                    rhs_scale=z_mx[1][:],
-                    start=True,
-                    stop=True,
-                )
-                total = res[n][:, cols]
-                nc.vector.tensor_tensor(total, total, acc[:], ALU.add)
-                nc.sync.dma_start(out[rows, cols], total)
+        def columns(i):
+            c, first, count = PIECES[i]
+            return slice(c * BANK + first * P, c * BANK + (first + count) * P)
 
-        close_gap(0)
-        z_mx = quantise(0, weave(0, floor_at_band(0)))
-        close_gap(1)
-        woven = weave(1, floor_at_band(1))
-        for c in range(2, CHUNKS):
-            close_gap(c)
-        for c in range(CHUNKS):
-            project(c, z_mx, range(0, 2))
-            if c + 1 < CHUNKS:
-                z_next = quantise(c + 1, woven)
-            if c + 2 < CHUNKS:
-                woven = weave(c + 2, floor_at_band(c + 2))
-            project(c, z_mx, range(2, OUT_TILES))
+        def product(i, n, z_mx, at):
+            acc = bank(at, [P, PIECES[i][2] * P], "acc")
+            nc.tensor.matmul_mx(
+                acc[:],
+                lhsT=wd_w[:, n * P : (n + 1) * P].bitcast(E4M3),
+                lhsT_scale=wd_sc[:, n * P : (n + 1) * P],
+                rhs=z_mx[0][:].bitcast(E4M3),
+                rhs_scale=z_mx[1][:],
+                start=True,
+                stop=True,
+            )
+            return acc
+
+        def store(i, n):
+            cols = columns(i)
+            if i == len(PIECES) - 1 and n >= OUT_TILES - 2:
+                nc.sync.dma_start(out[n * P : (n + 1) * P, cols], res[n // 2][:, n % 2, cols])
+            elif n % 2 == 1:
+                rows = out[(n - 1) * P : (n + 1) * P, cols].rearrange("(i p) m -> p i m", p=P)
+                nc.sync.dma_start(rows, res[n // 2][:, :, cols])
+
+        def project(i, z_mx, tiles):
+            cols = columns(i)
+            for n in tiles:
+                acc = product(i, n, z_mx, take(direct_banks))
+                total = res[n // 2][:, n % 2, cols]
+                nc.vector.tensor_tensor(total, total, acc[:], ALU.add)
+                store(i, n)
+
+        count = len(PIECES)
+        close(0)
+        z_mx = quantise(0, weave(0))
+        close(1)
+        woven = weave(1)
+        for i in range(2, count):
+            close(i)
+        for i in range(count):
+            project(i, z_mx, range(0, 2))
+            if i + 1 < count:
+                z_next = quantise(i + 1, woven)
+            if i + 2 < count:
+                woven = weave(i + 2)
+            project(i, z_mx, range(2, OUT_TILES))
             z_mx = z_next

@@ -82,7 +82,7 @@ def tile_list_stereo_patch_pages_kernel(
         nc.sync.dma_start(idx[:], offs)
         wl_w = sbuf([P, PASSES, 2 * H], U8, "wl_w")
         nc.sync.dma_start(wl_w[:].bitcast(I32), wl_words.rearrange("a p c -> p a c").bitcast(I32))
-        tab_sc = sbuf_at(THIRD + SLOT - T // 2, [P, T], U8, "tab_sc")
+        tab_sc = sbuf_at(THIRD + SLOT, [P, T], U8, "tab_sc")
         nc.sync.dma_start(
             tab_sc[SC0 : SC0 + PASSES * 16, :].bitcast(I32),
             tab_scales.rearrange("a q t -> q a t").bitcast(I32),
@@ -94,7 +94,7 @@ def tile_list_stereo_patch_pages_kernel(
             tab.append(sbuf_at((0, SLOT, THIRD - ALIGN)[a], [P, T], I32, f"tab{a}"))
             nc.sync.dma_start(tab[a][:], tab_words[a].rearrange("p t i -> p (t i)").bitcast(I32))
 
-        for a in range(PASSES - 1):
+        for a in range(PASSES):
             load_table(a)
         nc.sync.dma_start(idx2[:], offs2)
         nc.sync.dma_start(idx3[:], offs3)
@@ -111,11 +111,10 @@ def tile_list_stereo_patch_pages_kernel(
         v_sc = sbuf([P, PASSES * S], U8, "v_sc")
         clear(nc.vector, v_sc[:])
         for q in range(QUADS):
-            nc.sync.dma_start(
+            nc.scalar.dma_start(
                 v_sc[32 * q : 32 * q + 4, :].bitcast(I32).rearrange("r (a s) -> r a s", a=PASSES),
                 picked_sc[SC0 + 4 * PASSES * q : SC0 + 4 * PASSES * (q + 1), :].bitcast(I32),
             )
-        load_table(PASSES - 1)
         gain1 = sbuf_at(THIRD + SLOT, [P, S], F32, "gain1")
         nc.sync.dma_start(gain1[:], wg1)
         pageA = [sbuf([P, T2], F32, f"pageA{i}") for i in range(3)]

@@ -30,16 +30,11 @@ QUADS = 4
 SPAN = P // ROW_TILES
 ALIGN = 64
 PIECES = ((0, 0, 2), (0, 2, 2), (1, 0, 4), (2, 0, 4), (3, 0, 4))
-HELD_BANKS = (0, 4, 1, 2, 3)
-DIRECT_BANKS = (0, 4, 1, 2)
-SPARE_BANKS = (5, 6, 7)
+HELD_BANKS = (0, 1, 2, 4, 5)
+DIRECT_BANKS = (0, 1, 2, 4, 5)
+SPARE_BANKS = (3, 6, 7)
 SC0 = P - PASSES * 16
 KB = 1024
-SLOT = 16 * KB
-HALF = SLOT // 2
-THIRD = 2 * SLOT + HALF
-SPARE = THIRD + SLOT + 4 * KB
-TURNED = SPARE + SLOT
 
 
 def tile_list_stereo_patch_pages_kernel(
@@ -59,9 +54,6 @@ def tile_list_stereo_patch_pages_kernel(
         def sbuf_at(offset, shape, dtype, name):
             return placed.tile(shape, dtype, name=name, offset=offset, align_bytes=ALIGN)
 
-        def slot(a, half, shape, dtype, name):
-            return sbuf_at(SLOT * a + half * SLOT // 2, shape, dtype, name)
-
         def bank(i, shape, name):
             return ps.tile(shape, F32, name=name, tag=f"bank{i}", bufs=1)
 
@@ -80,46 +72,50 @@ def tile_list_stereo_patch_pages_kernel(
         idx3 = lists.tile([P, S // 16], U16, name="idx3")
 
         nc.sync.dma_start(idx[:], offs)
-        wl_w = sbuf([P, PASSES, 2 * H], U8, "wl_w")
-        nc.sync.dma_start(wl_w[:].bitcast(I32), wl_words.rearrange("a p c -> p a c").bitcast(I32))
-        tab_sc = sbuf_at(THIRD + SLOT, [P, T], U8, "tab_sc")
+        nc.sync.dma_start(idx2[:], offs2)
+        nc.sync.dma_start(idx3[:], offs3)
+        tab_sc = sbuf_at(80 * KB, [P, T], U8, "tab_sc")
         nc.sync.dma_start(
             tab_sc[SC0 : SC0 + PASSES * 16, :].bitcast(I32),
             tab_scales.rearrange("a q t -> q a t").bitcast(I32),
         )
         clear(nc.vector, tab_sc[0:SC0, :])
-        tab = []
 
-        def load_table(a):
-            tab.append(sbuf_at((0, SLOT, THIRD - ALIGN)[a], [P, T], I32, f"tab{a}"))
-            nc.sync.dma_start(tab[a][:], tab_words[a].rearrange("p t i -> p (t i)").bitcast(I32))
+        def load_left(pair, tile):
+            nc.sync.dma_start(
+                tile[:].bitcast(I32),
+                wl_words[:, :, pair * H : (pair + 1) * H].rearrange("a p c -> p a c").bitcast(I32),
+            )
+            return tile
 
-        for a in range(PASSES):
-            load_table(a)
-        nc.sync.dma_start(idx2[:], offs2)
-        nc.sync.dma_start(idx3[:], offs3)
-        wl_sc = sbuf([P, PASSES * H], U8, "wl_sc", "w_sc")
-        clear(nc.gpsimd, wl_sc[:])
+        wl_w = [load_left(0, sbuf_at(100 * KB, [P, PASSES, H], U8, "wl_w0"))]
+        wl_rows = sbuf([P, PASSES * H], U8, "wl_rows")
         for q in range(QUADS):
-            nc.gpsimd.dma_start(
-                wl_sc[32 * q : 32 * q + 4, :].bitcast(I32).rearrange("r (a c) -> r a c", a=PASSES),
+            nc.sync.dma_start(
+                wl_rows[32 * q : 32 * q + 4, :].bitcast(I32).rearrange("r (a c) -> r a c", a=PASSES),
                 wl_scales[:, 4 * q : 4 * q + 4, :].rearrange("a r c -> r a c").bitcast(I32),
             )
+        tab = []
+        for a, at in enumerate((0, 16, 48)):
+            tab.append(sbuf_at(at * KB, [P, T], I32, f"tab{a}"))
+            nc.sync.dma_start(tab[a][:], tab_words[a].rearrange("p t i -> p (t i)").bitcast(I32))
+        gain1 = sbuf([P, S], F32, "gain1")
+        nc.sync.dma_start(gain1[:], wg1)
+        wl_w.append(load_left(1, sbuf([P, PASSES, H], U8, "wl_w1")))
 
         picked_sc = sbuf([P, S], U8, "picked_sc")
         nc.vector.tensor_copy(picked_sc[:], tab_sc[:].indirect(idx[:]))
-        v_sc = sbuf([P, PASSES * S], U8, "v_sc")
-        clear(nc.vector, v_sc[:])
+        v_sc = sbuf_at(80 * KB, [P, PASSES * S], U8, "v_sc")
         for q in range(QUADS):
             nc.scalar.dma_start(
                 v_sc[32 * q : 32 * q + 4, :].bitcast(I32).rearrange("r (a s) -> r a s", a=PASSES),
                 picked_sc[SC0 + 4 * PASSES * q : SC0 + 4 * PASSES * (q + 1), :].bitcast(I32),
             )
-        gain1 = sbuf_at(THIRD + SLOT, [P, S], F32, "gain1")
-        nc.sync.dma_start(gain1[:], wg1)
-        pageA = [sbuf([P, T2], F32, f"pageA{i}") for i in range(3)]
-        for page in pageA:
-            nc.vector.memset(page[:], 0.0)
+        wl_sc = sbuf([P, PASSES * H], U8, "wl_sc", "w_sc")
+        clear(nc.vector, wl_sc[:])
+        for q in range(QUADS):
+            rows = slice(32 * q, 32 * q + 4)
+            nc.vector.tensor_copy(wl_sc[rows, :].bitcast(I32), wl_rows[rows, :].bitcast(I32))
         v_w, pageB = [], []
         for a in range(PASSES):
             v_w.append(sbuf([P, S], U32, f"v_w{a}"))
@@ -131,34 +127,34 @@ def tile_list_stereo_patch_pages_kernel(
                     tab[a][:].bitcast(U32).indirect(idx[:, i * n // 16 : (i + 1) * n // 16]),
                 )
             if a < 2:
-                pageB.append(slot(a, a, [P, T2], F32, f"pageB{a}"))
+                pageB.append(sbuf_at(24 * a * KB, [P, T2], F32, f"pageB{a}"))
                 nc.vector.memset(pageB[a][:], 0.0)
+        pageA = [sbuf([P, T2], F32, f"pageA{i}") for i in range(3)]
+        for page in pageA:
+            nc.vector.memset(page[:], 0.0)
 
         ident = sbuf([P, P], F32, "ident")
         make_identity(nc, ident[:])
 
-        def half_features(row, i, weights, scales, dst, negate, at=None):
-            cols = slice(i * BANK, (i + 1) * BANK)
-            acc = bank(2 * (row % 2) + i if at is None else at, [P, BANK], "acc")
-            for a in range(PASSES):
-                nc.tensor.matmul_mx(
-                    acc[:],
-                    lhsT=weights(a, row),
-                    lhsT_scale=scales[:, a * H + row * P : a * H + (row + 1) * P],
-                    rhs=v_w[a][:, cols].bitcast(E4M3),
-                    rhs_scale=v_sc[:, a * S + i * BANK : a * S + (i + 1) * BANK],
-                    start=(a == 0),
-                    stop=(a == PASSES - 1),
-                )
-            if negate:
-                nc.scalar.activation(dst, acc[:], ACT.Copy, scale=-1.0)
-            else:
-                nc.scalar.copy(dst, acc[:])
-
-        def features(row, weights, scales, h, negate):
+        def features(row, weights, scales, h, banks, func):
             for i in range(HALVES):
-                half_features(row, i, weights, scales, h[:, i * BANK : (i + 1) * BANK], negate)
+                cols = slice(i * BANK, (i + 1) * BANK)
+                acc = bank(banks + i, [P, BANK], "acc")
+                for a in range(PASSES):
+                    nc.tensor.matmul_mx(
+                        acc[:],
+                        lhsT=weights(a, row),
+                        lhsT_scale=scales[:, a * H + row * P : a * H + (row + 1) * P],
+                        rhs=v_w[a][:, cols].bitcast(E4M3),
+                        rhs_scale=v_sc[:, a * S + i * BANK : a * S + (i + 1) * BANK],
+                        start=(a == 0),
+                        stop=(a == PASSES - 1),
+                    )
+                func(h[:, cols], acc[:])
             return h
+
+        def negated(dst, src):
+            nc.scalar.activation(dst, src, ACT.Copy, scale=-1.0)
 
         def place(page, h, gain, places, first=0, count=S):
             nc.vector.tensor_tensor(
@@ -167,21 +163,20 @@ def tile_list_stereo_patch_pages_kernel(
             )
 
         def left(a, r):
-            return wl_w[:, a, 2 * P * r : 2 * P * (r + 1)].bitcast(E2M1)
+            return wl_w[r // 2][:, a, 2 * P * (r % 2) : 2 * P * (r % 2 + 1)].bitcast(E2M1)
 
         last = ROW_TILES - 1
-        h = features(0, left, wl_sc, sbuf_at(TURNED + 2 * KB, [P, S], F32, "h1_0"), False)
+        h = features(0, left, wl_sc, sbuf_at(32 * KB, [P, S], F32, "h1_0"), 0, nc.scalar.copy)
         for i in range(HALVES):
             place(pageA[0], h[:, i * BANK : (i + 1) * BANK], gain1, idx2, i * BANK, BANK)
-        h = features(1, left, wl_sc, sbuf([P, S], F32, "h1_1"), False)
+        h = features(1, left, wl_sc, sbuf_at(36 * KB, [P, S], F32, "h1_1"), 2, nc.scalar.copy)
         place(pageA[1], h[:], gain1, idx2)
-        h1_last = features(last, left, wl_sc, sbuf([P, S], F32, "h1_last"), False)
 
-        wr_bf = sbuf([P, PASSES, H * PACK], BF16, "wr_bf")
+        wr_bf = sbuf_at(100 * KB, [P, PASSES, H * PACK], BF16, "wr_bf")
         wr_w = sbuf([P, PASSES, H], U32, "wr_w")
         wr_sc = sbuf([P, PASSES * H], U8, "wr_sc")
-        for a in range(PASSES):
-            raw = sbuf_at((HALF, SLOT, THIRD)[a], [P, PACK, H], F32, f"wr_raw{a}")
+        for a, at in enumerate((8, 16, 54)):
+            raw = sbuf_at(at * KB, [P, PACK, H], F32, f"wr_raw{a}")
             nc.sync.dma_start(
                 raw[:], wr[a * P * PACK : (a + 1) * P * PACK, :].rearrange("(p t) c -> p t c", t=PACK)
             )
@@ -189,32 +184,21 @@ def tile_list_stereo_patch_pages_kernel(
                 wr_bf[:, a, :].rearrange("p (c i t) -> p c t i", i=PACK, t=PACK),
                 raw[:].rearrange("p t (c i) -> p c t i", i=PACK),
             )
-        h = features(2, left, wl_sc, sbuf_at(THIRD, [P, S], F32, "h1_2"), False)
+        h1_last = features(last, left, wl_sc, sbuf([P, S], F32, "h1_last"), 0, nc.scalar.copy)
+        h = features(2, left, wl_sc, sbuf_at(54 * KB, [P, S], F32, "h1_2"), 2, nc.scalar.copy)
         for a in range(PASSES):
             nc.vector.quantize_mx(wr_w[:, a, :].bitcast(E4M3), wr_sc[:, a * H : (a + 1) * H], wr_bf[:, a, :])
         place(pageA[2], h[:], gain1, idx2)
-        gain2 = sbuf_at(TURNED + 2 * KB, [P, S], F32, "gain2")
+        gain2 = sbuf_at(50 * KB, [P, S], F32, "gain2")
         nc.sync.dma_start(gain2[:], wg2)
 
         def right(a, r):
             return wr_w[:, a, P * r : P * (r + 1)].bitcast(E4M3)
 
         h2 = [
-            features(r, right, wr_sc, sbuf_at(at, [P, S], F32, f"h2_{r}"), True)
-            for r, at in enumerate((SPARE, SPARE + HALF, THIRD + 4 * KB))
+            features(r, right, wr_sc, sbuf_at(at * KB, [P, S], F32, f"h2_{r}"), 2 * (r % 2), negated)
+            for r, at in enumerate((70, 74, 112, 58))
         ]
-        h2_last = sbuf_at(TURNED + 10 * KB, [P, S], F32, "h2_last")
-        half_features(last, 0, right, wr_sc, h2_last[:, 0:BANK], True)
-
-        wd_w = sbuf([P, N], I32, "wd_w", "wr_bf")
-        nc.sync.dma_start(wd_w[:], wd_words[0].rearrange("p c i -> p (c i)").bitcast(I32))
-        wd_sc = sbuf([P, N], U8, "wd_sc", "w_sc")
-        clear(nc.gpsimd, wd_sc[:])
-        for q in range(QUADS):
-            nc.sync.dma_start(
-                wd_sc[32 * q : 32 * q + 4, :].bitcast(I32),
-                wd_scales[0, 4 * q : 4 * q + 4, :].bitcast(I32),
-            )
 
         def turn(turned, page, c, start, stop, first=0, count=BLOCKS):
             for b in range(count):
@@ -233,46 +217,50 @@ def tile_list_stereo_patch_pages_kernel(
                 turned[:].rearrange("m b (p u e) -> m u b p e", u=2, e=2), func,
             )
 
-        floor = [sbuf([P, 2, BLOCKS, P, 2], BF16, f"floor{c}") for c in range(CHUNKS)]
-        band_raw = []
-        for r, at in enumerate((THIRD + HALF, 2 * SLOT, HALF, SLOT)):
-            band_raw.append(sbuf_at(at, [P, T2], F32, f"band_raw{r}"))
-            nc.sync.dma_start(band_raw[r][:], band[r * P : (r + 1) * P, :])
-
-        def turn_band(r):
+        floor = [sbuf_at((84 + 4 * c) * KB, [P, 2, BLOCKS, P, 2], BF16, f"floor{c}") for c in range(CHUNKS)]
+        for r, at in enumerate((42, 62, 8, 16)):
+            band_raw = sbuf_at(at * KB, [P, T2], F32, f"band_raw{r}")
+            nc.sync.dma_start(band_raw[:], band[r * P : (r + 1) * P, :])
             for c in range(CHUNKS):
                 turned = bank(4 + c, [P, BLOCKS, P], "band_turned")
-                turn(turned, band_raw[r], c, True, True)
+                turn(turned, band_raw, c, True, True)
                 leave_bank(floor[c], turned, r, ACT.Copy)
 
-        turn_band(0)
+        wd_w = sbuf_at(100 * KB, [P, N], I32, "wd_w")
+        nc.sync.dma_start(wd_w[:], wd_words[0].rearrange("p c i -> p (c i)").bitcast(I32))
+        wd_sc = sbuf([P, N], U8, "wd_sc", "w_sc")
+        for q in range(QUADS):
+            nc.sync.dma_start(
+                wd_sc[32 * q : 32 * q + 4, :].bitcast(I32),
+                wd_scales[0, 4 * q : 4 * q + 4, :].bitcast(I32),
+            )
+        res = []
+        for s, at in enumerate((32, 64, 8)):
+            res.append(sbuf_at(at * KB, [P, 2, T2], F32, f"res{s}"))
+            nc.sync.dma_start(
+                res[s][:], style[2 * P * s : 2 * P * (s + 1), :].rearrange("(i p) m -> p i m", p=P)
+            )
 
         gap = [sbuf([P, 2, BLOCKS, P, 2], BF16, f"gap{c}") for c in range(CHUNKS)]
         for r in range(last):
             place(pageB[r % 2], h2[r][:], gain2, idx3)
+            turned = [bank(4 + c, [P, BLOCKS, P], "turned") for c in range(CHUNKS)]
             for c in range(CHUNKS):
-                turned = bank(4 + c, [P, BLOCKS, P], "turned")
-                turn(turned, pageA[r], c, True, False)
-                turn(turned, pageB[r % 2], c, False, True)
-                leave_bank(gap[c], turned, r, ACT.Abs)
-            for later in ((1,), (2, 3), ())[r]:
-                turn_band(later)
-        place(pageA[1], h1_last[:], gain1, idx2)
-        half_features(last, 1, right, wr_sc, h2_last[:, BANK:S], True, 7)
-        res = []
-        for s, at in enumerate((SPARE, HALF, THIRD)):
-            res.append(sbuf_at(at, [P, 2, T2], F32, f"res{s}"))
-            nc.sync.dma_start(
-                res[s][:], style[2 * P * s : 2 * P * (s + 1), :].rearrange("(i p) m -> p i m", p=P)
-            )
+                turn(turned[c], pageA[r], c, True, False)
+            for c in range(CHUNKS):
+                turn(turned[c], pageB[r % 2], c, False, True)
+                leave_bank(gap[c], turned[c], r, ACT.Abs)
+            if r == 1:
+                place(pageA[0], h1_last[:], gain1, idx2)
         held = []
         for (c, first, count), at in zip(PIECES, HELD_BANKS):
             held.append(bank(at, [P, count, P], "held"))
-            turn(held[-1], pageA[1], c, True, False, first, count)
-        for i in range(HALVES):
-            place(pageB[last % 2], h2_last[:, i * BANK : (i + 1) * BANK], gain2, idx3, i * BANK, BANK)
+            turn(held[-1], pageA[0], c, True, False, first, count)
+        place(pageB[last % 2], h2[last][:], gain2, idx3)
 
-        z_t = [sbuf_at(TURNED + 4 * KB * c, [P, 2, BLOCKS, P, 2], BF16, f"z_t{c}") for c in range(CHUNKS)]
+        z_t = [
+            sbuf_at(at * KB, [P, 2, BLOCKS, P, 2], BF16, f"z_t{c}") for c, at in enumerate((50, 84, 88, 92))
+        ]
         spare_banks = cycle(SPARE_BANKS)
         direct_banks = cycle(DIRECT_BANKS)
 

@@ -33,8 +33,10 @@ PIECES = ((0, 0, 2), (0, 2, 2), (1, 0, 4), (2, 0, 4), (3, 0, 4))
 HELD_BANKS = (0, 1, 2, 4, 5)
 DIRECT_BANKS = (0, 1, 2, 4, 5)
 SPARE_BANKS = (3, 6, 7)
-SC0 = P - PASSES * 16
+SC0 = 48
+SC1 = SC0 + PASSES * 16
 KB = 1024
+LAST_PASS = 55 * KB + 256
 
 
 def tile_list_stereo_patch_pages_kernel(
@@ -71,15 +73,21 @@ def tile_list_stereo_patch_pages_kernel(
         idx2 = lists.tile([P, S // 16], U16, name="idx2")
         idx3 = lists.tile([P, S // 16], U16, name="idx3")
 
-        nc.sync.dma_start(idx[:], offs)
-        nc.sync.dma_start(idx2[:], offs2)
-        nc.sync.dma_start(idx3[:], offs3)
-        tab_sc = sbuf_at(80 * KB, [P, T], U8, "tab_sc")
+        tab_sc = sbuf_at(52 * KB - ALIGN, [P, T], U8, "tab_sc")
         nc.sync.dma_start(
-            tab_sc[SC0 : SC0 + PASSES * 16, :].bitcast(I32),
+            tab_sc[SC0:SC1, :].bitcast(I32),
             tab_scales.rearrange("a q t -> q a t").bitcast(I32),
         )
         clear(nc.vector, tab_sc[0:SC0, :])
+        clear(nc.vector, tab_sc[SC1:P, :])
+        nc.sync.dma_start(idx[:], offs)
+
+        def load_scale_rows(tile, scales, passes):
+            for r in range(4):
+                nc.sync.dma_start(
+                    tile[r:P:32, :].bitcast(I32).rearrange("q (a c) -> q a c", a=passes),
+                    scales[:, r:16:4, :].rearrange("a q c -> q a c").bitcast(I32),
+                )
 
         def load_left(pair, tile):
             nc.sync.dma_start(
@@ -88,29 +96,38 @@ def tile_list_stereo_patch_pages_kernel(
             )
             return tile
 
-        wl_w = [load_left(0, sbuf_at(100 * KB, [P, PASSES, H], U8, "wl_w0"))]
-        wl_rows = sbuf([P, PASSES * H], U8, "wl_rows")
-        for q in range(QUADS):
-            nc.sync.dma_start(
-                wl_rows[32 * q : 32 * q + 4, :].bitcast(I32).rearrange("r (a c) -> r a c", a=PASSES),
-                wl_scales[:, 4 * q : 4 * q + 4, :].rearrange("a r c -> r a c").bitcast(I32),
-            )
-        tab = []
-        for a, at in enumerate((0, 16, 48)):
-            tab.append(sbuf_at(at * KB, [P, T], I32, f"tab{a}"))
+        def load_table(a, at):
+            tab.append(sbuf_at(at, [P, T], I32, f"tab{a}"))
             nc.sync.dma_start(tab[a][:], tab_words[a].rearrange("p t i -> p (t i)").bitcast(I32))
-        gain1 = sbuf([P, S], F32, "gain1")
-        nc.sync.dma_start(gain1[:], wg1)
-        wl_w.append(load_left(1, sbuf([P, PASSES, H], U8, "wl_w1")))
+
+        def move_scales(i):
+            for q in (0, 2, 1, 3):
+                nc.sync.dma_start(
+                    v_sc[i][32 * q : 32 * q + 4, :].bitcast(I32).rearrange("r (a s) -> r a s", a=PASSES),
+                    picked_sc[
+                        SC0 + 4 * PASSES * q : SC0 + 4 * PASSES * (q + 1), i * BANK : (i + 1) * BANK
+                    ].bitcast(I32),
+                )
+
+        wl_rows = sbuf([P, PASSES * H], U8, "wl_rows")
+        load_scale_rows(wl_rows, wl_scales, PASSES)
+        wl_w = [load_left(0, sbuf_at(100 * KB, [P, PASSES, H], U8, "wl_w0"))]
+        tab = []
+        load_table(0, 0)
+        load_table(1, 16 * KB)
+        nc.sync.dma_start(idx2[:], offs2)
+        nc.sync.dma_start(idx3[:], offs3)
 
         picked_sc = sbuf([P, S], U8, "picked_sc")
         nc.vector.tensor_copy(picked_sc[:], tab_sc[:].indirect(idx[:]))
-        v_sc = sbuf_at(80 * KB, [P, PASSES * S], U8, "v_sc")
-        for q in range(QUADS):
-            nc.scalar.dma_start(
-                v_sc[32 * q : 32 * q + 4, :].bitcast(I32).rearrange("r (a s) -> r a s", a=PASSES),
-                picked_sc[SC0 + 4 * PASSES * q : SC0 + 4 * PASSES * (q + 1), :].bitcast(I32),
-            )
+        v_sc = [
+            sbuf_at(52 * KB + i * PASSES * BANK, [P, PASSES * BANK], U8, f"v_sc{i}") for i in range(HALVES)
+        ]
+        move_scales(0)
+        load_table(2, LAST_PASS)
+        gain1 = sbuf_at(48 * KB, [P, S], F32, "gain1")
+        nc.sync.dma_start(gain1[:], wg1)
+        move_scales(1)
         wl_sc = sbuf([P, PASSES * H], U8, "wl_sc", "w_sc")
         clear(nc.vector, wl_sc[:])
         for q in range(QUADS):
@@ -146,7 +163,7 @@ def tile_list_stereo_patch_pages_kernel(
                         lhsT=weights(a, row),
                         lhsT_scale=scales[:, a * H + row * P : a * H + (row + 1) * P],
                         rhs=v_w[a][:, cols].bitcast(E4M3),
-                        rhs_scale=v_sc[:, a * S + i * BANK : a * S + (i + 1) * BANK],
+                        rhs_scale=v_sc[i][:, a * BANK : (a + 1) * BANK],
                         start=(a == 0),
                         stop=(a == PASSES - 1),
                     )
@@ -175,8 +192,8 @@ def tile_list_stereo_patch_pages_kernel(
         wr_bf = sbuf_at(100 * KB, [P, PASSES, H * PACK], BF16, "wr_bf")
         wr_w = sbuf([P, PASSES, H], U32, "wr_w")
         wr_sc = sbuf([P, PASSES * H], U8, "wr_sc")
-        for a, at in enumerate((8, 16, 54)):
-            raw = sbuf_at(at * KB, [P, PACK, H], F32, f"wr_raw{a}")
+        for a, at in enumerate((8 * KB, 16 * KB, LAST_PASS + 4 * KB)):
+            raw = sbuf_at(at, [P, PACK, H], F32, f"wr_raw{a}")
             nc.sync.dma_start(
                 raw[:], wr[a * P * PACK : (a + 1) * P * PACK, :].rearrange("(p t) c -> p t c", t=PACK)
             )
@@ -184,20 +201,21 @@ def tile_list_stereo_patch_pages_kernel(
                 wr_bf[:, a, :].rearrange("p (c i t) -> p c t i", i=PACK, t=PACK),
                 raw[:].rearrange("p t (c i) -> p c t i", i=PACK),
             )
+        wl_w.append(load_left(1, sbuf_at(LAST_PASS + 12 * KB, [P, PASSES, H], U8, "wl_w1")))
         h1_last = features(last, left, wl_sc, sbuf([P, S], F32, "h1_last"), 0, nc.scalar.copy)
-        h = features(2, left, wl_sc, sbuf_at(54 * KB, [P, S], F32, "h1_2"), 2, nc.scalar.copy)
+        h = features(2, left, wl_sc, sbuf_at(LAST_PASS + 4 * KB, [P, S], F32, "h1_2"), 2, nc.scalar.copy)
         for a in range(PASSES):
             nc.vector.quantize_mx(wr_w[:, a, :].bitcast(E4M3), wr_sc[:, a * H : (a + 1) * H], wr_bf[:, a, :])
         place(pageA[2], h[:], gain1, idx2)
-        gain2 = sbuf_at(50 * KB, [P, S], F32, "gain2")
+        gain2 = sbuf_at(LAST_PASS, [P, S], F32, "gain2")
         nc.sync.dma_start(gain2[:], wg2)
 
         def right(a, r):
             return wr_w[:, a, P * r : P * (r + 1)].bitcast(E4M3)
 
         h2 = [
-            features(r, right, wr_sc, sbuf_at(at * KB, [P, S], F32, f"h2_{r}"), 2 * (r % 2), negated)
-            for r, at in enumerate((70, 74, 112, 58))
+            features(r, right, wr_sc, sbuf_at(at, [P, S], F32, f"h2_{r}"), 2 * (r % 2), negated)
+            for r, at in enumerate((112 * KB, 116 * KB, 120 * KB, LAST_PASS + 8 * KB))
         ]
 
         def turn(turned, page, c, start, stop, first=0, count=BLOCKS):
@@ -218,8 +236,8 @@ def tile_list_stereo_patch_pages_kernel(
             )
 
         floor = [sbuf_at((84 + 4 * c) * KB, [P, 2, BLOCKS, P, 2], BF16, f"floor{c}") for c in range(CHUNKS)]
-        for r, at in enumerate((42, 62, 8, 16)):
-            band_raw = sbuf_at(at * KB, [P, T2], F32, f"band_raw{r}")
+        for r, at in enumerate((LAST_PASS + 14 * KB, 32 * KB, 8 * KB, 16 * KB)):
+            band_raw = sbuf_at(at, [P, T2], F32, f"band_raw{r}")
             nc.sync.dma_start(band_raw[:], band[r * P : (r + 1) * P, :])
             for c in range(CHUNKS):
                 turned = bank(4 + c, [P, BLOCKS, P], "band_turned")
@@ -229,14 +247,10 @@ def tile_list_stereo_patch_pages_kernel(
         wd_w = sbuf_at(100 * KB, [P, N], I32, "wd_w")
         nc.sync.dma_start(wd_w[:], wd_words[0].rearrange("p c i -> p (c i)").bitcast(I32))
         wd_sc = sbuf([P, N], U8, "wd_sc", "w_sc")
-        for q in range(QUADS):
-            nc.sync.dma_start(
-                wd_sc[32 * q : 32 * q + 4, :].bitcast(I32),
-                wd_scales[0, 4 * q : 4 * q + 4, :].bitcast(I32),
-            )
+        load_scale_rows(wd_sc, wd_scales, 1)
         res = []
-        for s, at in enumerate((32, 64, 8)):
-            res.append(sbuf_at(at * KB, [P, 2, T2], F32, f"res{s}"))
+        for s, at in enumerate((LAST_PASS + 12 * KB, 32 * KB, 8 * KB)):
+            res.append(sbuf_at(at, [P, 2, T2], F32, f"res{s}"))
             nc.sync.dma_start(
                 res[s][:], style[2 * P * s : 2 * P * (s + 1), :].rearrange("(i p) m -> p i m", p=P)
             )
@@ -259,7 +273,8 @@ def tile_list_stereo_patch_pages_kernel(
         place(pageB[last % 2], h2[last][:], gain2, idx3)
 
         z_t = [
-            sbuf_at(at * KB, [P, 2, BLOCKS, P, 2], BF16, f"z_t{c}") for c, at in enumerate((50, 84, 88, 92))
+            sbuf_at(at, [P, 2, BLOCKS, P, 2], BF16, f"z_t{c}")
+            for c, at in enumerate((LAST_PASS, 84 * KB, 88 * KB, 92 * KB))
         ]
         spare_banks = cycle(SPARE_BANKS)
         direct_banks = cycle(DIRECT_BANKS)

@@ -30,9 +30,9 @@ QUADS = 4
 SPAN = P // ROW_TILES
 ALIGN = 64
 PIECES = ((0, 0, 2), (0, 2, 2), (1, 0, 4), (2, 0, 4), (3, 0, 4))
-HELD_BANKS = (0, 1, 2, 4, 5)
-DIRECT_BANKS = (0, 1, 2, 4, 5)
-SPARE_BANKS = (3, 6, 7)
+HELD_BANKS = (0, 1, 2, 3, 4)
+DIRECT_BANKS = (0, 1, 2, 3, 4)
+SPARE_BANKS = (5, 6, 7)
 SC0 = 48
 SC1 = SC0 + PASSES * 16
 KB = 1024
@@ -213,10 +213,9 @@ def tile_list_stereo_patch_pages_kernel(
         def right(a, r):
             return wr_w[:, a, P * r : P * (r + 1)].bitcast(E4M3)
 
-        h2 = [
-            features(r, right, wr_sc, sbuf_at(at, [P, S], F32, f"h2_{r}"), 2 * (r % 2), negated)
-            for r, at in enumerate((112 * KB, 116 * KB, 120 * KB, LAST_PASS + 8 * KB))
-        ]
+        def right_features(r, banks):
+            at = (112 * KB, 116 * KB, 120 * KB, LAST_PASS + 8 * KB)[r]
+            return features(r, right, wr_sc, sbuf_at(at, [P, S], F32, f"h2_{r}"), banks, negated)
 
         def turn(turned, page, c, start, stop, first=0, count=BLOCKS):
             for b in range(count):
@@ -236,13 +235,31 @@ def tile_list_stereo_patch_pages_kernel(
             )
 
         floor = [sbuf_at((84 + 4 * c) * KB, [P, 2, BLOCKS, P, 2], BF16, f"floor{c}") for c in range(CHUNKS)]
-        for r, at in enumerate((LAST_PASS + 14 * KB, 32 * KB, 8 * KB, 16 * KB)):
+
+        def turn_band(r, banks):
+            at = (LAST_PASS + 14 * KB, 32 * KB, 8 * KB, 16 * KB)[r]
             band_raw = sbuf_at(at, [P, T2], F32, f"band_raw{r}")
             nc.sync.dma_start(band_raw[:], band[r * P : (r + 1) * P, :])
             for c in range(CHUNKS):
-                turned = bank(4 + c, [P, BLOCKS, P], "band_turned")
+                turned = bank(banks + c, [P, BLOCKS, P], "band_turned")
                 turn(turned, band_raw, c, True, True)
                 leave_bank(floor[c], turned, r, ACT.Copy)
+
+        def open_difference(r):
+            turned = [bank(4 + c, [P, BLOCKS, P], "turned") for c in range(CHUNKS)]
+            for c in range(CHUNKS):
+                turn(turned[c], pageA[r], c, True, False)
+            return turned
+
+        turn_band(0, 4)
+        h2 = [right_features(0, 0)]
+        turn_band(1, 2)
+        h2.append(right_features(1, 6))
+        turned = open_difference(0)
+        turn_band(2, 0)
+        h2.append(right_features(2, 0))
+        h2.append(right_features(3, 2))
+        turn_band(3, 0)
 
         wd_w = sbuf_at(100 * KB, [P, N], I32, "wd_w")
         nc.sync.dma_start(wd_w[:], wd_words[0].rearrange("p c i -> p (c i)").bitcast(I32))
@@ -258,12 +275,11 @@ def tile_list_stereo_patch_pages_kernel(
         gap = [sbuf([P, 2, BLOCKS, P, 2], BF16, f"gap{c}") for c in range(CHUNKS)]
         for r in range(last):
             place(pageB[r % 2], h2[r][:], gain2, idx3)
-            turned = [bank(4 + c, [P, BLOCKS, P], "turned") for c in range(CHUNKS)]
-            for c in range(CHUNKS):
-                turn(turned[c], pageA[r], c, True, False)
             for c in range(CHUNKS):
                 turn(turned[c], pageB[r % 2], c, False, True)
                 leave_bank(gap[c], turned[c], r, ACT.Abs)
+            if r + 1 < last:
+                turned = open_difference(r + 1)
             if r == 1:
                 place(pageA[0], h1_last[:], gain1, idx2)
         held = []

@@ -73,15 +73,6 @@ def tile_list_stereo_patch_pages_kernel(
         idx2 = lists.tile([P, S // 16], U16, name="idx2")
         idx3 = lists.tile([P, S // 16], U16, name="idx3")
 
-        tab_sc = sbuf_at(52 * KB - ALIGN, [P, T], U8, "tab_sc")
-        nc.sync.dma_start(
-            tab_sc[SC0:SC1, :].bitcast(I32),
-            tab_scales.rearrange("a q t -> q a t").bitcast(I32),
-        )
-        clear(nc.vector, tab_sc[0:SC0, :])
-        clear(nc.vector, tab_sc[SC1:P, :])
-        nc.sync.dma_start(idx[:], offs)
-
         def load_scale_rows(tile, scales, passes):
             for r in range(4):
                 nc.sync.dma_start(
@@ -109,8 +100,16 @@ def tile_list_stereo_patch_pages_kernel(
                     ].bitcast(I32),
                 )
 
+        nc.sync.dma_start(idx[:], offs)
         wl_rows = sbuf([P, PASSES * H], U8, "wl_rows")
         load_scale_rows(wl_rows, wl_scales, PASSES)
+        tab_sc = sbuf_at(52 * KB - ALIGN, [P, T], U8, "tab_sc")
+        nc.sync.dma_start(
+            tab_sc[SC0:SC1, :].bitcast(I32),
+            tab_scales.rearrange("a q t -> q a t").bitcast(I32),
+        )
+        clear(nc.vector, tab_sc[0:SC0, :])
+        clear(nc.vector, tab_sc[SC1:P, :])
         wl_w = [load_left(0, sbuf_at(100 * KB, [P, PASSES, H], U8, "wl_w0"))]
         tab = []
         load_table(0, 0)
@@ -189,6 +188,7 @@ def tile_list_stereo_patch_pages_kernel(
         h = features(1, left, wl_sc, sbuf_at(36 * KB, [P, S], F32, "h1_1"), 2, nc.scalar.copy)
         place(pageA[1], h[:], gain1, idx2)
 
+        wl_w.append(load_left(1, sbuf_at(LAST_PASS + 12 * KB, [P, PASSES, H], U8, "wl_w1")))
         wr_bf = sbuf_at(100 * KB, [P, PASSES, H * PACK], BF16, "wr_bf")
         wr_w = sbuf([P, PASSES, H], U32, "wr_w")
         wr_sc = sbuf([P, PASSES * H], U8, "wr_sc")
@@ -201,9 +201,8 @@ def tile_list_stereo_patch_pages_kernel(
                 wr_bf[:, a, :].rearrange("p (c i t) -> p c t i", i=PACK, t=PACK),
                 raw[:].rearrange("p t (c i) -> p c t i", i=PACK),
             )
-        wl_w.append(load_left(1, sbuf_at(LAST_PASS + 12 * KB, [P, PASSES, H], U8, "wl_w1")))
-        h1_last = features(last, left, wl_sc, sbuf([P, S], F32, "h1_last"), 0, nc.scalar.copy)
         h = features(2, left, wl_sc, sbuf_at(LAST_PASS + 4 * KB, [P, S], F32, "h1_2"), 2, nc.scalar.copy)
+        h1_last = features(last, left, wl_sc, sbuf([P, S], F32, "h1_last"), 0, nc.scalar.copy)
         for a in range(PASSES):
             nc.vector.quantize_mx(wr_w[:, a, :].bitcast(E4M3), wr_sc[:, a * H : (a + 1) * H], wr_bf[:, a, :])
         place(pageA[2], h[:], gain1, idx2)

@@ -87,9 +87,9 @@ def tile_list_stereo_patch_pages_kernel(
             )
             return tile
 
-        def load_table(a, at):
-            tab.append(sbuf_at(at, [P, T], I32, f"tab{a}"))
-            nc.sync.dma_start(tab[a][:], tab_words[a].rearrange("p t i -> p (t i)").bitcast(I32))
+        def load_table(a, first=0, count=T):
+            words = tab_words[a].rearrange("p t i -> p (t i)").bitcast(I32)
+            nc.sync.dma_start(tab[a][:, first : first + count], words[:, first : first + count])
 
         def move_scales(i):
             for q in (0, 2, 1, 3):
@@ -100,7 +100,9 @@ def tile_list_stereo_patch_pages_kernel(
                     ].bitcast(I32),
                 )
 
+        tab = [sbuf_at(at, [P, T], I32, f"tab{a}") for a, at in enumerate((0, 16 * KB))]
         nc.sync.dma_start(idx[:], offs)
+        load_table(0, 0, T // 2)
         wl_rows = sbuf([P, PASSES * H], U8, "wl_rows")
         load_scale_rows(wl_rows, wl_scales, PASSES)
         tab_sc = sbuf_at(52 * KB - ALIGN, [P, T], U8, "tab_sc")
@@ -111,9 +113,8 @@ def tile_list_stereo_patch_pages_kernel(
         clear(nc.vector, tab_sc[0:SC0, :])
         clear(nc.vector, tab_sc[SC1:P, :])
         wl_w = [load_left(0, sbuf_at(100 * KB, [P, PASSES, H], U8, "wl_w0"))]
-        tab = []
-        load_table(0, 0)
-        load_table(1, 16 * KB)
+        load_table(0, T // 2, T // 2)
+        load_table(1)
         nc.sync.dma_start(idx2[:], offs2)
         nc.sync.dma_start(idx3[:], offs3)
 
@@ -123,7 +124,8 @@ def tile_list_stereo_patch_pages_kernel(
             sbuf_at(52 * KB + i * PASSES * BANK, [P, PASSES * BANK], U8, f"v_sc{i}") for i in range(HALVES)
         ]
         move_scales(0)
-        load_table(2, LAST_PASS)
+        tab.append(sbuf_at(LAST_PASS, [P, T], I32, "tab2"))
+        load_table(2)
         gain1 = sbuf_at(48 * KB, [P, S], F32, "gain1")
         nc.sync.dma_start(gain1[:], wg1)
         move_scales(1)
@@ -152,8 +154,8 @@ def tile_list_stereo_patch_pages_kernel(
         ident = sbuf([P, P], F32, "ident")
         make_identity(nc, ident[:])
 
-        def features(row, weights, scales, h, banks, func):
-            for i in range(HALVES):
+        def features(row, weights, scales, h, banks, func, halves=range(HALVES)):
+            for i in halves:
                 cols = slice(i * BANK, (i + 1) * BANK)
                 acc = bank(banks + i, [P, BANK], "acc")
                 for a in range(PASSES):
@@ -182,11 +184,12 @@ def tile_list_stereo_patch_pages_kernel(
             return wl_w[r // 2][:, a, 2 * P * (r % 2) : 2 * P * (r % 2 + 1)].bitcast(E2M1)
 
         last = ROW_TILES - 1
-        h = features(0, left, wl_sc, sbuf_at(32 * KB, [P, S], F32, "h1_0"), 0, nc.scalar.copy)
-        for i in range(HALVES):
-            place(pageA[0], h[:, i * BANK : (i + 1) * BANK], gain1, idx2, i * BANK, BANK)
+        h1_first = features(0, left, wl_sc, sbuf_at(32 * KB, [P, S], F32, "h1_0"), 0, nc.scalar.copy, (0,))
+        place(pageA[0], h1_first[:, 0:BANK], gain1, idx2, 0, BANK)
         h = features(1, left, wl_sc, sbuf_at(36 * KB, [P, S], F32, "h1_1"), 2, nc.scalar.copy)
         place(pageA[1], h[:], gain1, idx2)
+        features(0, left, wl_sc, h1_first, 0, nc.scalar.copy, (1,))
+        place(pageA[0], h1_first[:, BANK:S], gain1, idx2, BANK, BANK)
 
         wl_w.append(load_left(1, sbuf_at(LAST_PASS + 12 * KB, [P, PASSES, H], U8, "wl_w1")))
         wr_bf = sbuf_at(100 * KB, [P, PASSES, H * PACK], BF16, "wr_bf")
@@ -364,8 +367,14 @@ def tile_list_stereo_patch_pages_kernel(
             for n in tiles:
                 acc = product(i, n, z_mx, take(direct_banks))
                 total = res[n // 2][:, n % 2, cols]
-                nc.vector.tensor_tensor(total, total, acc[:], ALU.add)
-                store(i, n)
+                if i == len(PIECES) - 1 and n == OUT_TILES - 1:
+                    for k in range(2):
+                        half = slice(k * BANK // 2, (k + 1) * BANK // 2)
+                        nc.vector.tensor_tensor(total[:, half], total[:, half], acc[:, half], ALU.add)
+                        nc.sync.dma_start(out[n * P : (n + 1) * P, cols][:, half], total[:, half])
+                else:
+                    nc.vector.tensor_tensor(total, total, acc[:], ALU.add)
+                    store(i, n)
 
         count = len(PIECES)
         close(0)

@@ -157,7 +157,7 @@ def tile_list_stereo_patch_pages_kernel(
         def features(row, weights, scales, h, banks, func, halves=range(HALVES)):
             for i in halves:
                 cols = slice(i * BANK, (i + 1) * BANK)
-                acc = bank(banks + i, [P, BANK], "acc")
+                acc = bank(banks[i], [P, BANK], "acc")
                 for a in range(PASSES):
                     nc.tensor.matmul_mx(
                         acc[:],
@@ -184,12 +184,13 @@ def tile_list_stereo_patch_pages_kernel(
             return wl_w[r // 2][:, a, 2 * P * (r % 2) : 2 * P * (r % 2 + 1)].bitcast(E2M1)
 
         last = ROW_TILES - 1
-        h1_first = features(0, left, wl_sc, sbuf_at(32 * KB, [P, S], F32, "h1_0"), 0, nc.scalar.copy, (0,))
+        h1_first = features(0, left, wl_sc, sbuf_at(120 * KB, [P, S], F32, "h1_0"), (0, 0), nc.scalar.copy, (0,))
         place(pageA[0], h1_first[:, 0:BANK], gain1, idx2, 0, BANK)
-        h = features(1, left, wl_sc, sbuf_at(36 * KB, [P, S], F32, "h1_1"), 2, nc.scalar.copy)
-        place(pageA[1], h[:], gain1, idx2)
-        features(0, left, wl_sc, h1_first, 0, nc.scalar.copy, (1,))
-        place(pageA[0], h1_first[:, BANK:S], gain1, idx2, BANK, BANK)
+        h1_second = features(1, left, wl_sc, sbuf_at(124 * KB, [P, S], F32, "h1_1"), (1, 1), nc.scalar.copy, (0,))
+        place(pageA[1], h1_second[:, 0:BANK], gain1, idx2, 0, BANK)
+        for r, h in enumerate((h1_first, h1_second)):
+            features(r, left, wl_sc, h, (r, r), nc.scalar.copy, (1,))
+            place(pageA[r], h[:, BANK:S], gain1, idx2, BANK, BANK)
 
         wl_w.append(load_left(1, sbuf_at(LAST_PASS + 12 * KB, [P, PASSES, H], U8, "wl_w1")))
         wr_bf = sbuf_at(100 * KB, [P, PASSES, H * PACK], BF16, "wr_bf")
@@ -204,8 +205,8 @@ def tile_list_stereo_patch_pages_kernel(
                 wr_bf[:, a, :].rearrange("p (c i t) -> p c t i", i=PACK, t=PACK),
                 raw[:].rearrange("p t (c i) -> p c t i", i=PACK),
             )
-        h = features(2, left, wl_sc, sbuf_at(LAST_PASS + 4 * KB, [P, S], F32, "h1_2"), 2, nc.scalar.copy)
-        h1_last = features(last, left, wl_sc, sbuf([P, S], F32, "h1_last"), 0, nc.scalar.copy)
+        h = features(2, left, wl_sc, sbuf_at(LAST_PASS + 4 * KB, [P, S], F32, "h1_2"), (2, 3), nc.scalar.copy)
+        h1_last = features(last, left, wl_sc, sbuf_at(LAST_PASS + 8 * KB, [P, S], F32, "h1_last"), (0, 1), nc.scalar.copy)
         for a in range(PASSES):
             nc.vector.quantize_mx(wr_w[:, a, :].bitcast(E4M3), wr_sc[:, a * H : (a + 1) * H], wr_bf[:, a, :])
         place(pageA[2], h[:], gain1, idx2)
@@ -216,8 +217,8 @@ def tile_list_stereo_patch_pages_kernel(
             return wr_w[:, a, P * r : P * (r + 1)].bitcast(E4M3)
 
         def right_features(r, banks):
-            at = (112 * KB, 116 * KB, 120 * KB, LAST_PASS + 8 * KB)[r]
-            return features(r, right, wr_sc, sbuf_at(at, [P, S], F32, f"h2_{r}"), banks, negated)
+            at = (32 + 4 * r) * KB
+            return features(r, right, wr_sc, sbuf_at(at, [P, S], F32, f"h2_{r}"), (banks, banks + 1), negated)
 
         def turn(turned, page, c, start, stop, first=0, count=BLOCKS):
             for b in range(count):
@@ -239,7 +240,7 @@ def tile_list_stereo_patch_pages_kernel(
         floor = [sbuf_at((84 + 4 * c) * KB, [P, 2, BLOCKS, P, 2], BF16, f"floor{c}") for c in range(CHUNKS)]
 
         def turn_band(r, banks):
-            at = (LAST_PASS + 14 * KB, 32 * KB, 8 * KB, 16 * KB)[r]
+            at = (LAST_PASS + 14 * KB, 8 * KB, 16 * KB, 104 * KB)[r]
             band_raw = sbuf_at(at, [P, T2], F32, f"band_raw{r}")
             nc.sync.dma_start(band_raw[:], band[r * P : (r + 1) * P, :])
             for c in range(CHUNKS):
@@ -253,14 +254,14 @@ def tile_list_stereo_patch_pages_kernel(
                 turn(turned[c], pageA[r], c, True, False)
             return turned
 
+        h2 = [right_features(0, 2)]
         turn_band(0, 4)
-        h2 = [right_features(0, 0)]
-        turn_band(1, 2)
-        h2.append(right_features(1, 6))
+        h2.append(right_features(1, 0))
+        turn_band(1, 4)
+        h2.append(right_features(2, 2))
+        h2.append(right_features(3, 0))
         turned = open_difference(0)
         turn_band(2, 0)
-        h2.append(right_features(2, 0))
-        h2.append(right_features(3, 2))
         turn_band(3, 0)
 
         wd_w = sbuf_at(100 * KB, [P, N], I32, "wd_w")
@@ -268,7 +269,7 @@ def tile_list_stereo_patch_pages_kernel(
         wd_sc = sbuf([P, N], U8, "wd_sc", "w_sc")
         load_scale_rows(wd_sc, wd_scales, 1)
         res = []
-        for s, at in enumerate((LAST_PASS + 12 * KB, 32 * KB, 8 * KB)):
+        for s, at in enumerate((LAST_PASS + 12 * KB, 8 * KB, 104 * KB)):
             res.append(sbuf_at(at, [P, 2, T2], F32, f"res{s}"))
             nc.sync.dma_start(
                 res[s][:], style[2 * P * s : 2 * P * (s + 1), :].rearrange("(i p) m -> p i m", p=P)
@@ -341,10 +342,9 @@ def tile_list_stereo_patch_pages_kernel(
             c, first, count = PIECES[i]
             return slice(c * BANK + first * P, c * BANK + (first + count) * P)
 
-        def product(i, n, z_mx, at):
-            acc = bank(at, [P, PIECES[i][2] * P], "acc")
+        def product(acc, n, z_mx):
             nc.tensor.matmul_mx(
-                acc[:],
+                acc,
                 lhsT=wd_w[:, n * P : (n + 1) * P].bitcast(E4M3),
                 lhsT_scale=wd_sc[:, n * P : (n + 1) * P],
                 rhs=z_mx[0][:].bitcast(E4M3),
@@ -352,7 +352,6 @@ def tile_list_stereo_patch_pages_kernel(
                 start=True,
                 stop=True,
             )
-            return acc
 
         def store(i, n):
             cols = columns(i)
@@ -364,8 +363,19 @@ def tile_list_stereo_patch_pages_kernel(
 
         def project(i, z_mx, tiles):
             cols = columns(i)
+            width = PIECES[i][2] * P
+            if 2 * width <= BANK:
+                for n in tiles[::2]:
+                    acc = bank(take(direct_banks), [P, 2, width], "acc")
+                    for k in range(2):
+                        product(acc[:, k, :], n + k, z_mx)
+                    total = res[n // 2][:, :, cols]
+                    nc.vector.tensor_tensor(total, total, acc[:], ALU.add)
+                    store(i, n + 1)
+                return
             for n in tiles:
-                acc = product(i, n, z_mx, take(direct_banks))
+                acc = bank(take(direct_banks), [P, width], "acc")
+                product(acc[:], n, z_mx)
                 total = res[n // 2][:, n % 2, cols]
                 if i == len(PIECES) - 1 and n == OUT_TILES - 1:
                     for k in range(2):

@@ -37,6 +37,8 @@ SC0 = 48
 SC1 = SC0 + PASSES * 16
 KB = 1024
 LAST_PASS = 55 * KB + 256
+WINDOW = 128 * KB
+FIRST = 256
 
 
 def tile_list_stereo_patch_pages_kernel(
@@ -100,34 +102,34 @@ def tile_list_stereo_patch_pages_kernel(
                     ].bitcast(I32),
                 )
 
-        tab = [sbuf_at(at, [P, T], I32, f"tab{a}") for a, at in enumerate((0, 16 * KB))]
+        tab = [sbuf_at(at, [P, T], I32, f"tab{a}") for a, at in enumerate((0, 16 * KB, LAST_PASS))]
         nc.sync.dma_start(idx[:], offs)
         load_table(0, 0, T // 2)
         wl_rows = sbuf([P, PASSES * H], U8, "wl_rows")
         load_scale_rows(wl_rows, wl_scales, PASSES)
-        tab_sc = sbuf_at(52 * KB - ALIGN, [P, T], U8, "tab_sc")
+        tab_sc = sbuf_at(WINDOW, [P, T], U8, "tab_sc")
         nc.sync.dma_start(
             tab_sc[SC0:SC1, :].bitcast(I32),
             tab_scales.rearrange("a q t -> q a t").bitcast(I32),
         )
         clear(nc.vector, tab_sc[0:SC0, :])
         clear(nc.vector, tab_sc[SC1:P, :])
-        wl_w = [load_left(0, sbuf_at(100 * KB, [P, PASSES, H], U8, "wl_w0"))]
         load_table(0, T // 2, T // 2)
-        load_table(1)
         nc.sync.dma_start(idx2[:], offs2)
         nc.sync.dma_start(idx3[:], offs3)
+        load_table(1)
+        load_table(2)
+        wl_w = [load_left(0, sbuf_at(100 * KB, [P, PASSES, H], U8, "wl_w0"))]
 
         picked_sc = sbuf([P, S], U8, "picked_sc")
         nc.vector.tensor_copy(picked_sc[:], tab_sc[:].indirect(idx[:]))
         v_sc = [
-            sbuf_at(52 * KB + i * PASSES * BANK, [P, PASSES * BANK], U8, f"v_sc{i}") for i in range(HALVES)
+            sbuf_at(WINDOW + i * PASSES * BANK, [P, PASSES * BANK], U8, f"v_sc{i}") for i in range(HALVES)
         ]
         move_scales(0)
-        tab.append(sbuf_at(LAST_PASS, [P, T], I32, "tab2"))
-        load_table(2)
-        gain1 = sbuf_at(48 * KB, [P, S], F32, "gain1")
-        nc.sync.dma_start(gain1[:], wg1)
+        gain1 = sbuf_at(WINDOW + PASSES * S, [P, S], F32, "gain1")
+        nc.sync.dma_start(gain1[:, 0:FIRST], wg1[:, 0:FIRST])
+        nc.sync.dma_start(gain1[:, FIRST:S], wg1[:, FIRST:S])
         move_scales(1)
         wl_sc = sbuf([P, PASSES * H], U8, "wl_sc", "w_sc")
         clear(nc.vector, wl_sc[:])
@@ -137,12 +139,10 @@ def tile_list_stereo_patch_pages_kernel(
         v_w, pageB = [], []
         for a in range(PASSES):
             v_w.append(sbuf([P, S], U32, f"v_w{a}"))
-            pieces = HALVES if a == PASSES - 1 else 1
-            n = S // pieces
-            for i in range(pieces):
+            cuts = (0, FIRST, S) if a == PASSES - 1 else (0, S)
+            for lo, hi in zip(cuts, cuts[1:]):
                 nc.vector.tensor_copy(
-                    v_w[a][:, i * n : (i + 1) * n],
-                    tab[a][:].bitcast(U32).indirect(idx[:, i * n // 16 : (i + 1) * n // 16]),
+                    v_w[a][:, lo:hi], tab[a][:].bitcast(U32).indirect(idx[:, lo // 16 : hi // 16])
                 )
             if a < 2:
                 pageB.append(sbuf_at(24 * a * KB, [P, T2], F32, f"pageB{a}"))
@@ -154,17 +154,18 @@ def tile_list_stereo_patch_pages_kernel(
         ident = sbuf([P, P], F32, "ident")
         make_identity(nc, ident[:])
 
-        def features(row, weights, scales, h, banks, func, halves=range(HALVES)):
-            for i in halves:
-                cols = slice(i * BANK, (i + 1) * BANK)
-                acc = bank(banks[i], [P, BANK], "acc")
+        def features(row, weights, scales, h, banks, func, spans=((0, BANK), (BANK, BANK))):
+            for first, count in spans:
+                i, within = divmod(first, BANK)
+                cols = slice(first, first + count)
+                acc = bank(banks[i], [P, count], "acc")
                 for a in range(PASSES):
                     nc.tensor.matmul_mx(
                         acc[:],
                         lhsT=weights(a, row),
                         lhsT_scale=scales[:, a * H + row * P : a * H + (row + 1) * P],
                         rhs=v_w[a][:, cols].bitcast(E4M3),
-                        rhs_scale=v_sc[i][:, a * BANK : (a + 1) * BANK],
+                        rhs_scale=v_sc[i][:, a * BANK + within : a * BANK + within + count],
                         start=(a == 0),
                         stop=(a == PASSES - 1),
                     )
@@ -184,13 +185,11 @@ def tile_list_stereo_patch_pages_kernel(
             return wl_w[r // 2][:, a, 2 * P * (r % 2) : 2 * P * (r % 2 + 1)].bitcast(E2M1)
 
         last = ROW_TILES - 1
-        h1_first = features(0, left, wl_sc, sbuf_at(120 * KB, [P, S], F32, "h1_0"), (0, 0), nc.scalar.copy, (0,))
-        place(pageA[0], h1_first[:, 0:BANK], gain1, idx2, 0, BANK)
-        h1_second = features(1, left, wl_sc, sbuf_at(124 * KB, [P, S], F32, "h1_1"), (1, 1), nc.scalar.copy, (0,))
-        place(pageA[1], h1_second[:, 0:BANK], gain1, idx2, 0, BANK)
-        for r, h in enumerate((h1_first, h1_second)):
-            features(r, left, wl_sc, h, (r, r), nc.scalar.copy, (1,))
-            place(pageA[r], h[:, BANK:S], gain1, idx2, BANK, BANK)
+        h1_first = [sbuf_at((120 + 4 * r) * KB, [P, S], F32, f"h1_{r}") for r in range(2)]
+        for first, count in ((0, FIRST), (FIRST, BANK - FIRST), (BANK, BANK)):
+            for r, h in enumerate(h1_first):
+                features(r, left, wl_sc, h, (r, r), nc.scalar.copy, ((first, count),))
+                place(pageA[r], h[:, first : first + count], gain1, idx2, first, count)
 
         wl_w.append(load_left(1, sbuf_at(LAST_PASS + 12 * KB, [P, PASSES, H], U8, "wl_w1")))
         wr_bf = sbuf_at(100 * KB, [P, PASSES, H * PACK], BF16, "wr_bf")

@@ -236,15 +236,17 @@ def tile_list_stereo_patch_pages_kernel(
                 turned[:].rearrange("m b (p u e) -> m u b p e", u=2, e=2), func,
             )
 
-        floor = [sbuf_at((84 + 4 * c) * KB, [P, 2, BLOCKS, P, 2], BF16, f"floor{c}") for c in range(CHUNKS)]
+        floor = [sbuf_at(84 * KB, [P, BANK, PACK], BF16, "floor0")] + [
+            sbuf_at((84 + 4 * c) * KB, [P, 2, BLOCKS, P, 2], BF16, f"floor{c}") for c in range(1, CHUNKS)
+        ]
 
         def turn_band(r, banks):
             at = (LAST_PASS + 14 * KB, 8 * KB, 16 * KB, 104 * KB)[r]
-            band_raw = sbuf_at(at, [P, T2], F32, f"band_raw{r}")
-            nc.sync.dma_start(band_raw[:], band[r * P : (r + 1) * P, :])
-            for c in range(CHUNKS):
+            band_raw = sbuf_at(at, [P, T2 - BANK], F32, f"band_raw{r}")
+            nc.sync.dma_start(band_raw[:], band[r * P : (r + 1) * P, BANK:T2])
+            for c in range(1, CHUNKS):
                 turned = bank(banks + c, [P, BLOCKS, P], "band_turned")
-                turn(turned, band_raw, c, True, True)
+                turn(turned, band_raw, c - 1, True, True)
                 leave_bank(floor[c], turned, r, ACT.Copy)
 
         def open_difference(r):
@@ -262,6 +264,12 @@ def tile_list_stereo_patch_pages_kernel(
         turned = open_difference(0)
         turn_band(2, 0)
         turn_band(3, 0)
+        band_first = sbuf_at(110 * KB, [P, PACK, BANK], F32, "band_first")
+        nc.sync.dma_start(band_first[:], band[:, 0:BANK].rearrange("(p t) m -> p t m", t=PACK))
+        nc.scalar.copy(
+            floor[0][:].rearrange("p (c i) t -> p c t i", i=PACK),
+            band_first[:].rearrange("p t (c i) -> p c t i", i=PACK),
+        )
 
         wd_w = sbuf_at(100 * KB, [P, N], I32, "wd_w")
         nc.sync.dma_start(wd_w[:], wd_words[0].rearrange("p c i -> p (c i)").bitcast(I32))
@@ -290,9 +298,9 @@ def tile_list_stereo_patch_pages_kernel(
             turn(held[-1], pageA[0], c, True, False, first, count)
         place(pageB[last % 2], h2[last][:], gain2, idx3)
 
-        z_t = [
-            sbuf_at(at, [P, 2, BLOCKS, P, 2], BF16, f"z_t{c}")
-            for c, at in enumerate((LAST_PASS, 84 * KB, 88 * KB, 92 * KB))
+        z_t = [gap[0]] + [
+            sbuf_at(at, [P, 2, BLOCKS, P, 2], BF16, f"z_t{c + 1}")
+            for c, at in enumerate((LAST_PASS, 44 * KB, 136 * KB))
         ]
         spare_banks = cycle(SPARE_BANKS)
         direct_banks = cycle(DIRECT_BANKS)
@@ -307,14 +315,17 @@ def tile_list_stereo_patch_pages_kernel(
             c, first, count = PIECES[i]
             turn(held[i], pageB[last % 2], c, False, True, first, count)
             leave_bank(gap[c], held[i], last, ACT.Abs, first, count)
-            if first == 0:
+            if c > 0:
                 floor_at_band(c, 0, last)
-            floor_at_band(c, last, 1, first, count)
+                floor_at_band(c, last, 1, first, count)
 
         def weave(i):
             c, first, count = PIECES[i]
             words = z_t[c][:].rearrange("m u b p e -> m (u b p e)").bitcast(F32)
-            woven = sbuf([P, count * P, 2], F32, f"woven{i}")
+            if i == 0:
+                woven = sbuf_at(136 * KB, [P, count * P, 2], F32, "woven0")
+            else:
+                woven = sbuf([P, count * P, 2], F32, f"woven{i}")
             for k in range(count // 2):
                 back = bank(take(spare_banks), [P, 2, 2 * P], "back")
                 for u in range(2):
@@ -323,8 +334,16 @@ def tile_list_stereo_patch_pages_kernel(
                         nc.tensor.transpose(
                             back[:, u, b * P : (b + 1) * P], words[:, w0 : w0 + P], ident[:]
                         )
-                nc.scalar.copy(
-                    woven[:, 2 * P * k : 2 * P * (k + 1), :], back[:].rearrange("p u m -> p m u")
+                dst = woven[:, 2 * P * k : 2 * P * (k + 1), :]
+                if c > 0:
+                    nc.scalar.copy(dst, back[:].rearrange("p u m -> p m u"))
+                    continue
+                m0 = (first + 2 * k) * P
+                nc.vector.tensor_tensor(
+                    dst.rearrange("p m u -> p (m u)").bitcast(BF16).rearrange("p (m u e) -> p m u e", u=2, e=2),
+                    back[:].rearrange("p u m -> p (u m)").bitcast(BF16).rearrange("p (u m e) -> p m u e", u=2, e=2),
+                    floor[0][:, m0 : m0 + 2 * P, :].rearrange("p m (u e) -> p m u e", u=2),
+                    ALU.max,
                 )
             return woven
 
@@ -385,18 +404,48 @@ def tile_list_stereo_patch_pages_kernel(
                     nc.vector.tensor_tensor(total, total, acc[:], ALU.add)
                     store(i, n)
 
-        count = len(PIECES)
+        def stage(i, z_mx, n):
+            width = PIECES[i][2] * P
+            acc = bank(take(direct_banks), [P, BANK // width, width], "acc")
+            for k in range(BANK // width):
+                product(acc[:, k, :], n + k, z_mx)
+            staged = sbuf([P, BANK // width, width], F32, f"staged{i}", "staged", bufs=2)
+            nc.scalar.copy(staged[:], acc[:])
+            return staged
+
+        def add_aside(i, z_mx, n):
+            total = res[n // 2][:, n % 2, columns(i)]
+            nc.gpsimd.tensor_tensor(total, total, stage(i, z_mx, n)[:, 0, :], ALU.add)
+
+        z_mx = {}
         close(0)
-        z_mx = quantise(0, weave(0))
+        z_mx[0] = quantise(0, weave(0))
         close(1)
         woven = weave(1)
-        for i in range(2, count):
+        for i in range(2, len(PIECES)):
             close(i)
-        for i in range(count):
-            project(i, z_mx, range(0, 2))
-            if i + 1 < count:
-                z_next = quantise(i + 1, woven)
-            if i + 2 < count:
-                woven = weave(i + 2)
-            project(i, z_mx, range(2, OUT_TILES))
-            z_mx = z_next
+        project(0, z_mx[0], range(0, 2))
+        staged = stage(0, z_mx[0], 4)
+        z_mx[1] = quantise(1, woven)
+        woven = weave(2)
+        total = sbuf([P, 2, BANK // 2], F32, "total", "woven1")
+        nc.gpsimd.tensor_tensor(total[:], staged[:], res[2][:, :, columns(0)], ALU.add)
+        project(0, z_mx[0], range(2, 4))
+        nc.sync.dma_start(out[4 * P : 6 * P, columns(0)].rearrange("(i p) m -> p i m", p=P), total[:])
+        project(1, z_mx[1], range(0, 4))
+        z_mx[2] = quantise(2, woven)
+        woven = weave(3)
+        project(1, z_mx[1], range(4, 6))
+        for i in (2, 3):
+            add_aside(i, z_mx[i], 4)
+            project(i, z_mx[i], range(0, 3))
+            z_mx[i + 1] = quantise(i + 1, woven)
+            if i == 2:
+                woven = weave(4)
+            project(i, z_mx[i], (3, 5))
+        add_aside(4, z_mx[4], 2)
+        project(4, z_mx[4], (0, 1))
+        add_aside(4, z_mx[4], 4)
+        project(4, z_mx[4], (3,))
+        store(4, 4)
+        project(4, z_mx[4], (5,))

from contextlib import ExitStack

import concourse.mybir as mybir
from concourse.masks import make_identity

K, H, N, T, S, T2 = 1536, 512, 768, 4096, 1024, 2048
FLOPS = 2 * (2 * K * H * S + H * N * T2)

F32 = mybir.dt.float32
BF16 = mybir.dt.bfloat16
I32 = mybir.dt.int32
U32 = mybir.dt.uint32
U16 = mybir.dt.uint16
U8 = mybir.dt.uint8
E4M3 = mybir.dt.float8_e4m3fn_x4
E2M1 = mybir.dt.float4_e2m1fn_x4
ALU = mybir.AluOpType
ACT = mybir.ActivationFunctionType

P = 128
PACK = 4
PASSES = K // (P * PACK)
BANK = 512
HALVES = S // BANK
ROW_TILES = H // P
OUT_TILES = N // P
CHUNKS = T2 // BANK
BLOCKS = BANK // P
QUADS = 4
SPAN = P // ROW_TILES
ALIGN = 64
PIECES = ((0, 0, 2), (0, 2, 2), (1, 0, 4), (2, 0, 4), (3, 0, 4))
HELD_BANKS = (0, 1, 2, 3, 4)
DIRECT_BANKS = (0, 1, 2, 3, 4)
SPARE_BANKS = (5, 6, 7)
SC0 = 48
SC1 = SC0 + PASSES * 16
KB = 1024
LAST_PASS = 55 * KB + 256
WINDOW = 128 * KB
FIRST = 256


def tile_list_stereo_patch_pages_kernel(
    tc, tab_words, tab_scales, wl_words, wl_scales, wr, wd_words, wd_scales,
    offs, offs2, offs3, wg1, wg2, band, style, out,
):
    nc = tc.nc
    with ExitStack() as ctx:
        lists = ctx.enter_context(tc.tile_pool(name="lists", bufs=1))
        sb = ctx.enter_context(tc.tile_pool(name="sb", bufs=1))
        placed = ctx.enter_context(tc.tile_pool(name="placed", bufs=1))
        ps = ctx.enter_context(tc.psum_pool(name="ps", bufs=1))

        def sbuf(shape, dtype, name, tag=None, bufs=1):
            return sb.tile(shape, dtype, name=name, tag=tag or name, bufs=bufs, align_bytes=ALIGN)

        def sbuf_at(offset, shape, dtype, name):
            return placed.tile(shape, dtype, name=name, offset=offset, align_bytes=ALIGN)

        def bank(i, shape, name):
            return ps.tile(shape, F32, name=name, tag=f"bank{i}", bufs=1)

        def cycle(banks):
            return {"banks": banks, "turn": 0}

        def take(ring):
            ring["turn"] += 1
            return ring["banks"][(ring["turn"] - 1) % len(ring["banks"])]

        def clear(engine, tile):
            engine.memset(tile.bitcast(I32), 0)

        idx = lists.tile([P, S // 16], U16, name="idx")
        idx2 = lists.tile([P, S // 16], U16, name="idx2")
        idx3 = lists.tile([P, S // 16], U16, name="idx3")

        def load_scale_rows(tile, scales, passes):
            for r in range(4):
                nc.sync.dma_start(
                    tile[r:P:32, :].bitcast(I32).rearrange("q (a c) -> q a c", a=passes),
                    scales[:, r:16:4, :].rearrange("a q c -> q a c").bitcast(I32),
                )

        def load_left(pair, tile):
            nc.sync.dma_start(
                tile[:].bitcast(I32),
                wl_words[:, :, pair * H : (pair + 1) * H].rearrange("a p c -> p a c").bitcast(I32),
            )
            return tile

        def load_table(a, first=0, count=T):
            words = tab_words[a].rearrange("p t i -> p (t i)").bitcast(I32)
            nc.sync.dma_start(tab[a][:, first : first + count], words[:, first : first + count])

        def move_scales(i):
            for q in (0, 2, 1, 3):
                nc.sync.dma_start(
                    v_sc[i][32 * q : 32 * q + 4, :].bitcast(I32).rearrange("r (a s) -> r a s", a=PASSES),
                    picked_sc[
                        SC0 + 4 * PASSES * q : SC0 + 4 * PASSES * (q + 1), i * BANK : (i + 1) * BANK
                    ].bitcast(I32),
                )

        tab = [sbuf_at(at, [P, T], I32, f"tab{a}") for a, at in enumerate((0, 16 * KB, LAST_PASS))]
        nc.sync.dma_start(idx[:], offs)
        load_table(0, 0, T // 2)
        wl_rows = sbuf([P, PASSES * H], U8, "wl_rows")
        load_scale_rows(wl_rows, wl_scales, PASSES)
        tab_sc = sbuf_at(WINDOW, [P, T], U8, "tab_sc")
        nc.sync.dma_start(
            tab_sc[SC0:SC1, :].bitcast(I32),
            tab_scales.rearrange("a q t -> q a t").bitcast(I32),
        )
        clear(nc.vector, tab_sc[0:SC0, :])
        clear(nc.vector, tab_sc[SC1:P, :])
        load_table(0, T // 2, T // 2)
        nc.sync.dma_start(idx2[:], offs2)
        nc.sync.dma_start(idx3[:], offs3)
        load_table(1)
        load_table(2)
        wl_w = [load_left(0, sbuf_at(100 * KB, [P, PASSES, H], U8, "wl_w0"))]

        picked_sc = sbuf([P, S], U8, "picked_sc")
        nc.vector.tensor_copy(picked_sc[:], tab_sc[:].indirect(idx[:]))
        v_sc = [
            sbuf_at(WINDOW + i * PASSES * BANK, [P, PASSES * BANK], U8, f"v_sc{i}") for i in range(HALVES)
        ]
        move_scales(0)
        gain1 = sbuf_at(WINDOW + PASSES * S, [P, S], F32, "gain1")
        nc.sync.dma_start(gain1[:, 0:FIRST], wg1[:, 0:FIRST])
        nc.sync.dma_start(gain1[:, FIRST:S], wg1[:, FIRST:S])
        move_scales(1)
        wl_sc = sbuf([P, PASSES * H], U8, "wl_sc", "w_sc")
        clear(nc.vector, wl_sc[:])
        for q in range(QUADS):
            rows = slice(32 * q, 32 * q + 4)
            nc.vector.tensor_copy(wl_sc[rows, :].bitcast(I32), wl_rows[rows, :].bitcast(I32))
        v_w, pageB = [], []
        for a in range(PASSES):
            v_w.append(sbuf([P, S], U32, f"v_w{a}"))
            cuts = (0, FIRST, S) if a == PASSES - 1 else (0, S)
            for lo, hi in zip(cuts, cuts[1:]):
                nc.vector.tensor_copy(
                    v_w[a][:, lo:hi], tab[a][:].bitcast(U32).indirect(idx[:, lo // 16 : hi // 16])
                )
            if a < 2:
                pageB.append(sbuf_at(24 * a * KB, [P, T2], F32, f"pageB{a}"))
                nc.vector.memset(pageB[a][:], 0.0)
        pageA = [sbuf([P, T2], F32, f"pageA{i}") for i in range(3)]
        for page in pageA:
            nc.vector.memset(page[:], 0.0)

        ident = sbuf([P, P], F32, "ident")
        make_identity(nc, ident[:])

        def features(row, weights, scales, h, banks, func, spans=((0, BANK), (BANK, BANK))):
            for first, count in spans:
                i, within = divmod(first, BANK)
                cols = slice(first, first + count)
                acc = bank(banks[i], [P, count], "acc")
                for a in range(PASSES):
                    nc.tensor.matmul_mx(
                        acc[:],
                        lhsT=weights(a, row),
                        lhsT_scale=scales[:, a * H + row * P : a * H + (row + 1) * P],
                        rhs=v_w[a][:, cols].bitcast(E4M3),
                        rhs_scale=v_sc[i][:, a * BANK + within : a * BANK + within + count],
                        start=(a == 0),
                        stop=(a == PASSES - 1),
                    )
                func(h[:, cols], acc[:])
            return h

        def negated(dst, src):
            nc.scalar.activation(dst, src, ACT.Copy, scale=-1.0)

        def place(page, h, gain, places, first=0, count=S):
            nc.vector.tensor_tensor(
                page[:].indirect(places[:, first // 16 : (first + count) // 16]),
                h, gain[:, first : first + count], ALU.mult,
            )

        def left(a, r):
            return wl_w[r // 2][:, a, 2 * P * (r % 2) : 2 * P * (r % 2 + 1)].bitcast(E2M1)

        last = ROW_TILES - 1
        h1_first = [sbuf_at((120 + 4 * r) * KB, [P, S], F32, f"h1_{r}") for r in range(2)]
        for first, count in ((0, FIRST), (FIRST, BANK - FIRST), (BANK, BANK)):
            for r, h in enumerate(h1_first):
                features(r, left, wl_sc, h, (r, r), nc.scalar.copy, ((first, count),))
                place(pageA[r], h[:, first : first + count], gain1, idx2, first, count)

        wl_w.append(load_left(1, sbuf_at(LAST_PASS + 12 * KB, [P, PASSES, H], U8, "wl_w1")))
        wr_bf = sbuf_at(100 * KB, [P, PASSES, H * PACK], BF16, "wr_bf")
        wr_w = sbuf([P, PASSES, H], U32, "wr_w")
        wr_sc = sbuf([P, PASSES * H], U8, "wr_sc")
        for a, at in enumerate((8 * KB, 16 * KB, LAST_PASS + 4 * KB)):
            raw = sbuf_at(at, [P, PACK, H], F32, f"wr_raw{a}")
            nc.sync.dma_start(
                raw[:], wr[a * P * PACK : (a + 1) * P * PACK, :].rearrange("(p t) c -> p t c", t=PACK)
            )
            nc.scalar.copy(
                wr_bf[:, a, :].rearrange("p (c i t) -> p c t i", i=PACK, t=PACK),
                raw[:].rearrange("p t (c i) -> p c t i", i=PACK),
            )
        h = features(2, left, wl_sc, sbuf_at(LAST_PASS + 4 * KB, [P, S], F32, "h1_2"), (2, 3), nc.scalar.copy)
        h1_last = features(last, left, wl_sc, sbuf_at(LAST_PASS + 8 * KB, [P, S], F32, "h1_last"), (0, 1), nc.scalar.copy)
        for a in range(PASSES):
            nc.vector.quantize_mx(wr_w[:, a, :].bitcast(E4M3), wr_sc[:, a * H : (a + 1) * H], wr_bf[:, a, :])
        place(pageA[2], h[:], gain1, idx2)
        gain2 = sbuf_at(LAST_PASS, [P, S], F32, "gain2")
        nc.sync.dma_start(gain2[:], wg2)

        def right(a, r):
            return wr_w[:, a, P * r : P * (r + 1)].bitcast(E4M3)

        def right_features(r, banks):
            at = (32 + 4 * r) * KB
            return features(r, right, wr_sc, sbuf_at(at, [P, S], F32, f"h2_{r}"), (banks, banks + 1), negated)

        def turn(turned, page, c, start, stop, first=0, count=BLOCKS):
            for b in range(count):
                m0 = c * BANK + (first + b) * P
                nc.tensor.matmul(
                    turned[:, b, :], page[:, m0 : m0 + P], ident[:],
                    start=(start and b == 0), stop=(stop and b == count - 1), is_transpose=True,
                )

        def rows_of(tile, r, tiles, first=0, count=BLOCKS):
            return tile[:, :, first : first + count, SPAN * r : SPAN * (r + tiles), :]

        def leave_bank(dst, turned, r, func, first=0, count=BLOCKS):
            nc.scalar.activation(
                rows_of(dst, r, 1, first, count),
                turned[:].rearrange("m b (p u e) -> m u b p e", u=2, e=2), func,
            )

        floor = [sbuf_at(84 * KB, [P, BANK, PACK], BF16, "floor0")] + [
            sbuf_at((84 + 4 * c) * KB, [P, 2, BLOCKS, P, 2], BF16, f"floor{c}") for c in range(1, CHUNKS)
        ]

        def turn_band(r, banks):
            at = (LAST_PASS + 14 * KB, 8 * KB, 16 * KB, 104 * KB)[r]
            band_raw = sbuf_at(at, [P, T2 - BANK], F32, f"band_raw{r}")
            nc.sync.dma_start(band_raw[:], band[r * P : (r + 1) * P, BANK:T2])
            for c in range(1, CHUNKS):
                turned = bank(banks + c, [P, BLOCKS, P], "band_turned")
                turn(turned, band_raw, c - 1, True, True)
                leave_bank(floor[c], turned, r, ACT.Copy)

        def open_difference(r):
            turned = [bank(4 + c, [P, BLOCKS, P], "turned") for c in range(CHUNKS)]
            for c in range(CHUNKS):
                turn(turned[c], pageA[r], c, True, False)
            return turned

        h2 = [right_features(0, 2)]
        turn_band(0, 4)
        h2.append(right_features(1, 0))
        turn_band(1, 4)
        h2.append(right_features(2, 2))
        h2.append(right_features(3, 0))
        turned = open_difference(0)
        turn_band(2, 0)
        turn_band(3, 0)
        band_first = sbuf_at(110 * KB, [P, PACK, BANK], F32, "band_first")
        nc.sync.dma_start(band_first[:], band[:, 0:BANK].rearrange("(p t) m -> p t m", t=PACK))
        nc.scalar.copy(
            floor[0][:].rearrange("p (c i) t -> p c t i", i=PACK),
            band_first[:].rearrange("p t (c i) -> p c t i", i=PACK),
        )

        wd_w = sbuf_at(100 * KB, [P, N], I32, "wd_w")
        nc.sync.dma_start(wd_w[:], wd_words[0].rearrange("p c i -> p (c i)").bitcast(I32))
        wd_sc = sbuf([P, N], U8, "wd_sc", "w_sc")
        load_scale_rows(wd_sc, wd_scales, 1)
        res = []
        for s, at in enumerate((LAST_PASS + 12 * KB, 8 * KB, 104 * KB)):
            res.append(sbuf_at(at, [P, 2, T2], F32, f"res{s}"))
            nc.sync.dma_start(
                res[s][:], style[2 * P * s : 2 * P * (s + 1), :].rearrange("(i p) m -> p i m", p=P)
            )

        gap = [sbuf([P, 2, BLOCKS, P, 2], BF16, f"gap{c}") for c in range(CHUNKS)]
        for r in range(last):
            place(pageB[r % 2], h2[r][:], gain2, idx3)
            for c in range(CHUNKS):
                turn(turned[c], pageB[r % 2], c, False, True)
                leave_bank(gap[c], turned[c], r, ACT.Abs)
            if r + 1 < last:
                turned = open_difference(r + 1)
            if r == 1:
                place(pageA[0], h1_last[:], gain1, idx2)
        held = []
        for (c, first, count), at in zip(PIECES, HELD_BANKS):
            held.append(bank(at, [P, count, P], "held"))
            turn(held[-1], pageA[0], c, True, False, first, count)
        place(pageB[last % 2], h2[last][:], gain2, idx3)

        z_t = [gap[0]] + [
            sbuf_at(at, [P, 2, BLOCKS, P, 2], BF16, f"z_t{c + 1}")
            for c, at in enumerate((LAST_PASS, 44 * KB, 136 * KB))
        ]
        spare_banks = cycle(SPARE_BANKS)
        direct_banks = cycle(DIRECT_BANKS)

        def floor_at_band(c, r, tiles, first=0, count=BLOCKS):
            nc.vector.tensor_tensor(
                rows_of(z_t[c], r, tiles, first, count), rows_of(gap[c], r, tiles, first, count),
                rows_of(floor[c], r, tiles, first, count), ALU.max,
            )

        def close(i):
            c, first, count = PIECES[i]
            turn(held[i], pageB[last % 2], c, False, True, first, count)
            leave_bank(gap[c], held[i], last, ACT.Abs, first, count)
            if c > 0:
                floor_at_band(c, 0, last)
                floor_at_band(c, last, 1, first, count)

        def weave(i):
            c, first, count = PIECES[i]
            words = z_t[c][:].rearrange("m u b p e -> m (u b p e)").bitcast(F32)
            if i == 0:
                woven = sbuf_at(136 * KB, [P, count * P, 2], F32, "woven0")
            else:
                woven = sbuf([P, count * P, 2], F32, f"woven{i}")
            for k in range(count // 2):
                back = bank(take(spare_banks), [P, 2, 2 * P], "back")
                for u in range(2):
                    for b in range(2):
                        w0 = (u * BLOCKS + first + 2 * k + b) * P
                        nc.tensor.transpose(
                            back[:, u, b * P : (b + 1) * P], words[:, w0 : w0 + P], ident[:]
                        )
                dst = woven[:, 2 * P * k : 2 * P * (k + 1), :]
                if c > 0:
                    nc.scalar.copy(dst, back[:].rearrange("p u m -> p m u"))
                    continue
                m0 = (first + 2 * k) * P
                nc.vector.tensor_tensor(
                    dst.rearrange("p m u -> p (m u)").bitcast(BF16).rearrange("p (m u e) -> p m u e", u=2, e=2),
                    back[:].rearrange("p u m -> p (u m)").bitcast(BF16).rearrange("p (u m e) -> p m u e", u=2, e=2),
                    floor[0][:, m0 : m0 + 2 * P, :].rearrange("p m (u e) -> p m u e", u=2),
                    ALU.max,
                )
            return woven

        def quantise(i, woven):
            width = PIECES[i][2] * P
            z_w = sbuf([P, width], U32, f"z_w{i}")
            z_sc = sbuf([P, width], U8, f"z_sc{i}")
            nc.vector.quantize_mx(
                z_w[:].bitcast(E4M3), z_sc[:], woven[:].rearrange("p m u -> p (m u)").bitcast(BF16)
            )
            return z_w, z_sc

        def columns(i):
            c, first, count = PIECES[i]
            return slice(c * BANK + first * P, c * BANK + (first + count) * P)

        def product(acc, n, z_mx):
            nc.tensor.matmul_mx(
                acc,
                lhsT=wd_w[:, n * P : (n + 1) * P].bitcast(E4M3),
                lhsT_scale=wd_sc[:, n * P : (n + 1) * P],
                rhs=z_mx[0][:].bitcast(E4M3),
                rhs_scale=z_mx[1][:],
                start=True,
                stop=True,
            )

        def store(i, n):
            cols = columns(i)
            if i == len(PIECES) - 1 and n >= OUT_TILES - 2:
                nc.sync.dma_start(out[n * P : (n + 1) * P, cols], res[n // 2][:, n % 2, cols])
            elif n % 2 == 1:
                rows = out[(n - 1) * P : (n + 1) * P, cols].rearrange("(i p) m -> p i m", p=P)
                nc.sync.dma_start(rows, res[n // 2][:, :, cols])

        def project(i, z_mx, tiles):
            cols = columns(i)
            width = PIECES[i][2] * P
            if 2 * width <= BANK:
                for n in tiles[::2]:
                    acc = bank(take(direct_banks), [P, 2, width], "acc")
                    for k in range(2):
                        product(acc[:, k, :], n + k, z_mx)
                    total = res[n // 2][:, :, cols]
                    nc.vector.tensor_tensor(total, total, acc[:], ALU.add)
                    store(i, n + 1)
                return
            for n in tiles:
                acc = bank(take(direct_banks), [P, width], "acc")
                product(acc[:], n, z_mx)
                total = res[n // 2][:, n % 2, cols]
                if i == len(PIECES) - 1 and n == OUT_TILES - 1:
                    for k in range(2):
                        half = slice(k * BANK // 2, (k + 1) * BANK // 2)
                        nc.vector.tensor_tensor(total[:, half], total[:, half], acc[:, half], ALU.add)
                        nc.sync.dma_start(out[n * P : (n + 1) * P, cols][:, half], total[:, half])
                else:
                    nc.vector.tensor_tensor(total, total, acc[:], ALU.add)
                    store(i, n)

        def stage(i, z_mx, n):
            width = PIECES[i][2] * P
            acc = bank(take(direct_banks), [P, BANK // width, width], "acc")
            for k in range(BANK // width):
                product(acc[:, k, :], n + k, z_mx)
            staged = sbuf([P, BANK // width, width], F32, f"staged{i}", "staged", bufs=2)
            nc.scalar.copy(staged[:], acc[:])
            return staged

        def add_aside(i, z_mx, n):
            total = res[n // 2][:, n % 2, columns(i)]
            nc.gpsimd.tensor_tensor(total, total, stage(i, z_mx, n)[:, 0, :], ALU.add)

        z_mx = {}
        close(0)
        z_mx[0] = quantise(0, weave(0))
        close(1)
        woven = weave(1)
        for i in range(2, len(PIECES)):
            close(i)
        project(0, z_mx[0], range(0, 2))
        staged = stage(0, z_mx[0], 4)
        z_mx[1] = quantise(1, woven)
        woven = weave(2)
        total = sbuf([P, 2, BANK // 2], F32, "total", "woven1")
        nc.gpsimd.tensor_tensor(total[:], staged[:], res[2][:, :, columns(0)], ALU.add)
        project(0, z_mx[0], range(2, 4))
        nc.sync.dma_start(out[4 * P : 6 * P, columns(0)].rearrange("(i p) m -> p i m", p=P), total[:])
        project(1, z_mx[1], range(0, 4))
        z_mx[2] = quantise(2, woven)
        woven = weave(3)
        project(1, z_mx[1], range(4, 6))
        for i in (2, 3):
            add_aside(i, z_mx[i], 4)
            project(i, z_mx[i], range(0, 3))
            z_mx[i + 1] = quantise(i + 1, woven)
            if i == 2:
                woven = weave(4)
            project(i, z_mx[i], (3, 5))
        add_aside(4, z_mx[4], 2)
        project(4, z_mx[4], (0, 1))
        add_aside(4, z_mx[4], 4)
        project(4, z_mx[4], (3,))
        store(4, 4)
        project(4, z_mx[4], (5,))
